import numpy as np
import ml_dtypes


def mxq(x, axis, fmt="e4m3"):
    dtype, down = {"e4m3": (ml_dtypes.float8_e4m3fn, 7), "e5m2": (ml_dtypes.float8_e5m2, 14)}[fmt]
    v = np.moveaxis(np.asarray(x, np.float32).astype(ml_dtypes.bfloat16).astype(np.float64), axis, -1)
    blocks = v.reshape(v.shape[:-1] + (-1, 32))
    amax = np.abs(blocks).max(-1, keepdims=True)
    byte = np.maximum(np.where(amax > 0, np.frexp(amax)[1] - 1 + 127, 0) - down, 1)
    scale = np.exp2(byte - 127.0)
    codes = (blocks / scale).astype(np.float32).astype(dtype).astype(np.float64)
    return np.moveaxis((codes * scale).reshape(v.shape), -1, axis)


WIDE = False


def mx_kscale(k):
    if not WIDE:
        return np.ones(k)
    levels = np.array([10, -10, 5, -5, 0])
    if k % 512:
        return np.exp2(np.random.permutation(np.resize(levels, k // 32))).repeat(32)
    a = np.empty((k // 512, 16))
    for p in range(k // 512):
        a[p, :8] = np.random.permutation(np.resize(levels, 8))
        for g in range(8):
            far = levels[np.abs(levels - a[p, g]) >= 10]
            a[p, g + 8] = far[np.random.randint(len(far))]
    return np.exp2(a.ravel()).repeat(32)


def f64(x):
    return np.asarray(x).astype(np.float64)


def striped(idx):
    return np.tile(idx.reshape(-1, 16).T, (8, 1)).astype(np.uint16)


def unstriped(offs):
    return offs[:16].T.reshape(-1).astype(np.int64)


E2M1 = np.array([0.0, 0.5, 1.0, 1.5, 2.0, 3.0, 4.0, 6.0, -0.0, -0.5, -1.0, -1.5, -2.0, -3.0, -4.0, -6.0])


def pack_weight(w, fmt):
    k, n = w.shape
    w = f64(np.asarray(w, np.float32).astype(ml_dtypes.bfloat16)).reshape(k // 32, 32, n)
    amax = np.abs(w).max(1)
    if fmt == "e4m3":
        byte = np.frexp(amax)[1] - 1 + 127 - 7
    else:
        mant, ex = np.frexp(amax / 6.0)
        byte = np.where(mant > 0.5, ex, ex - 1) + 127
    byte = np.clip(np.where(amax > 0, byte, 1), 1, 254)
    scaled = (w * np.exp2(127.0 - byte)[:, None, :]).reshape(k, n).astype(np.float32)
    by_word = np.ascontiguousarray(scaled.reshape(k // 512, 128, 4, n).transpose(0, 1, 3, 2))
    if fmt == "e4m3":
        words = by_word.astype(ml_dtypes.float8_e4m3fn).view(np.uint8)
    else:
        c = by_word.astype(ml_dtypes.float4_e2m1fn).view(np.uint8) & 0xF
        words = (c[..., 0::2] | (c[..., 1::2] << 4)).reshape(k // 512, 128, 2 * n)
    return np.ascontiguousarray(words), np.ascontiguousarray(byte.astype(np.uint8).reshape(k // 512, 16, n))


def unpack_weight(words, scales, fmt):
    g, _, n = scales.shape
    words = np.ascontiguousarray(words).reshape(g, 128, n, -1)
    if fmt == "e4m3":
        vals = words.view(ml_dtypes.float8_e4m3fn).astype(np.float64)
    else:
        nib = np.empty((g, 128, n, 4), np.uint8)
        nib[..., 0::2] = words & 0xF
        nib[..., 1::2] = words >> 4
        vals = E2M1[nib]
    vals = vals * np.repeat(np.exp2(scales.astype(np.float64) - 127.0), 8, axis=1)[..., None]
    return vals.transpose(0, 1, 3, 2).reshape(g * 512, n)


def gelu(v):
    return 0.5 * v * (1.0 + np.tanh(np.sqrt(2.0 / np.pi) * (v + 0.044715 * v**3)))


def striped8(idx):
    return np.concatenate([v.reshape(-1, 16).T for v in idx]).astype(np.uint16)


def unstriped8(offs):
    return np.stack([offs[16 * g:16 * g + 16].T.reshape(-1) for g in range(8)]).astype(np.int64)


def runs(v, idx8):
    k = np.arange(v.shape[0])
    return v[k[:, None], idx8[k % 512 // 64]]


K, T, S, H, M, N = 1024, 2048, 1024, 512, 1024, 256

def setup_inputs():
    n = np.random.standard_normal
    s = mx_kscale(K)[:, None]
    u = mx_kscale(H)[:, None]
    w = mx_kscale(M)[:, None]
    tab_words, tab_scales = pack_weight(n((K, T)) * s, "e4m3")
    w1_words, w1_scales = pack_weight(n((K, H)) / np.sqrt(K) / s, "e2m1")
    w2_words, w2_scales = pack_weight(n((H, M)) / np.sqrt(H) / u, "e4m3")
    return {
        "tab_words": tab_words, "tab_scales": tab_scales,
        "offs": striped8(np.stack([np.random.permutation(T)[:S] for _ in range(8)])),
        "w1_words": w1_words, "w1_scales": w1_scales,
        "w2_words": w2_words, "w2_scales": w2_scales,
        "w3": (n((K, M)) / np.sqrt(K) / s).astype(np.float32),
        "w4": (n((M, N)) / np.sqrt(M) / w).astype(np.float32),
        "gain1": (np.exp(0.3 * n(H)) * u[:, 0]).astype(np.float32),
        "gain2": (np.exp(0.3 * n(M)) * w[:, 0]).astype(np.float32),
        "clim": (0.5 * n(N)).astype(np.float32),
    }

def reference(tab_words, tab_scales, offs, w1_words, w1_scales, w2_words, w2_scales, w3, w4, gain1, gain2, clim):
    v = runs(unpack_weight(tab_words, tab_scales, "e4m3"), unstriped8(offs))
    w1 = unpack_weight(w1_words, w1_scales, "e2m1")
    w2 = unpack_weight(w2_words, w2_scales, "e4m3")
    h = np.tanh(w1.T @ v) * f64(gain1)[:, None]
    a = w2.T @ mxq(h, 0, "e4m3") + mxq(f64(w3), 0, "e4m3").T @ v
    z = a / (1.0 + np.exp(-a)) * f64(gain2)[:, None]
    return (mxq(f64(w4), 0, "e4m3").T @ mxq(z, 0, "e4m3")) + f64(clim)[:, None]

@@ -1,0 +1,283 @@
+from contextlib import ExitStack
+
+import concourse.mybir as mybir
+
+K, T, S, H, M, N = 1024, 2048, 1024, 512, 1024, 256
+FLOPS = 2 * S * (K * H + H * M + K * M + M * N)
+
+F32 = mybir.dt.float32
+BF16 = mybir.dt.bfloat16
+I32 = mybir.dt.int32
+U32 = mybir.dt.uint32
+U16 = mybir.dt.uint16
+U8 = mybir.dt.uint8
+FP8X4 = mybir.dt.float8_e4m3fn_x4
+FP4X4 = mybir.dt.float4_e2m1fn_x4
+ACT = mybir.ActivationFunctionType
+MULT = mybir.AluOpType.mult
+
+P = 128
+PACK = 4
+KP = P * PACK
+CHUNK = 256
+CHUNKS = S // CHUNK
+LIST_COLS = CHUNK // 16
+
+
+def tile_list_cyclone_intensity_nowcast_kernel(
+    tc, tab_words, tab_scales, offs, w1_words, w1_scales, w2_words, w2_scales, w3, w4, gain1, gain2, clim, out
+):
+    nc = tc.nc
+    with ExitStack() as ctx:
+        keep = ctx.enter_context(tc.tile_pool(name="keep", bufs=1))
+        work = ctx.enter_context(tc.tile_pool(name="work", bufs=3))
+        psum = ctx.enter_context(tc.psum_pool(name="psum", bufs=8))
+
+        def held(name, shape, dtype, tag=None):
+            return keep.tile(shape, dtype, name=name, tag=tag or name, align_bytes=64)
+
+        offsets = keep.tile([P, S // 16], U16, name="offsets")
+        nc.sync.dma_start(offsets[:], offs)
+
+        scale_window = held("scale_window", [P, T], U8)
+        nc.vector.memset(scale_window[:].bitcast(I32), 0)
+        for e in range(2):
+            nc.sync.dma_start(scale_window[e:P:16, :].bitcast(I32), tab_scales[0, e:16:2, :].bitcast(I32))
+        nc.sync.dma_start(scale_window[4:P:8, :].bitcast(I32), tab_scales[1].bitcast(I32))
+
+        w1_raw = held("w1_raw", [P, 2, 2 * H], U8)
+        nc.sync.dma_start(w1_raw[:].bitcast(I32), w1_words.rearrange("a p c -> p a c").bitcast(I32))
+
+        windows = []
+        for a in range(2):
+            window = held("window%d" % a, [P, T], I32, tag="big%d" % a)
+            nc.sync.dma_start(window[:], tab_words[a].rearrange("p t i -> p (t i)").bitcast(I32))
+            windows.append(window)
+
+        def load_w3(g, am, tag):
+            raw = held("w3_raw%d%d" % (g, am), [P, PACK, KP], F32, tag=tag)
+            rows = w3[g * KP : (g + 1) * KP, am * KP : (am + 1) * KP]
+            nc.sync.dma_start(raw[:], rows.rearrange("(p j) m -> p j m", j=PACK))
+            return raw
+
+        w3_raw = {(g, 0): load_w3(g, 0, "big%d" % (2 + g)) for g in range(2)}
+
+        w1s_raw = held("w1s_raw", [P, 2 * H], U8)
+        w2s_raw = held("w2s_raw", [P, M], U8)
+        nc.gpsimd.memset(w1s_raw[:].bitcast(I32), 0)
+        nc.vector.memset(w2s_raw[:].bitcast(I32), 0)
+        for r in range(4):
+            nc.gpsimd.dma_start(
+                w1s_raw[r:P:32, :].rearrange("d (a c) -> d a c", a=2).bitcast(I32),
+                w1_scales[:, r:16:4, :].rearrange("a d c -> d a c").bitcast(I32),
+            )
+        gain1_sb = held("gain1_sb", [P, PACK], F32)
+        nc.gpsimd.dma_start(gain1_sb[:], gain1.rearrange("(p t) -> p t", t=PACK))
+        for r in range(4):
+            nc.gpsimd.dma_start(w2s_raw[r:P:32, :].bitcast(I32), w2_scales[0, r:16:4, :].bitcast(I32))
+        gain2_raw = held("gain2_raw", [P, 2, 8], F32)
+        for i in range(2):
+            nc.gpsimd.dma_start(
+                gain2_raw[i:P:2, :, 0:7], gain2.rearrange("(a c x) -> c a x", a=2, x=8)[:, :, i : i + 7]
+            )
+        clim_sb = held("clim_sb", [P, N // P], F32)
+        with nc.allow_non_contiguous_dma(reason="one value a partition"):
+            nc.gpsimd.dma_start(clim_sb[:], clim.rearrange("(b p) -> p b", p=P))
+
+        zero_in = held("zero_in", [P, 1], F32)
+        zero_bias = held("zero_bias", [P, 1], F32)
+        nc.vector.memset(zero_in[:], 0.0)
+        nc.scalar.activation(zero_bias[:], zero_in[:], ACT.Silu)
+
+        v_scales = [held("v_scales%d" % a, [P, S], U8) for a in range(2)]
+        nc.vector.memset(v_scales[1][:].bitcast(I32), 0)
+        picked_scales = held("picked_scales", [P, S], U8, tag="picked")
+        nc.vector.tensor_copy(picked_scales[:], scale_window[:].indirect(offsets[:]))
+        nc.vector.tensor_copy(v_scales[0][:].bitcast(I32), picked_scales[:].bitcast(I32))
+        for r in range(4):
+            nc.scalar.dma_start(
+                v_scales[1][r:P:32, :].bitcast(I32), picked_scales[8 * r + 4 : P : 32, :].bitcast(I32)
+            )
+        for r in range(2, 4):
+            nc.scalar.dma_start(
+                v_scales[0][r:P:32, :].bitcast(I32), picked_scales[14 + r : P : 32, :].bitcast(I32)
+            )
+
+        w1_codes = held("w1_codes", [P, 2, 2 * H], U8)
+        nc.vector.tensor_copy(
+            w1_codes[:].bitcast(U16).rearrange("p a (t m) -> p a t m", t=PACK),
+            w1_raw[:].bitcast(U16).rearrange("p a (m t) -> p a t m", t=PACK),
+        )
+        w1_sc = held("w1_sc", [P, 2, H], U8)
+        nc.vector.tensor_copy(
+            w1_sc[:].rearrange("p a (t m) -> p a t m", t=PACK),
+            w1s_raw[:].rearrange("p (a m t) -> p a t m", a=2, t=PACK),
+        )
+
+        v_codes = [held("v_codes%d" % a, [P, S], U32) for a in range(2)]
+        nc.vector.tensor_copy(v_codes[0][:], windows[0][:].bitcast(U32).indirect(offsets[:]))
+
+        def gather_pass1(c):
+            nc.vector.tensor_copy(
+                v_codes[1][:, c * CHUNK : (c + 1) * CHUNK],
+                windows[1][:].bitcast(U32).indirect(offsets[:, c * LIST_COLS : (c + 1) * LIST_COLS]),
+            )
+
+        for c in range(CHUNKS):
+            gather_pass1(c)
+
+        w2_raw = held("w2_raw", [P, M], I32, tag="picked")
+        nc.sync.dma_start(w2_raw[:], w2_words[0].rearrange("p c i -> p (c i)").bitcast(I32))
+        for g in range(2):
+            w3_raw[(g, 1)] = load_w3(g, 1, "big%d" % g)
+
+        w3_codes, w3_sc = {}, {}
+
+        def cast_w3(g, am):
+            grouped = work.tile([P, KP * PACK], BF16, name="w_bf", tag="w_bf", align_bytes=64)
+            nc.scalar.copy(
+                grouped[:].rearrange("p (t c i j) -> p c t j i", t=PACK, i=2, j=PACK),
+                w3_raw[(g, am)][:].rearrange("p j (c t i) -> p c t j i", t=PACK, i=2),
+            )
+            return grouped
+
+        def quantize(name, grouped, width):
+            codes = held(name + "_codes", [P, width], U32)
+            scales = held(name + "_sc", [P, width], U8)
+            nc.vector.quantize_mx(codes[:].bitcast(FP8X4), scales[:], grouped[:])
+            return codes, scales
+
+        h_q, z_q = {}, {}
+
+        def stage1(c):
+            th = work.tile([P, CHUNK * PACK], F32, name="act32", tag="act32", bufs=4)
+            for half in range(2):
+                bank = psum.tile([P, PACK, P], F32, name="bank", tag="bank")
+                cols = slice(c * CHUNK + half * P, c * CHUNK + (half + 1) * P)
+                for t in range(PACK):
+                    for a in range(2):
+                        nc.tensor.matmul_mx(
+                            bank[:, t, :],
+                            lhsT=w1_codes[:, a, 2 * P * t : 2 * P * (t + 1)].bitcast(FP4X4),
+                            lhsT_scale=w1_sc[:, a, P * t : P * (t + 1)],
+                            rhs=v_codes[a][:, cols].bitcast(FP8X4),
+                            rhs_scale=v_scales[a][:, cols],
+                            start=(a == 0),
+                            stop=(a == 1),
+                        )
+                nc.scalar.activation(
+                    th[:, half * KP : (half + 1) * KP].rearrange("p (n t) -> p n t", t=PACK),
+                    bank[:].rearrange("p t n -> p n t"),
+                    ACT.Tanh,
+                    bias=zero_bias[:],
+                )
+            h_bf = work.tile([P, CHUNK * PACK], BF16, name="act16", tag="act16", align_bytes=64)
+            nc.vector.tensor_tensor(
+                h_bf[:].rearrange("p (n t) -> p n t", t=PACK),
+                th[:].rearrange("p (n t) -> p n t", t=PACK),
+                gain1_sb[:].unsqueeze(1).to_broadcast([P, CHUNK, PACK]),
+                MULT,
+            )
+            h_q[c] = quantize("h%d" % c, h_bf, CHUNK)
+
+        stage1(0)
+        for g in range(2):
+            w3_codes[(g, 0)], w3_sc[(g, 0)] = quantize("w3_%d0" % g, cast_w3(g, 0), KP)
+            stage1(1 + g)
+
+        w2_codes = held("w2_codes", [P, M], I32)
+        nc.vector.tensor_copy(
+            w2_codes[:].rearrange("p (a t c i) -> p a t c i", a=2, t=PACK, i=2),
+            w2_raw[:].rearrange("p (a c t i) -> p a t c i", a=2, t=PACK, i=2),
+        )
+        w2_sc = held("w2_sc", [P, M], U8)
+        nc.vector.tensor_copy(
+            w2_sc[:].rearrange("p (a t c i) -> p a t c i", a=2, t=PACK, i=2),
+            w2s_raw[:].rearrange("p (a c t i) -> p a t c i", a=2, t=PACK, i=2),
+        )
+        stage1(3)
+
+        w4_raw = held("w4_raw", [P, 2, PACK, N], F32, tag="big2")
+        for am in range(2):
+            for i in range(2):
+                rows = w4[am * KP : (am + 1) * KP, :].rearrange("(c t i) n -> i c t n", t=PACK, i=2)
+                nc.sync.dma_start(w4_raw[i:P:2, am, :, :], rows[i])
+
+        def stage2(am, c):
+            sl = work.tile([P, CHUNK * PACK], F32, name="act32", tag="act32", bufs=4)
+            cols = slice(c * CHUNK, (c + 1) * CHUNK)
+            for u in range(2):
+                bank = psum.tile([P, 2, CHUNK], F32, name="bank", tag="bank")
+                for e in range(2):
+                    t = 2 * u + e
+                    wcols = slice(P * t, P * (t + 1))
+                    for g in range(2):
+                        nc.tensor.matmul_mx(
+                            bank[:, e, :],
+                            lhsT=w3_codes[(g, am)][:, wcols].bitcast(FP8X4),
+                            lhsT_scale=w3_sc[(g, am)][:, wcols],
+                            rhs=v_codes[g][:, cols].bitcast(FP8X4),
+                            rhs_scale=v_scales[g][:, cols],
+                            start=(g == 0),
+                            stop=False,
+                        )
+                    w2cols = slice(am * KP + P * t, am * KP + P * (t + 1))
+                    nc.tensor.matmul_mx(
+                        bank[:, e, :],
+                        lhsT=w2_codes[:, w2cols].bitcast(FP8X4),
+                        lhsT_scale=w2_sc[:, w2cols],
+                        rhs=h_q[c][0][:].bitcast(FP8X4),
+                        rhs_scale=h_q[c][1][:],
+                        start=False,
+                        stop=True,
+                    )
+                nc.scalar.activation(
+                    sl[:, u * KP : (u + 1) * KP].rearrange("p (n e) -> p n e", e=2),
+                    bank[:].rearrange("p e n -> p n e"),
+                    ACT.Silu,
+                )
+            z_bf = work.tile([P, CHUNK * PACK], BF16, name="act16", tag="act16", align_bytes=64)
+            nc.vector.tensor_tensor(
+                z_bf[:].rearrange("p (n u e) -> p n u e", u=2, e=2),
+                sl[:].rearrange("p (u n e) -> p n u e", u=2, e=2),
+                gain2_raw[:, am, 0:7:2].rearrange("p (u e) -> p u e", u=2).unsqueeze(1).to_broadcast([P, CHUNK, 2, 2]),
+                MULT,
+            )
+            z_q[(am, c)] = quantize("z%d%d" % (am, c), z_bf, CHUNK)
+
+        for c in range(CHUNKS):
+            stage2(0, c)
+            if c < 2:
+                w3_codes[(c, 1)], w3_sc[(c, 1)] = quantize("w3_%d1" % c, cast_w3(c, 1), KP)
+
+        w4_bf = work.tile([P, 2 * N * PACK], BF16, name="w_bf", tag="w_bf", align_bytes=64)
+        nc.scalar.copy(
+            w4_bf[:].rearrange("p (a c i t) -> p a c t i", a=2, t=PACK, i=2),
+            w4_raw[:].rearrange("p a t (c i) -> p a c t i", i=2),
+        )
+        w4_codes, w4_sc = quantize("w4", w4_bf, 2 * N)
+
+        def stage3(c):
+            bank = psum.tile([P, 2, CHUNK], F32, name="bank", tag="bank")
+            for b in range(2):
+                for am in range(2):
+                    wcols = slice(am * N + b * P, am * N + (b + 1) * P)
+                    nc.tensor.matmul_mx(
+                        bank[:, b, :],
+                        lhsT=w4_codes[:, wcols].bitcast(FP8X4),
+                        lhsT_scale=w4_sc[:, wcols],
+                        rhs=z_q[(am, c)][0][:].bitcast(FP8X4),
+                        rhs_scale=z_q[(am, c)][1][:],
+                        start=(am == 0),
+                        stop=(am == 1),
+                    )
+            res = work.tile([P, 2, CHUNK], F32, name="res", tag="res")
+            for b in range(2):
+                nc.scalar.activation(res[:, b, :], bank[:, b, :], ACT.Identity, bias=clim_sb[:, b : b + 1])
+            nc.sync.dma_start(out[:, c * CHUNK : (c + 1) * CHUNK].rearrange("(b p) j -> p b j", p=P), res[:])
+
+        for c in range(CHUNKS):
+            stage2(1, c)
+            if c > 0:
+                stage3(c - 1)
+        stage3(CHUNKS - 1)

@@ -39,20 +39,39 @@ def tile_list_cyclone_intensity_nowcast_kernel(
         offsets = keep.tile([P, S // 16], U16, name="offsets")
         nc.sync.dma_start(offsets[:], offs)
 
-        scale_window = held("scale_window", [P, T], U8)
+        w1_raw = held("w1_raw", [P, 2, 2 * H], U8)
+        nc.sync.dma_start(w1_raw[:].bitcast(I32), w1_words.rearrange("a p c -> p a c").bitcast(I32))
+
+        scale_window = held("scale_window", [P, T], U8, tag="slot_c")
         nc.vector.memset(scale_window[:].bitcast(I32), 0)
         for e in range(2):
             nc.sync.dma_start(scale_window[e:P:16, :].bitcast(I32), tab_scales[0, e:16:2, :].bitcast(I32))
         nc.sync.dma_start(scale_window[4:P:8, :].bitcast(I32), tab_scales[1].bitcast(I32))
 
-        w1_raw = held("w1_raw", [P, 2, 2 * H], U8)
-        nc.sync.dma_start(w1_raw[:].bitcast(I32), w1_words.rearrange("a p c -> p a c").bitcast(I32))
+        zero_a = held("zero_a", [P, 1], F32, tag="slot_d")
+        zero_b = held("zero_b", [P, 1], F32, tag="slot_f")
+        zero_in = held("zero_in", [P, 1], F32, tag="slot_a")
+        zero_bias = held("zero_bias", [P, 1], F32)
+        nc.vector.memset(zero_a[:], 0.0)
+        nc.vector.memset(zero_b[:], 0.0)
+        nc.vector.tensor_tensor(zero_in[:], zero_a[:], zero_b[:], MULT)
+        nc.scalar.activation(zero_bias[:], zero_in[:], ACT.Silu)
 
-        windows = []
-        for a in range(2):
-            window = held("window%d" % a, [P, T], I32, tag="big%d" % a)
+        def load_window(a, tag):
+            window = held("window%d" % a, [P, T], I32, tag=tag)
             nc.sync.dma_start(window[:], tab_words[a].rearrange("p t i -> p (t i)").bitcast(I32))
-            windows.append(window)
+            return window
+
+        windows = [load_window(0, "slot_d")]
+
+        w1s_raw = held("w1s_raw", [P, 2 * H], U8, tag="slot_f")
+        nc.vector.memset(w1s_raw[:].bitcast(I32), 0)
+        for r in range(4):
+            nc.sync.dma_start(
+                w1s_raw[r:P:32, :].rearrange("d (a c) -> d a c", a=2).bitcast(I32),
+                w1_scales[:, r:16:4, :].rearrange("a d c -> d a c").bitcast(I32),
+            )
+        windows.append(load_window(1, "slot_a"))
 
         def load_w3(g, am, tag):
             raw = held("w3_raw%d%d" % (g, am), [P, PACK, KP], F32, tag=tag)
@@ -60,82 +79,65 @@ def tile_list_cyclone_intensity_nowcast_kernel(
             nc.sync.dma_start(raw[:], rows.rearrange("(p j) m -> p j m", j=PACK))
             return raw
 
-        w3_raw = {(g, 0): load_w3(g, 0, "big%d" % (2 + g)) for g in range(2)}
-
-        w1s_raw = held("w1s_raw", [P, 2 * H], U8)
-        w2s_raw = held("w2s_raw", [P, M], U8)
-        nc.gpsimd.memset(w1s_raw[:].bitcast(I32), 0)
-        nc.vector.memset(w2s_raw[:].bitcast(I32), 0)
-        for r in range(4):
-            nc.gpsimd.dma_start(
-                w1s_raw[r:P:32, :].rearrange("d (a c) -> d a c", a=2).bitcast(I32),
-                w1_scales[:, r:16:4, :].rearrange("a d c -> d a c").bitcast(I32),
-            )
-        gain1_sb = held("gain1_sb", [P, PACK], F32)
-        nc.gpsimd.dma_start(gain1_sb[:], gain1.rearrange("(p t) -> p t", t=PACK))
-        for r in range(4):
-            nc.gpsimd.dma_start(w2s_raw[r:P:32, :].bitcast(I32), w2_scales[0, r:16:4, :].bitcast(I32))
-        gain2_raw = held("gain2_raw", [P, 2, 8], F32)
+        w1_sc = held("w1_sc", [P, 2, H], U8)
+        nc.gpsimd.tensor_copy(
+            w1_sc[:].rearrange("p a (t m) -> p a t m", t=PACK),
+            w1s_raw[:].rearrange("p (a m t) -> p a t m", a=2, t=PACK),
+        )
+        vectors = held("vectors", [P, 32], F32)
+        gain2_raw = vectors[:, 0:16].rearrange("p (a x) -> p a x", a=2)
+        gain1_sb = vectors[:, 16 : 16 + PACK]
+        clim_sb = vectors[:, 24 : 24 + N // P]
+        nc.gpsimd.dma_start(gain1_sb, gain1.rearrange("(p t) -> p t", t=PACK))
         for i in range(2):
             nc.gpsimd.dma_start(
                 gain2_raw[i:P:2, :, 0:7], gain2.rearrange("(a c x) -> c a x", a=2, x=8)[:, :, i : i + 7]
             )
-        clim_sb = held("clim_sb", [P, N // P], F32)
         with nc.allow_non_contiguous_dma(reason="one value a partition"):
-            nc.gpsimd.dma_start(clim_sb[:], clim.rearrange("(b p) -> p b", p=P))
-
-        zero_in = held("zero_in", [P, 1], F32)
-        zero_bias = held("zero_bias", [P, 1], F32)
-        nc.vector.memset(zero_in[:], 0.0)
-        nc.scalar.activation(zero_bias[:], zero_in[:], ACT.Silu)
+            nc.gpsimd.dma_start(clim_sb, clim.rearrange("(b p) -> p b", p=P))
 
         v_scales = [held("v_scales%d" % a, [P, S], U8) for a in range(2)]
         nc.vector.memset(v_scales[1][:].bitcast(I32), 0)
-        picked_scales = held("picked_scales", [P, S], U8, tag="picked")
+        picked_scales = held("picked_scales", [P, S], U8, tag="slot_e")
         nc.vector.tensor_copy(picked_scales[:], scale_window[:].indirect(offsets[:]))
         nc.vector.tensor_copy(v_scales[0][:].bitcast(I32), picked_scales[:].bitcast(I32))
         for r in range(4):
-            nc.scalar.dma_start(
+            nc.sync.dma_start(
                 v_scales[1][r:P:32, :].bitcast(I32), picked_scales[8 * r + 4 : P : 32, :].bitcast(I32)
             )
         for r in range(2, 4):
-            nc.scalar.dma_start(
+            nc.sync.dma_start(
                 v_scales[0][r:P:32, :].bitcast(I32), picked_scales[14 + r : P : 32, :].bitcast(I32)
             )
+        w3_raw = {(0, 0): load_w3(0, 0, "slot_c"), (1, 0): load_w3(1, 0, "slot_e")}
 
         w1_codes = held("w1_codes", [P, 2, 2 * H], U8)
         nc.vector.tensor_copy(
             w1_codes[:].bitcast(U16).rearrange("p a (t m) -> p a t m", t=PACK),
             w1_raw[:].bitcast(U16).rearrange("p a (m t) -> p a t m", t=PACK),
         )
-        w1_sc = held("w1_sc", [P, 2, H], U8)
-        nc.vector.tensor_copy(
-            w1_sc[:].rearrange("p a (t m) -> p a t m", t=PACK),
-            w1s_raw[:].rearrange("p (a m t) -> p a t m", a=2, t=PACK),
-        )
 
         v_codes = [held("v_codes%d" % a, [P, S], U32) for a in range(2)]
-        nc.vector.tensor_copy(v_codes[0][:], windows[0][:].bitcast(U32).indirect(offsets[:]))
-
-        def gather_pass1(c):
-            nc.vector.tensor_copy(
-                v_codes[1][:, c * CHUNK : (c + 1) * CHUNK],
-                windows[1][:].bitcast(U32).indirect(offsets[:, c * LIST_COLS : (c + 1) * LIST_COLS]),
-            )
-
         for c in range(CHUNKS):
-            gather_pass1(c)
+            for a in range(2):
+                nc.vector.tensor_copy(
+                    v_codes[a][:, c * CHUNK : (c + 1) * CHUNK],
+                    windows[a][:].bitcast(U32).indirect(offsets[:, c * LIST_COLS : (c + 1) * LIST_COLS]),
+                )
 
-        w2_raw = held("w2_raw", [P, M], I32, tag="picked")
-        nc.sync.dma_start(w2_raw[:], w2_words[0].rearrange("p c i -> p (c i)").bitcast(I32))
-        for g in range(2):
-            w3_raw[(g, 1)] = load_w3(g, 1, "big%d" % g)
+        w2_staged = held("w2_staged", [P, M + M // 4], I32, tag="slot_a")
+        w2_raw = w2_staged[:, 0:M]
+        w2s_raw = w2_staged[:, M:]
+        nc.sync.dma_start(w2_raw, w2_words[0].rearrange("p c i -> p (c i)").bitcast(I32))
+        nc.vector.memset(w2s_raw, 0)
+        for r in range(4):
+            nc.sync.dma_start(w2_staged[r:P:32, M:], w2_scales[0, r:16:4, :].bitcast(I32))
 
         w3_codes, w3_sc = {}, {}
 
-        def cast_w3(g, am):
+        def cast_w3(g, am, copy):
             grouped = work.tile([P, KP * PACK], BF16, name="w_bf", tag="w_bf", align_bytes=64)
-            nc.scalar.copy(
+            copy(
                 grouped[:].rearrange("p (t c i j) -> p c t j i", t=PACK, i=2, j=PACK),
                 w3_raw[(g, am)][:].rearrange("p j (c t i) -> p c t j i", t=PACK, i=2),
             )
@@ -175,41 +177,51 @@ def tile_list_cyclone_intensity_nowcast_kernel(
             nc.vector.tensor_tensor(
                 h_bf[:].rearrange("p (n t) -> p n t", t=PACK),
                 th[:].rearrange("p (n t) -> p n t", t=PACK),
-                gain1_sb[:].unsqueeze(1).to_broadcast([P, CHUNK, PACK]),
+                gain1_sb.unsqueeze(1).to_broadcast([P, CHUNK, PACK]),
                 MULT,
             )
             h_q[c] = quantize("h%d" % c, h_bf, CHUNK)
 
         stage1(0)
-        for g in range(2):
-            w3_codes[(g, 0)], w3_sc[(g, 0)] = quantize("w3_%d0" % g, cast_w3(g, 0), KP)
-            stage1(1 + g)
+        w3_codes[(0, 0)], w3_sc[(0, 0)] = quantize("w3_00", cast_w3(0, 0, nc.scalar.copy), KP)
+        w3_raw[(0, 1)] = load_w3(0, 1, "slot_c")
+        w3_codes[(1, 0)], w3_sc[(1, 0)] = quantize("w3_10", cast_w3(1, 0, nc.vector.tensor_copy), KP)
+        w3_raw[(1, 1)] = load_w3(1, 1, "slot_e")
+        stage1(1)
 
         w2_codes = held("w2_codes", [P, M], I32)
         nc.vector.tensor_copy(
             w2_codes[:].rearrange("p (a t c i) -> p a t c i", a=2, t=PACK, i=2),
-            w2_raw[:].rearrange("p (a c t i) -> p a t c i", a=2, t=PACK, i=2),
+            w2_raw.rearrange("p (a c t i) -> p a t c i", a=2, t=PACK, i=2),
         )
         w2_sc = held("w2_sc", [P, M], U8)
         nc.vector.tensor_copy(
-            w2_sc[:].rearrange("p (a t c i) -> p a t c i", a=2, t=PACK, i=2),
-            w2s_raw[:].rearrange("p (a c t i) -> p a t c i", a=2, t=PACK, i=2),
+            w2_sc[:].bitcast(U16).rearrange("p (a t c) -> p a t c", a=2, t=PACK),
+            w2s_raw.bitcast(U16).rearrange("p (a c t) -> p a t c", a=2, t=PACK),
         )
+        stage1(2)
         stage1(3)
 
-        w4_raw = held("w4_raw", [P, 2, PACK, N], F32, tag="big2")
+        w4_raw = held("w4_raw", [P, 2, PACK, N], F32, tag="slot_a")
         for am in range(2):
             for i in range(2):
                 rows = w4[am * KP : (am + 1) * KP, :].rearrange("(c t i) n -> i c t n", t=PACK, i=2)
                 nc.sync.dma_start(w4_raw[i:P:2, am, :, :], rows[i])
 
-        def stage2(am, c):
-            sl = work.tile([P, CHUNK * PACK], F32, name="act32", tag="act32", bufs=4)
-            cols = slice(c * CHUNK, (c + 1) * CHUNK)
-            for u in range(2):
-                bank = psum.tile([P, 2, CHUNK], F32, name="bank", tag="bank")
-                for e in range(2):
-                    t = 2 * u + e
+        def chunk_part(pair, j0, n):
+            cols = slice(j0 % CHUNK, j0 % CHUNK + n)
+            return pair[0][:, cols].bitcast(FP8X4), pair[1][:, cols]
+
+        def stage2(am, j0, n):
+            slots = KP // n
+            banks = PACK // slots
+            sl = work.tile([P, n * PACK], F32, name="act32", tag="act32", bufs=4)
+            cols = slice(j0, j0 + n)
+            h_codes, h_sc = chunk_part(h_q[j0 // CHUNK], j0, n)
+            for u in range(banks):
+                bank = psum.tile([P, slots, n], F32, name="bank", tag="bank")
+                for e in range(slots):
+                    t = slots * u + e
                     wcols = slice(P * t, P * (t + 1))
                     for g in range(2):
                         nc.tensor.matmul_mx(
@@ -226,29 +238,30 @@ def tile_list_cyclone_intensity_nowcast_kernel(
                         bank[:, e, :],
                         lhsT=w2_codes[:, w2cols].bitcast(FP8X4),
                         lhsT_scale=w2_sc[:, w2cols],
-                        rhs=h_q[c][0][:].bitcast(FP8X4),
-                        rhs_scale=h_q[c][1][:],
+                        rhs=h_codes,
+                        rhs_scale=h_sc,
                         start=False,
                         stop=True,
                     )
                 nc.scalar.activation(
-                    sl[:, u * KP : (u + 1) * KP].rearrange("p (n e) -> p n e", e=2),
+                    sl[:, u * KP : (u + 1) * KP].rearrange("p (n e) -> p n e", e=slots),
                     bank[:].rearrange("p e n -> p n e"),
                     ACT.Silu,
                 )
-            z_bf = work.tile([P, CHUNK * PACK], BF16, name="act16", tag="act16", align_bytes=64)
+            z_bf = work.tile([P, n * PACK], BF16, name="act16", tag="act16", align_bytes=64)
+            gains = gain2_raw[:, am, 0:7:2].rearrange("p (u e) -> p u e", u=banks)
             nc.vector.tensor_tensor(
-                z_bf[:].rearrange("p (n u e) -> p n u e", u=2, e=2),
-                sl[:].rearrange("p (u n e) -> p n u e", u=2, e=2),
-                gain2_raw[:, am, 0:7:2].rearrange("p (u e) -> p u e", u=2).unsqueeze(1).to_broadcast([P, CHUNK, 2, 2]),
+                z_bf[:].rearrange("p (n u e) -> p n u e", u=banks, e=slots),
+                sl[:].rearrange("p (u n e) -> p n u e", u=banks, e=slots),
+                gains.unsqueeze(1).to_broadcast([P, n, banks, slots]),
                 MULT,
             )
-            z_q[(am, c)] = quantize("z%d%d" % (am, c), z_bf, CHUNK)
+            return quantize("z%d_%d" % (am, j0), z_bf, n)
 
         for c in range(CHUNKS):
-            stage2(0, c)
+            z_q[c] = stage2(0, c * CHUNK, CHUNK)
             if c < 2:
-                w3_codes[(c, 1)], w3_sc[(c, 1)] = quantize("w3_%d1" % c, cast_w3(c, 1), KP)
+                w3_codes[(c, 1)], w3_sc[(c, 1)] = quantize("w3_%d1" % c, cast_w3(c, 1, nc.scalar.copy), KP)
 
         w4_bf = work.tile([P, 2 * N * PACK], BF16, name="w_bf", tag="w_bf", align_bytes=64)
         nc.scalar.copy(
@@ -257,8 +270,9 @@ def tile_list_cyclone_intensity_nowcast_kernel(
         )
         w4_codes, w4_sc = quantize("w4", w4_bf, 2 * N)
 
-        def stage3(c):
-            bank = psum.tile([P, 2, CHUNK], F32, name="bank", tag="bank")
+        def stage3(j0, n, z_last):
+            z_parts = [chunk_part(z_q[j0 // CHUNK], j0, n), (z_last[0][:].bitcast(FP8X4), z_last[1][:])]
+            bank = psum.tile([P, 2, n], F32, name="bank", tag="bank")
             for b in range(2):
                 for am in range(2):
                     wcols = slice(am * N + b * P, am * N + (b + 1) * P)
@@ -266,18 +280,21 @@ def tile_list_cyclone_intensity_nowcast_kernel(
                         bank[:, b, :],
                         lhsT=w4_codes[:, wcols].bitcast(FP8X4),
                         lhsT_scale=w4_sc[:, wcols],
-                        rhs=z_q[(am, c)][0][:].bitcast(FP8X4),
-                        rhs_scale=z_q[(am, c)][1][:],
+                        rhs=z_parts[am][0],
+                        rhs_scale=z_parts[am][1],
                         start=(am == 0),
                         stop=(am == 1),
                     )
-            res = work.tile([P, 2, CHUNK], F32, name="res", tag="res")
+            res = work.tile([P, 2, n], F32, name="res", tag="res")
             for b in range(2):
                 nc.scalar.activation(res[:, b, :], bank[:, b, :], ACT.Identity, bias=clim_sb[:, b : b + 1])
-            nc.sync.dma_start(out[:, c * CHUNK : (c + 1) * CHUNK].rearrange("(b p) j -> p b j", p=P), res[:])
+            nc.sync.dma_start(out[:, j0 : j0 + n].rearrange("(b p) j -> p b j", p=P), res[:])
 
-        for c in range(CHUNKS):
-            stage2(1, c)
-            if c > 0:
-                stage3(c - 1)
-        stage3(CHUNKS - 1)
+        pieces = [(c * CHUNK, CHUNK) for c in range(CHUNKS - 1)] + [(S - CHUNK, P), (S - P, P)]
+        waiting = None
+        for j0, n in pieces:
+            z_last = stage2(1, j0, n)
+            if waiting is not None:
+                stage3(*waiting)
+            waiting = (j0, n, z_last)
+        stage3(*waiting)

@@ -15,6 +15,7 @@ FP8X4 = mybir.dt.float8_e4m3fn_x4
 FP4X4 = mybir.dt.float4_e2m1fn_x4
 ACT = mybir.ActivationFunctionType
 MULT = mybir.AluOpType.mult
+ADD = mybir.AluOpType.add
 
 P = 128
 PACK = 4
@@ -22,6 +23,7 @@ KP = P * PACK
 CHUNK = 256
 CHUNKS = S // CHUNK
 LIST_COLS = CHUNK // 16
+SH00, SH10, STEP, AFTER, W4AT = 0, 32, 64, (0, 1), 1
 
 
 def tile_list_cyclone_intensity_nowcast_kernel(
@@ -39,7 +41,7 @@ def tile_list_cyclone_intensity_nowcast_kernel(
         offsets = keep.tile([P, S // 16], U16, name="offsets")
         nc.sync.dma_start(offsets[:], offs)
 
-        w1_raw = held("w1_raw", [P, 2, 2 * H], U8)
+        w1_raw = held("w1_raw", [P, 2, 2 * H], U8, tag="slot_b")
         nc.sync.dma_start(w1_raw[:].bitcast(I32), w1_words.rearrange("a p c -> p a c").bitcast(I32))
 
         scale_window = held("scale_window", [P, T], U8, tag="slot_c")
@@ -51,11 +53,13 @@ def tile_list_cyclone_intensity_nowcast_kernel(
         zero_a = held("zero_a", [P, 1], F32, tag="slot_d")
         zero_b = held("zero_b", [P, 1], F32, tag="slot_f")
         zero_in = held("zero_in", [P, 1], F32, tag="slot_a")
+        zero_shift = held("zero_shift", [P, 1], F32, tag="slot_e")
         zero_bias = held("zero_bias", [P, 1], F32)
         nc.vector.memset(zero_a[:], 0.0)
         nc.vector.memset(zero_b[:], 0.0)
+        nc.gpsimd.memset(zero_shift[:], 0.0)
         nc.vector.tensor_tensor(zero_in[:], zero_a[:], zero_b[:], MULT)
-        nc.scalar.activation(zero_bias[:], zero_in[:], ACT.Silu)
+        nc.scalar.activation(zero_bias[:], zero_in[:], ACT.Silu, bias=zero_shift[:])
 
         def load_window(a, tag):
             window = held("window%d" % a, [P, T], I32, tag=tag)
@@ -71,7 +75,8 @@ def tile_list_cyclone_intensity_nowcast_kernel(
                 w1s_raw[r:P:32, :].rearrange("d (a c) -> d a c", a=2).bitcast(I32),
                 w1_scales[:, r:16:4, :].rearrange("a d c -> d a c").bitcast(I32),
             )
-        windows.append(load_window(1, "slot_a"))
+        v_scales = [held("v_scales%d" % a, [P, S], U8) for a in range(2)]
+        nc.gpsimd.memset(v_scales[1][:].bitcast(I32), 0)
 
         def load_w3(g, am, tag):
             raw = held("w3_raw%d%d" % (g, am), [P, PACK, KP], F32, tag=tag)
@@ -79,26 +84,23 @@ def tile_list_cyclone_intensity_nowcast_kernel(
             nc.sync.dma_start(raw[:], rows.rearrange("(p j) m -> p j m", j=PACK))
             return raw
 
-        w1_sc = held("w1_sc", [P, 2, H], U8)
-        nc.gpsimd.tensor_copy(
-            w1_sc[:].rearrange("p a (t m) -> p a t m", t=PACK),
-            w1s_raw[:].rearrange("p (a m t) -> p a t m", a=2, t=PACK),
-        )
-        vectors = held("vectors", [P, 32], F32)
-        gain2_raw = vectors[:, 0:16].rearrange("p (a x) -> p a x", a=2)
-        gain1_sb = vectors[:, 16 : 16 + PACK]
-        clim_sb = vectors[:, 24 : 24 + N // P]
-        nc.gpsimd.dma_start(gain1_sb, gain1.rearrange("(p t) -> p t", t=PACK))
+        w3_raw = {(0, 0): load_w3(0, 0, "slot_a")}
+        windows.append(load_window(1, "slot_e"))
+
+        gain1_sb = held("gain1_sb", [P, PACK], F32)
+        gain2_raw = held("gain2_raw", [P, 2, 8], F32, tag="slot_g")
+        clim_sb = held("clim_sb", [P, N // P], F32)
+        nc.gpsimd.dma_start(gain1_sb[:], gain1.rearrange("(p t) -> p t", t=PACK))
         for i in range(2):
             nc.gpsimd.dma_start(
                 gain2_raw[i:P:2, :, 0:7], gain2.rearrange("(a c x) -> c a x", a=2, x=8)[:, :, i : i + 7]
             )
         with nc.allow_non_contiguous_dma(reason="one value a partition"):
-            nc.gpsimd.dma_start(clim_sb, clim.rearrange("(b p) -> p b", p=P))
+            nc.gpsimd.dma_start(clim_sb[:], clim.rearrange("(b p) -> p b", p=P))
+        gain2_sb = held("gain2_sb", [P, 2, PACK], F32)
+        nc.gpsimd.tensor_copy(gain2_sb[:], gain2_raw[:, :, 0:7:2])
 
-        v_scales = [held("v_scales%d" % a, [P, S], U8) for a in range(2)]
-        nc.vector.memset(v_scales[1][:].bitcast(I32), 0)
-        picked_scales = held("picked_scales", [P, S], U8, tag="slot_e")
+        picked_scales = held("picked_scales", [P, S], U8)
         nc.vector.tensor_copy(picked_scales[:], scale_window[:].indirect(offsets[:]))
         nc.vector.tensor_copy(v_scales[0][:].bitcast(I32), picked_scales[:].bitcast(I32))
         for r in range(4):
@@ -109,38 +111,53 @@ def tile_list_cyclone_intensity_nowcast_kernel(
             nc.sync.dma_start(
                 v_scales[0][r:P:32, :].bitcast(I32), picked_scales[14 + r : P : 32, :].bitcast(I32)
             )
-        w3_raw = {(0, 0): load_w3(0, 0, "slot_c"), (1, 0): load_w3(1, 0, "slot_e")}
+        w3_raw[(1, 0)] = load_w3(1, 0, "slot_c")
 
         w1_codes = held("w1_codes", [P, 2, 2 * H], U8)
         nc.vector.tensor_copy(
             w1_codes[:].bitcast(U16).rearrange("p a (t m) -> p a t m", t=PACK),
             w1_raw[:].bitcast(U16).rearrange("p a (m t) -> p a t m", t=PACK),
         )
+        w1_sc = held("w1_sc", [P, 2, H], U8)
+        nc.vector.tensor_copy(
+            w1_sc[:].rearrange("p a (t m) -> p a t m", t=PACK),
+            w1s_raw[:].rearrange("p (a m t) -> p a t m", a=2, t=PACK),
+        )
 
         v_codes = [held("v_codes%d" % a, [P, S], U32) for a in range(2)]
-        for c in range(CHUNKS):
-            for a in range(2):
-                nc.vector.tensor_copy(
-                    v_codes[a][:, c * CHUNK : (c + 1) * CHUNK],
-                    windows[a][:].bitcast(U32).indirect(offsets[:, c * LIST_COLS : (c + 1) * LIST_COLS]),
-                )
 
-        w2_staged = held("w2_staged", [P, M + M // 4], I32, tag="slot_a")
-        w2_raw = w2_staged[:, 0:M]
-        w2s_raw = w2_staged[:, M:]
-        nc.sync.dma_start(w2_raw, w2_words[0].rearrange("p c i -> p (c i)").bitcast(I32))
-        nc.vector.memset(w2s_raw, 0)
+        def gather_words(a, j0, n):
+            nc.vector.tensor_copy(
+                v_codes[a][:, j0 : j0 + n],
+                windows[a][:].bitcast(U32).indirect(offsets[:, j0 // 16 : (j0 + n) // 16]),
+            )
+
+        gather_words(0, 0, S)
+        for j0, n in ((0, CHUNK), (CHUNK, CHUNK), (2 * CHUNK, 2 * CHUNK)):
+            gather_words(1, j0, n)
+
+        w2s_raw = held("w2s_raw", [P, M], U8, tag="slot_b")
+        nc.gpsimd.memset(w2s_raw[:].bitcast(I32), 0)
         for r in range(4):
-            nc.sync.dma_start(w2_staged[r:P:32, M:], w2_scales[0, r:16:4, :].bitcast(I32))
+            nc.sync.dma_start(w2s_raw[r:P:32, :].bitcast(I32), w2_scales[0, r:16:4, :].bitcast(I32))
+        w2_raw = held("w2_raw", [P, M], I32, tag="slot_g")
+        nc.sync.dma_start(w2_raw[:], w2_words[0].rearrange("p c i -> p (c i)").bitcast(I32))
+        w2_codes = held("w2_codes", [P, M], I32)
+        nc.vector.tensor_copy(
+            w2_codes[:].rearrange("p (a t c i) -> p a t c i", a=2, t=PACK, i=2),
+            w2_raw[:].rearrange("p (a c t i) -> p a t c i", a=2, t=PACK, i=2),
+        )
 
         w3_codes, w3_sc = {}, {}
 
-        def cast_w3(g, am, copy):
+        def cast_w3(g, am, vector_share):
             grouped = work.tile([P, KP * PACK], BF16, name="w_bf", tag="w_bf", align_bytes=64)
-            copy(
-                grouped[:].rearrange("p (t c i j) -> p c t j i", t=PACK, i=2, j=PACK),
-                w3_raw[(g, am)][:].rearrange("p j (c t i) -> p c t j i", t=PACK, i=2),
-            )
+            dst = grouped[:].rearrange("p (t c i j) -> p c t j i", t=PACK, i=2, j=PACK)
+            src = w3_raw[(g, am)][:].rearrange("p j (c t i) -> p c t j i", t=PACK, i=2)
+            if vector_share > 0:
+                nc.vector.tensor_copy(dst[:, :vector_share], src[:, :vector_share])
+            for c0 in range(vector_share, 64, STEP):
+                nc.scalar.copy(dst[:, c0 : min(64, c0 + STEP)], src[:, c0 : min(64, c0 + STEP)])
             return grouped
 
         def quantize(name, grouped, width):
@@ -177,32 +194,27 @@ def tile_list_cyclone_intensity_nowcast_kernel(
             nc.vector.tensor_tensor(
                 h_bf[:].rearrange("p (n t) -> p n t", t=PACK),
                 th[:].rearrange("p (n t) -> p n t", t=PACK),
-                gain1_sb.unsqueeze(1).to_broadcast([P, CHUNK, PACK]),
+                gain1_sb[:].unsqueeze(1).to_broadcast([P, CHUNK, PACK]),
                 MULT,
             )
             h_q[c] = quantize("h%d" % c, h_bf, CHUNK)
 
         stage1(0)
-        w3_codes[(0, 0)], w3_sc[(0, 0)] = quantize("w3_00", cast_w3(0, 0, nc.scalar.copy), KP)
-        w3_raw[(0, 1)] = load_w3(0, 1, "slot_c")
-        w3_codes[(1, 0)], w3_sc[(1, 0)] = quantize("w3_10", cast_w3(1, 0, nc.vector.tensor_copy), KP)
+        w3_codes[(0, 0)], w3_sc[(0, 0)] = quantize("w3_00", cast_w3(0, 0, SH00), KP)
+        w3_raw[(0, 1)] = load_w3(0, 1, "slot_a")
+        w3_codes[(1, 0)], w3_sc[(1, 0)] = quantize("w3_10", cast_w3(1, 0, SH10), KP)
         w3_raw[(1, 1)] = load_w3(1, 1, "slot_e")
         stage1(1)
 
-        w2_codes = held("w2_codes", [P, M], I32)
-        nc.vector.tensor_copy(
-            w2_codes[:].rearrange("p (a t c i) -> p a t c i", a=2, t=PACK, i=2),
-            w2_raw.rearrange("p (a c t i) -> p a t c i", a=2, t=PACK, i=2),
-        )
         w2_sc = held("w2_sc", [P, M], U8)
         nc.vector.tensor_copy(
             w2_sc[:].bitcast(U16).rearrange("p (a t c) -> p a t c", a=2, t=PACK),
-            w2s_raw.bitcast(U16).rearrange("p (a c t) -> p a t c", a=2, t=PACK),
+            w2s_raw[:].bitcast(U16).rearrange("p (a c t) -> p a t c", a=2, t=PACK),
         )
         stage1(2)
         stage1(3)
 
-        w4_raw = held("w4_raw", [P, 2, PACK, N], F32, tag="slot_a")
+        w4_raw = held("w4_raw", [P, 2, PACK, N], F32, tag="slot_c")
         for am in range(2):
             for i in range(2):
                 rows = w4[am * KP : (am + 1) * KP, :].rearrange("(c t i) n -> i c t n", t=PACK, i=2)
@@ -249,7 +261,7 @@ def tile_list_cyclone_intensity_nowcast_kernel(
                     ACT.Silu,
                 )
             z_bf = work.tile([P, n * PACK], BF16, name="act16", tag="act16", align_bytes=64)
-            gains = gain2_raw[:, am, 0:7:2].rearrange("p (u e) -> p u e", u=banks)
+            gains = gain2_sb[:, am, :].rearrange("p (u e) -> p u e", u=banks)
             nc.vector.tensor_tensor(
                 z_bf[:].rearrange("p (n u e) -> p n u e", u=banks, e=slots),
                 sl[:].rearrange("p (u n e) -> p n u e", u=banks, e=slots),
@@ -258,23 +270,27 @@ def tile_list_cyclone_intensity_nowcast_kernel(
             )
             return quantize("z%d_%d" % (am, j0), z_bf, n)
 
-        for c in range(CHUNKS):
-            z_q[c] = stage2(0, c * CHUNK, CHUNK)
-            if c < 2:
-                w3_codes[(c, 1)], w3_sc[(c, 1)] = quantize("w3_%d1" % c, cast_w3(c, 1, nc.scalar.copy), KP)
+        for c in range(-1, CHUNKS):
+            if c >= 0:
+                z_q[c] = stage2(0, c * CHUNK, CHUNK)
+            for g in range(2):
+                if c == AFTER[g]:
+                    w3_codes[(g, 1)], w3_sc[(g, 1)] = quantize("w3_%d1" % g, cast_w3(g, 1, 0), KP)
 
-        w4_bf = work.tile([P, 2 * N * PACK], BF16, name="w_bf", tag="w_bf", align_bytes=64)
-        nc.scalar.copy(
-            w4_bf[:].rearrange("p (a c i t) -> p a c t i", a=2, t=PACK, i=2),
-            w4_raw[:].rearrange("p a t (c i) -> p a c t i", i=2),
-        )
-        w4_codes, w4_sc = quantize("w4", w4_bf, 2 * N)
+        def prepare_w4():
+            w4_bf = work.tile([P, 2 * N * PACK], BF16, name="w_bf", tag="w_bf", align_bytes=64)
+            for am, copy in enumerate((nc.scalar.copy, nc.scalar.copy)):
+                copy(
+                    w4_bf[:, am * N * PACK : (am + 1) * N * PACK].rearrange("p (c i t) -> p c t i", t=PACK, i=2),
+                    w4_raw[:, am].rearrange("p t (c i) -> p c t i", i=2),
+                )
+            return quantize("w4", w4_bf, 2 * N)
 
         def stage3(j0, n, z_last):
             z_parts = [chunk_part(z_q[j0 // CHUNK], j0, n), (z_last[0][:].bitcast(FP8X4), z_last[1][:])]
             bank = psum.tile([P, 2, n], F32, name="bank", tag="bank")
-            for b in range(2):
-                for am in range(2):
+            for am in range(2):
+                for b in range(2):
                     wcols = slice(am * N + b * P, am * N + (b + 1) * P)
                     nc.tensor.matmul_mx(
                         bank[:, b, :],
@@ -282,19 +298,22 @@ def tile_list_cyclone_intensity_nowcast_kernel(
                         lhsT_scale=w4_sc[:, wcols],
                         rhs=z_parts[am][0],
                         rhs_scale=z_parts[am][1],
-                        start=(am == 0),
-                        stop=(am == 1),
+                        start=(am == 0 and b == 0),
+                        stop=(am == 1 and b == 1),
                     )
-            res = work.tile([P, 2, n], F32, name="res", tag="res")
-            for b in range(2):
-                nc.scalar.activation(res[:, b, :], bank[:, b, :], ACT.Identity, bias=clim_sb[:, b : b + 1])
+            res = work.tile([P, 2, n], F32, name="res", tag="res", bufs=5)
+            if j0 + n == S:
+                nc.vector.tensor_tensor(res[:], bank[:], clim_sb[:].unsqueeze(2).to_broadcast([P, 2, n]), ADD)
+            else:
+                for b in range(2):
+                    nc.scalar.activation(res[:, b, :], bank[:, b, :], ACT.Identity, bias=clim_sb[:, b : b + 1])
             nc.sync.dma_start(out[:, j0 : j0 + n].rearrange("(b p) j -> p b j", p=P), res[:])
 
         pieces = [(c * CHUNK, CHUNK) for c in range(CHUNKS - 1)] + [(S - CHUNK, P), (S - P, P)]
-        waiting = None
-        for j0, n in pieces:
-            z_last = stage2(1, j0, n)
-            if waiting is not None:
-                stage3(*waiting)
-            waiting = (j0, n, z_last)
-        stage3(*waiting)
+        z_last = []
+        for k, (j0, n) in enumerate(pieces):
+            if k == W4AT:
+                w4_codes, w4_sc = prepare_w4()
+            z_last.append(stage2(1, j0, n))
+        for (j0, n), z in zip(pieces, z_last):
+            stage3(j0, n, z)

@@ -19,11 +19,11 @@ ADD = mybir.AluOpType.add
 
 P = 128
 PACK = 4
-KP = P * PACK
+PASS = P * PACK
+ROWS = PASS // 32
+GROUP = 16
 CHUNK = 256
-CHUNKS = S // CHUNK
-LIST_COLS = CHUNK // 16
-SH00, SH10, STEP, AFTER, W4AT = 0, 32, 64, (0, 1), 1
+HALF = PASS // 2
 
 
 def tile_list_cyclone_intensity_nowcast_kernel(
@@ -35,25 +35,28 @@ def tile_list_cyclone_intensity_nowcast_kernel(
         work = ctx.enter_context(tc.tile_pool(name="work", bufs=3))
         psum = ctx.enter_context(tc.psum_pool(name="psum", bufs=8))
 
-        def held(name, shape, dtype, tag=None):
-            return keep.tile(shape, dtype, name=name, tag=tag or name, align_bytes=64)
+        def held(name, shape, dtype, slot=None):
+            return keep.tile(shape, dtype, name=name, tag=slot or name, align_bytes=64)
 
-        offsets = keep.tile([P, S // 16], U16, name="offsets")
+        def words(ap):
+            return ap.bitcast(I32)
+
+        offsets = keep.tile([P, S // GROUP], U16, name="offsets")
         nc.sync.dma_start(offsets[:], offs)
 
-        w1_raw = held("w1_raw", [P, 2, 2 * H], U8, tag="slot_b")
-        nc.sync.dma_start(w1_raw[:].bitcast(I32), w1_words.rearrange("a p c -> p a c").bitcast(I32))
+        w1_raw = held("w1_raw", [P, 2, 2 * H], U8, "slot_w1")
+        nc.sync.dma_start(words(w1_raw[:]), words(w1_words.rearrange("a p c -> p a c")))
 
-        scale_window = held("scale_window", [P, T], U8, tag="slot_c")
-        nc.vector.memset(scale_window[:].bitcast(I32), 0)
-        for e in range(2):
-            nc.sync.dma_start(scale_window[e:P:16, :].bitcast(I32), tab_scales[0, e:16:2, :].bitcast(I32))
-        nc.sync.dma_start(scale_window[4:P:8, :].bitcast(I32), tab_scales[1].bitcast(I32))
+        scale_window = held("scale_window", [P, T], U8, "slot_scales")
+        nc.vector.memset(words(scale_window[:]), 0)
+        for odd in range(2):
+            nc.sync.dma_start(words(scale_window[odd:P:GROUP, :]), words(tab_scales[0, odd:ROWS:2, :]))
+        nc.sync.dma_start(words(scale_window[4:P:8, :]), words(tab_scales[1]))
 
-        zero_a = held("zero_a", [P, 1], F32, tag="slot_d")
-        zero_b = held("zero_b", [P, 1], F32, tag="slot_f")
-        zero_in = held("zero_in", [P, 1], F32, tag="slot_a")
-        zero_shift = held("zero_shift", [P, 1], F32, tag="slot_e")
+        zero_a = held("zero_a", [P, 1], F32, "slot_table0")
+        zero_b = held("zero_b", [P, 1], F32, "slot_w1_scales")
+        zero_in = held("zero_in", [P, 1], F32, "slot_w3_first")
+        zero_shift = held("zero_shift", [P, 1], F32, "slot_table1")
         zero_bias = held("zero_bias", [P, 1], F32)
         nc.vector.memset(zero_a[:], 0.0)
         nc.vector.memset(zero_b[:], 0.0)
@@ -61,34 +64,35 @@ def tile_list_cyclone_intensity_nowcast_kernel(
         nc.vector.tensor_tensor(zero_in[:], zero_a[:], zero_b[:], MULT)
         nc.scalar.activation(zero_bias[:], zero_in[:], ACT.Silu, bias=zero_shift[:])
 
-        def load_window(a, tag):
-            window = held("window%d" % a, [P, T], I32, tag=tag)
-            nc.sync.dma_start(window[:], tab_words[a].rearrange("p t i -> p (t i)").bitcast(I32))
+        def load_table(a, slot):
+            window = held("table%d" % a, [P, T], I32, slot)
+            nc.sync.dma_start(window[:], words(tab_words[a].rearrange("p t i -> p (t i)")))
             return window
 
-        windows = [load_window(0, "slot_d")]
-
-        w1s_raw = held("w1s_raw", [P, 2 * H], U8, tag="slot_f")
-        nc.vector.memset(w1s_raw[:].bitcast(I32), 0)
-        for r in range(4):
-            nc.sync.dma_start(
-                w1s_raw[r:P:32, :].rearrange("d (a c) -> d a c", a=2).bitcast(I32),
-                w1_scales[:, r:16:4, :].rearrange("a d c -> d a c").bitcast(I32),
-            )
-        v_scales = [held("v_scales%d" % a, [P, S], U8) for a in range(2)]
-        nc.gpsimd.memset(v_scales[1][:].bitcast(I32), 0)
-
-        def load_w3(g, am, tag):
-            raw = held("w3_raw%d%d" % (g, am), [P, PACK, KP], F32, tag=tag)
-            rows = w3[g * KP : (g + 1) * KP, am * KP : (am + 1) * KP]
-            nc.sync.dma_start(raw[:], rows.rearrange("(p j) m -> p j m", j=PACK))
+        def load_w3(a, m0, width, slot):
+            raw = held("w3_raw%d_%d" % (a, m0), [P, PACK, width], F32, slot)
+            rows = w3[a * PASS : (a + 1) * PASS, m0 : m0 + width]
+            nc.sync.dma_start(raw[:], rows.rearrange("(p t) m -> p t m", t=PACK))
             return raw
 
-        w3_raw = {(0, 0): load_w3(0, 0, "slot_a")}
-        windows.append(load_window(1, "slot_e"))
+        tables = [load_table(0, "slot_table0")]
+
+        w1s_raw = held("w1s_raw", [P, 2 * H], U8, "slot_w1_scales")
+        nc.vector.memset(words(w1s_raw[:]), 0)
+        for r in range(4):
+            nc.sync.dma_start(
+                words(w1s_raw[r:P:32, :].rearrange("d (a c) -> d a c", a=2)),
+                words(w1_scales[:, r:ROWS:4, :].rearrange("a d c -> d a c")),
+            )
+
+        w3_first = [load_w3(0, 0, HALF, "slot_w3_first")]
+        tables.append(load_table(1, "slot_table1"))
+
+        v_scales = [held("v_scales%d" % a, [P, S], U8) for a in range(2)]
+        nc.gpsimd.memset(words(v_scales[1][:]), 0)
 
         gain1_sb = held("gain1_sb", [P, PACK], F32)
-        gain2_raw = held("gain2_raw", [P, 2, 8], F32, tag="slot_g")
+        gain2_raw = held("gain2_raw", [P, 2, 8], F32, "slot_w2")
         clim_sb = held("clim_sb", [P, N // P], F32)
         nc.gpsimd.dma_start(gain1_sb[:], gain1.rearrange("(p t) -> p t", t=PACK))
         for i in range(2):
@@ -102,63 +106,49 @@ def tile_list_cyclone_intensity_nowcast_kernel(
 
         picked_scales = held("picked_scales", [P, S], U8)
         nc.vector.tensor_copy(picked_scales[:], scale_window[:].indirect(offsets[:]))
-        nc.vector.tensor_copy(v_scales[0][:].bitcast(I32), picked_scales[:].bitcast(I32))
+        nc.vector.tensor_copy(words(v_scales[0][:]), words(picked_scales[:]))
         for r in range(4):
-            nc.sync.dma_start(
-                v_scales[1][r:P:32, :].bitcast(I32), picked_scales[8 * r + 4 : P : 32, :].bitcast(I32)
-            )
+            nc.sync.dma_start(words(v_scales[1][r:P:32, :]), words(picked_scales[8 * r + 4 : P : 32, :]))
         for r in range(2, 4):
-            nc.sync.dma_start(
-                v_scales[0][r:P:32, :].bitcast(I32), picked_scales[14 + r : P : 32, :].bitcast(I32)
-            )
-        w3_raw[(1, 0)] = load_w3(1, 0, "slot_c")
+            nc.sync.dma_start(words(v_scales[0][r:P:32, :]), words(picked_scales[GROUP + r - 2 : P : 32, :]))
+        w3_second = load_w3(1, 0, PASS, "slot_scales")
 
         w1_codes = held("w1_codes", [P, 2, 2 * H], U8)
         nc.vector.tensor_copy(
-            w1_codes[:].bitcast(U16).rearrange("p a (t m) -> p a t m", t=PACK),
-            w1_raw[:].bitcast(U16).rearrange("p a (m t) -> p a t m", t=PACK),
+            w1_codes[:].bitcast(U16).rearrange("p a (t c) -> p a t c", t=PACK),
+            w1_raw[:].bitcast(U16).rearrange("p a (c t) -> p a t c", t=PACK),
         )
         w1_sc = held("w1_sc", [P, 2, H], U8)
         nc.vector.tensor_copy(
-            w1_sc[:].rearrange("p a (t m) -> p a t m", t=PACK),
-            w1s_raw[:].rearrange("p (a m t) -> p a t m", a=2, t=PACK),
+            w1_sc[:].rearrange("p a (t c) -> p a t c", t=PACK),
+            w1s_raw[:].rearrange("p (a c t) -> p a t c", a=2, t=PACK),
         )
+        w3_first.append(load_w3(0, HALF, HALF, "slot_w1_scales"))
 
         v_codes = [held("v_codes%d" % a, [P, S], U32) for a in range(2)]
 
         def gather_words(a, j0, n):
             nc.vector.tensor_copy(
                 v_codes[a][:, j0 : j0 + n],
-                windows[a][:].bitcast(U32).indirect(offsets[:, j0 // 16 : (j0 + n) // 16]),
+                tables[a][:].bitcast(U32).indirect(offsets[:, j0 // GROUP : (j0 + n) // GROUP]),
             )
 
-        gather_words(0, 0, S)
+        gather_words(0, 0, CHUNK)
+        gather_words(0, CHUNK, S - CHUNK)
         for j0, n in ((0, CHUNK), (CHUNK, CHUNK), (2 * CHUNK, 2 * CHUNK)):
             gather_words(1, j0, n)
 
-        w2s_raw = held("w2s_raw", [P, M], U8, tag="slot_b")
-        nc.gpsimd.memset(w2s_raw[:].bitcast(I32), 0)
+        w2s_raw = held("w2s_raw", [P, M], U8, "slot_w1")
+        nc.gpsimd.memset(words(w2s_raw[:]), 0)
         for r in range(4):
-            nc.sync.dma_start(w2s_raw[r:P:32, :].bitcast(I32), w2_scales[0, r:16:4, :].bitcast(I32))
-        w2_raw = held("w2_raw", [P, M], I32, tag="slot_g")
-        nc.sync.dma_start(w2_raw[:], w2_words[0].rearrange("p c i -> p (c i)").bitcast(I32))
+            nc.sync.dma_start(words(w2s_raw[r:P:32, :]), words(w2_scales[0, r:ROWS:4, :]))
+        w2_raw = held("w2_raw", [P, M], I32, "slot_w2")
+        nc.sync.dma_start(w2_raw[:], words(w2_words[0].rearrange("p c i -> p (c i)")))
         w2_codes = held("w2_codes", [P, M], I32)
         nc.vector.tensor_copy(
             w2_codes[:].rearrange("p (a t c i) -> p a t c i", a=2, t=PACK, i=2),
             w2_raw[:].rearrange("p (a c t i) -> p a t c i", a=2, t=PACK, i=2),
         )
-
-        w3_codes, w3_sc = {}, {}
-
-        def cast_w3(g, am, vector_share):
-            grouped = work.tile([P, KP * PACK], BF16, name="w_bf", tag="w_bf", align_bytes=64)
-            dst = grouped[:].rearrange("p (t c i j) -> p c t j i", t=PACK, i=2, j=PACK)
-            src = w3_raw[(g, am)][:].rearrange("p j (c t i) -> p c t j i", t=PACK, i=2)
-            if vector_share > 0:
-                nc.vector.tensor_copy(dst[:, :vector_share], src[:, :vector_share])
-            for c0 in range(vector_share, 64, STEP):
-                nc.scalar.copy(dst[:, c0 : min(64, c0 + STEP)], src[:, c0 : min(64, c0 + STEP)])
-            return grouped
 
         def quantize(name, grouped, width):
             codes = held(name + "_codes", [P, width], U32)
@@ -166,154 +156,153 @@ def tile_list_cyclone_intensity_nowcast_kernel(
             nc.vector.quantize_mx(codes[:].bitcast(FP8X4), scales[:], grouped[:])
             return codes, scales
 
-        h_q, z_q = {}, {}
+        def prepare_w3(name, parts):
+            grouped = work.tile([P, PASS * PACK], BF16, name="w_bf", tag="w_bf", align_bytes=64)
+            dst = grouped[:].rearrange("p (t c i x) -> p c t x i", t=PACK, i=2, x=PACK)
+            c0 = 0
+            for raw, cast in parts:
+                src = raw.rearrange("p x (c t i) -> p c t x i", t=PACK, i=2)
+                cast(dst[:, c0 : c0 + src.shape[1]], src)
+                c0 = c0 + src.shape[1]
+            return quantize(name, grouped, PASS)
 
-        def stage1(c):
-            th = work.tile([P, CHUNK * PACK], F32, name="act32", tag="act32", bufs=4)
-            for half in range(2):
-                bank = psum.tile([P, PACK, P], F32, name="bank", tag="bank")
-                cols = slice(c * CHUNK + half * P, c * CHUNK + (half + 1) * P)
-                for t in range(PACK):
-                    for a in range(2):
+        def columns(done, j0, n):
+            first = max(j for j in done if j <= j0)
+            cols = slice(j0 - first, j0 - first + n)
+            return done[first][0][:, cols].bitcast(FP8X4), done[first][1][:, cols]
+
+        def scale_and_quantize(name, done, runs):
+            total = sum(run[1] for run in runs)
+            grouped = work.tile([P, total * PACK], BF16, name="act16", tag="act16", align_bytes=64)
+            for j0, n, values, gains in runs:
+                c0 = (j0 - runs[0][0]) * PACK
+                dst = grouped[:, c0 : c0 + n * PACK].rearrange("p (j u e) -> p j u e", j=n, u=values.shape[2])
+                nc.vector.tensor_tensor(dst, values, gains.unsqueeze(1).to_broadcast(list(values.shape)), MULT)
+            done[runs[0][0]] = quantize("%s_%d" % (name, runs[0][0]), grouped, total)
+
+        def activations(n):
+            return work.tile([P, n * PACK], F32, name="act32", tag="act32", bufs=4)
+
+        def stage1(j0):
+            th = activations(CHUNK)
+            banks = [psum.tile([P, PACK, P], F32, name="bank", tag="bank") for half in range(CHUNK // P)]
+            for a in range(2):
+                for half, bank in enumerate(banks):
+                    cols = slice(j0 + half * P, j0 + (half + 1) * P)
+                    for t in range(PACK):
                         nc.tensor.matmul_mx(
                             bank[:, t, :],
                             lhsT=w1_codes[:, a, 2 * P * t : 2 * P * (t + 1)].bitcast(FP4X4),
                             lhsT_scale=w1_sc[:, a, P * t : P * (t + 1)],
                             rhs=v_codes[a][:, cols].bitcast(FP8X4),
                             rhs_scale=v_scales[a][:, cols],
-                            start=(a == 0),
-                            stop=(a == 1),
+                            start=(a == 0 and t == 0),
+                            stop=(a == 1 and t == PACK - 1),
                         )
+            for half, bank in enumerate(banks):
                 nc.scalar.activation(
-                    th[:, half * KP : (half + 1) * KP].rearrange("p (n t) -> p n t", t=PACK),
-                    bank[:].rearrange("p t n -> p n t"),
+                    th[:, half * PASS : (half + 1) * PASS].rearrange("p (j t) -> p j t", t=PACK),
+                    bank[:].rearrange("p t j -> p j t"),
                     ACT.Tanh,
                     bias=zero_bias[:],
                 )
-            h_bf = work.tile([P, CHUNK * PACK], BF16, name="act16", tag="act16", align_bytes=64)
-            nc.vector.tensor_tensor(
-                h_bf[:].rearrange("p (n t) -> p n t", t=PACK),
-                th[:].rearrange("p (n t) -> p n t", t=PACK),
-                gain1_sb[:].unsqueeze(1).to_broadcast([P, CHUNK, PACK]),
-                MULT,
-            )
-            h_q[c] = quantize("h%d" % c, h_bf, CHUNK)
+            return j0, CHUNK, th[:].rearrange("p (j u e) -> p j u e", u=1, e=PACK), gain1_sb[:].unsqueeze(1)
 
-        stage1(0)
-        w3_codes[(0, 0)], w3_sc[(0, 0)] = quantize("w3_00", cast_w3(0, 0, SH00), KP)
-        w3_raw[(0, 1)] = load_w3(0, 1, "slot_a")
-        w3_codes[(1, 0)], w3_sc[(1, 0)] = quantize("w3_10", cast_w3(1, 0, SH10), KP)
-        w3_raw[(1, 1)] = load_w3(1, 1, "slot_e")
-        stage1(1)
+        h_done, w3_done = {}, {}
+        scale_and_quantize("h", h_done, [stage1(0)])
+        w3_done[(0, 0)] = prepare_w3("w3_00", [(raw[:], nc.scalar.copy) for raw in w3_first])
+        w3_done[(1, 0)] = prepare_w3("w3_10", [(w3_second[:], nc.vector.tensor_copy)])
+        w3_late = [load_w3(0, PASS, PASS, "slot_table1"), load_w3(1, PASS, PASS, "slot_w1_scales")]
+        scale_and_quantize("h", h_done, [stage1(CHUNK)])
 
         w2_sc = held("w2_sc", [P, M], U8)
         nc.vector.tensor_copy(
             w2_sc[:].bitcast(U16).rearrange("p (a t c) -> p a t c", a=2, t=PACK),
             w2s_raw[:].bitcast(U16).rearrange("p (a c t) -> p a t c", a=2, t=PACK),
         )
-        stage1(2)
-        stage1(3)
+        for j0 in (2 * CHUNK, 3 * CHUNK):
+            scale_and_quantize("h", h_done, [stage1(j0)])
 
-        w4_raw = held("w4_raw", [P, 2, PACK, N], F32, tag="slot_c")
+        w4_raw = held("w4_raw", [P, 2, PACK, N], F32, "slot_scales")
         for am in range(2):
+            rows = w4[am * PASS : (am + 1) * PASS, :].rearrange("(c t i) n -> i c t n", t=PACK, i=2)
             for i in range(2):
-                rows = w4[am * KP : (am + 1) * KP, :].rearrange("(c t i) n -> i c t n", t=PACK, i=2)
                 nc.sync.dma_start(w4_raw[i:P:2, am, :, :], rows[i])
 
-        def chunk_part(pair, j0, n):
-            cols = slice(j0 % CHUNK, j0 % CHUNK + n)
-            return pair[0][:, cols].bitcast(FP8X4), pair[1][:, cols]
-
         def stage2(am, j0, n):
-            slots = KP // n
-            banks = PACK // slots
-            sl = work.tile([P, n * PACK], F32, name="act32", tag="act32", bufs=4)
+            per_bank = PASS // n
+            banks = PACK // per_bank
+            sl = activations(n)
             cols = slice(j0, j0 + n)
-            h_codes, h_sc = chunk_part(h_q[j0 // CHUNK], j0, n)
+            h_codes, h_sc = columns(h_done, j0, n)
             for u in range(banks):
-                bank = psum.tile([P, slots, n], F32, name="bank", tag="bank")
-                for e in range(slots):
-                    t = slots * u + e
-                    wcols = slice(P * t, P * (t + 1))
-                    for g in range(2):
+                bank = psum.tile([P, per_bank, n], F32, name="bank", tag="bank")
+                for step in range(3):
+                    for e in range(per_bank):
+                        wcols = slice(P * (per_bank * u + e), P * (per_bank * u + e + 1))
+                        if step < 2:
+                            w_codes, w_sc = w3_done[(step, am)][0][:, wcols], w3_done[(step, am)][1][:, wcols]
+                            x_codes, x_sc = v_codes[step][:, cols].bitcast(FP8X4), v_scales[step][:, cols]
+                        else:
+                            w2cols = slice(am * PASS + wcols.start, am * PASS + wcols.stop)
+                            w_codes, w_sc = w2_codes[:, w2cols], w2_sc[:, w2cols]
+                            x_codes, x_sc = h_codes, h_sc
                         nc.tensor.matmul_mx(
                             bank[:, e, :],
-                            lhsT=w3_codes[(g, am)][:, wcols].bitcast(FP8X4),
-                            lhsT_scale=w3_sc[(g, am)][:, wcols],
-                            rhs=v_codes[g][:, cols].bitcast(FP8X4),
-                            rhs_scale=v_scales[g][:, cols],
-                            start=(g == 0),
-                            stop=False,
+                            lhsT=w_codes.bitcast(FP8X4),
+                            lhsT_scale=w_sc,
+                            rhs=x_codes,
+                            rhs_scale=x_sc,
+                            start=(step == 0 and e == 0),
+                            stop=(step == 2 and e == per_bank - 1),
                         )
-                    w2cols = slice(am * KP + P * t, am * KP + P * (t + 1))
-                    nc.tensor.matmul_mx(
-                        bank[:, e, :],
-                        lhsT=w2_codes[:, w2cols].bitcast(FP8X4),
-                        lhsT_scale=w2_sc[:, w2cols],
-                        rhs=h_codes,
-                        rhs_scale=h_sc,
-                        start=False,
-                        stop=True,
-                    )
                 nc.scalar.activation(
-                    sl[:, u * KP : (u + 1) * KP].rearrange("p (n e) -> p n e", e=slots),
-                    bank[:].rearrange("p e n -> p n e"),
+                    sl[:, u * PASS : (u + 1) * PASS].rearrange("p (j e) -> p j e", e=per_bank),
+                    bank[:].rearrange("p e j -> p j e"),
                     ACT.Silu,
                 )
-            z_bf = work.tile([P, n * PACK], BF16, name="act16", tag="act16", align_bytes=64)
-            gains = gain2_sb[:, am, :].rearrange("p (u e) -> p u e", u=banks)
-            nc.vector.tensor_tensor(
-                z_bf[:].rearrange("p (n u e) -> p n u e", u=banks, e=slots),
-                sl[:].rearrange("p (u n e) -> p n u e", u=banks, e=slots),
-                gains.unsqueeze(1).to_broadcast([P, n, banks, slots]),
-                MULT,
+            values = sl[:].rearrange("p (u j e) -> p j u e", u=banks, e=per_bank)
+            return j0, n, values, gain2_sb[:, am, :].rearrange("p (u e) -> p u e", u=banks)
+
+        z_done = [{}, {}]
+        for c in range(S // CHUNK):
+            scale_and_quantize("z0", z_done[0], [stage2(0, c * CHUNK, CHUNK)])
+            if c < len(w3_late):
+                w3_done[(c, 1)] = prepare_w3("w3_%d1" % c, [(w3_late[c][:], nc.scalar.copy)])
+
+        pieces = [(j0, CHUNK) for j0 in range(0, S - CHUNK, CHUNK)] + [(S - CHUNK, P), (S - P, P)]
+        scale_and_quantize("z1", z_done[1], [stage2(1, *pieces[0])])
+
+        w4_bf = work.tile([P, 2 * N * PACK], BF16, name="w_bf", tag="w_bf", align_bytes=64)
+        for am in range(2):
+            nc.scalar.copy(
+                w4_bf[:, am * N * PACK : (am + 1) * N * PACK].rearrange("p (c i t) -> p c t i", t=PACK, i=2),
+                w4_raw[:, am].rearrange("p t (c i) -> p c t i", i=2),
             )
-            return quantize("z%d_%d" % (am, j0), z_bf, n)
+        w4_codes, w4_sc = quantize("w4", w4_bf, 2 * N)
 
-        for c in range(-1, CHUNKS):
-            if c >= 0:
-                z_q[c] = stage2(0, c * CHUNK, CHUNK)
-            for g in range(2):
-                if c == AFTER[g]:
-                    w3_codes[(g, 1)], w3_sc[(g, 1)] = quantize("w3_%d1" % g, cast_w3(g, 1, 0), KP)
+        for j0, n in pieces[1:]:
+            scale_and_quantize("z1", z_done[1], [stage2(1, j0, n)])
 
-        def prepare_w4():
-            w4_bf = work.tile([P, 2 * N * PACK], BF16, name="w_bf", tag="w_bf", align_bytes=64)
-            for am, copy in enumerate((nc.scalar.copy, nc.scalar.copy)):
-                copy(
-                    w4_bf[:, am * N * PACK : (am + 1) * N * PACK].rearrange("p (c i t) -> p c t i", t=PACK, i=2),
-                    w4_raw[:, am].rearrange("p t (c i) -> p c t i", i=2),
-                )
-            return quantize("w4", w4_bf, 2 * N)
-
-        def stage3(j0, n, z_last):
-            z_parts = [chunk_part(z_q[j0 // CHUNK], j0, n), (z_last[0][:].bitcast(FP8X4), z_last[1][:])]
-            bank = psum.tile([P, 2, n], F32, name="bank", tag="bank")
+        for j0, n in pieces:
+            bank = psum.tile([P, N // P, n], F32, name="bank", tag="bank")
             for am in range(2):
-                for b in range(2):
+                z_codes, z_sc = columns(z_done[am], j0, n)
+                for b in range(N // P):
                     wcols = slice(am * N + b * P, am * N + (b + 1) * P)
                     nc.tensor.matmul_mx(
                         bank[:, b, :],
                         lhsT=w4_codes[:, wcols].bitcast(FP8X4),
                         lhsT_scale=w4_sc[:, wcols],
-                        rhs=z_parts[am][0],
-                        rhs_scale=z_parts[am][1],
+                        rhs=z_codes,
+                        rhs_scale=z_sc,
                         start=(am == 0 and b == 0),
-                        stop=(am == 1 and b == 1),
+                        stop=(am == 1 and b == N // P - 1),
                     )
-            res = work.tile([P, 2, n], F32, name="res", tag="res", bufs=5)
+            res = work.tile([P, N // P, n], F32, name="res", tag="res", bufs=len(pieces))
             if j0 + n == S:
-                nc.vector.tensor_tensor(res[:], bank[:], clim_sb[:].unsqueeze(2).to_broadcast([P, 2, n]), ADD)
+                nc.vector.tensor_tensor(res[:], bank[:], clim_sb[:].unsqueeze(2).to_broadcast([P, N // P, n]), ADD)
             else:
-                for b in range(2):
+                for b in range(N // P):
                     nc.scalar.activation(res[:, b, :], bank[:, b, :], ACT.Identity, bias=clim_sb[:, b : b + 1])
             nc.sync.dma_start(out[:, j0 : j0 + n].rearrange("(b p) j -> p b j", p=P), res[:])
-
-        pieces = [(c * CHUNK, CHUNK) for c in range(CHUNKS - 1)] + [(S - CHUNK, P), (S - P, P)]
-        z_last = []
-        for k, (j0, n) in enumerate(pieces):
-            if k == W4AT:
-                w4_codes, w4_sc = prepare_w4()
-            z_last.append(stage2(1, j0, n))
-        for (j0, n), z in zip(pieces, z_last):
-            stage3(j0, n, z)

@@ -44,86 +44,91 @@ def tile_list_cyclone_intensity_nowcast_kernel(
         offsets = keep.tile([P, S // GROUP], U16, name="offsets")
         nc.sync.dma_start(offsets[:], offs)
 
-        w1_raw = held("w1_raw", [P, 2, 2 * H], U8, "slot_w1")
+        w1_raw = held("w1_raw", [P, 2, 2 * H], U8)
         nc.sync.dma_start(words(w1_raw[:]), words(w1_words.rearrange("a p c -> p a c")))
 
-        scale_window = held("scale_window", [P, T], U8, "slot_scales")
-        nc.vector.memset(words(scale_window[:]), 0)
+        scale_window = held("scale_window", [P, T], U8)
+        nc.gpsimd.memset(words(scale_window[:]), 0)
         for odd in range(2):
             nc.sync.dma_start(words(scale_window[odd:P:GROUP, :]), words(tab_scales[0, odd:ROWS:2, :]))
         nc.sync.dma_start(words(scale_window[4:P:8, :]), words(tab_scales[1]))
 
-        zero_a = held("zero_a", [P, 1], F32, "slot_table0")
-        zero_b = held("zero_b", [P, 1], F32, "slot_w1_scales")
-        zero_in = held("zero_in", [P, 1], F32, "slot_w3_first")
-        zero_shift = held("zero_shift", [P, 1], F32, "slot_table1")
+        zero_in = held("zero_in", [P, 1], F32)
         zero_bias = held("zero_bias", [P, 1], F32)
-        nc.vector.memset(zero_a[:], 0.0)
-        nc.vector.memset(zero_b[:], 0.0)
-        nc.gpsimd.memset(zero_shift[:], 0.0)
-        nc.vector.tensor_tensor(zero_in[:], zero_a[:], zero_b[:], MULT)
-        nc.scalar.activation(zero_bias[:], zero_in[:], ACT.Silu, bias=zero_shift[:])
+        nc.vector.memset(zero_in[:], 0.0)
+        nc.scalar.activation(zero_bias[:], zero_in[:], ACT.Silu)
 
-        def load_table(a, slot):
+        def load_table(a, slot=None):
             window = held("table%d" % a, [P, T], I32, slot)
             nc.sync.dma_start(window[:], words(tab_words[a].rearrange("p t i -> p (t i)")))
             return window
 
-        def load_w3(a, m0, width, slot):
-            raw = held("w3_raw%d_%d" % (a, m0), [P, PACK, width], F32, slot)
+        def load_w3(a, m0, width, slot=None):
+            raw = held("w3_raw%d_%d" % (a, m0), [P, PACK, width], F32, slot)[:]
             rows = w3[a * PASS : (a + 1) * PASS, m0 : m0 + width]
-            nc.sync.dma_start(raw[:], rows.rearrange("(p t) m -> p t m", t=PACK))
+            nc.sync.dma_start(raw, rows.rearrange("(p t) m -> p t m", t=PACK))
             return raw
 
-        tables = [load_table(0, "slot_table0")]
+        tables = [load_table(0)]
 
-        w1s_raw = held("w1s_raw", [P, 2 * H], U8, "slot_w1_scales")
-        nc.vector.memset(words(w1s_raw[:]), 0)
+        w1s_raw = held("w1s_raw", [P, 2 * H], U8)
+        nc.gpsimd.memset(words(w1s_raw[:]), 0)
         for r in range(4):
             nc.sync.dma_start(
                 words(w1s_raw[r:P:32, :].rearrange("d (a c) -> d a c", a=2)),
                 words(w1_scales[:, r:ROWS:4, :].rearrange("a d c -> d a c")),
             )
 
-        w3_first = [load_w3(0, 0, HALF, "slot_w3_first")]
-        tables.append(load_table(1, "slot_table1"))
 
         v_scales = [held("v_scales%d" % a, [P, S], U8) for a in range(2)]
         nc.gpsimd.memset(words(v_scales[1][:]), 0)
+        w3_first = [load_w3(0, 0, HALF)]
+        tables.append(load_table(1, "slot_w2_sc"))
+        w2s_raw = held("w2s_raw", [P, M], U8)
+        nc.gpsimd.memset(words(w2s_raw[:]), 0)
 
         gain1_sb = held("gain1_sb", [P, PACK], F32)
-        gain2_raw = held("gain2_raw", [P, 2, 8], F32, "slot_w2")
+        gain2_raw = held("gain2_raw", [P, 2, 8], F32)
         clim_sb = held("clim_sb", [P, N // P], F32)
         nc.gpsimd.dma_start(gain1_sb[:], gain1.rearrange("(p t) -> p t", t=PACK))
-        for i in range(2):
-            nc.gpsimd.dma_start(
-                gain2_raw[i:P:2, :, 0:7], gain2.rearrange("(a c x) -> c a x", a=2, x=8)[:, :, i : i + 7]
-            )
-        with nc.allow_non_contiguous_dma(reason="one value a partition"):
-            nc.gpsimd.dma_start(clim_sb[:], clim.rearrange("(b p) -> p b", p=P))
-        gain2_sb = held("gain2_sb", [P, 2, PACK], F32)
-        nc.gpsimd.tensor_copy(gain2_sb[:], gain2_raw[:, :, 0:7:2])
-
-        picked_scales = held("picked_scales", [P, S], U8)
-        nc.vector.tensor_copy(picked_scales[:], scale_window[:].indirect(offsets[:]))
-        nc.vector.tensor_copy(words(v_scales[0][:]), words(picked_scales[:]))
         for r in range(4):
-            nc.sync.dma_start(words(v_scales[1][r:P:32, :]), words(picked_scales[8 * r + 4 : P : 32, :]))
-        for r in range(2, 4):
-            nc.sync.dma_start(words(v_scales[0][r:P:32, :]), words(picked_scales[GROUP + r - 2 : P : 32, :]))
-        w3_second = load_w3(1, 0, PASS, "slot_scales")
+            nc.gpsimd.dma_start(words(w2s_raw[r:P:32, :]), words(w2_scales[0, r:ROWS:4, :]))
 
         w1_codes = held("w1_codes", [P, 2, 2 * H], U8)
         nc.vector.tensor_copy(
             w1_codes[:].bitcast(U16).rearrange("p a (t c) -> p a t c", t=PACK),
             w1_raw[:].bitcast(U16).rearrange("p a (c t) -> p a t c", t=PACK),
         )
+
+        picked_scales = held("picked_scales", [P, S], U8)
+        nc.vector.tensor_copy(picked_scales[:], scale_window[:].indirect(offsets[:]))
         w1_sc = held("w1_sc", [P, 2, H], U8)
         nc.vector.tensor_copy(
             w1_sc[:].rearrange("p a (t c) -> p a t c", t=PACK),
             w1s_raw[:].rearrange("p (a c t) -> p a t c", a=2, t=PACK),
         )
-        w3_first.append(load_w3(0, HALF, HALF, "slot_w1_scales"))
+        nc.vector.tensor_copy(words(v_scales[0][:]), words(picked_scales[:]))
+        for r in range(4):
+            nc.sync.dma_start(words(v_scales[1][r:P:32, :]), words(picked_scales[8 * r + 4 : P : 32, :]))
+        for r in range(2, 4):
+            nc.sync.dma_start(words(v_scales[0][r:P:32, :]), words(picked_scales[GROUP + r - 2 : P : 32, :]))
+        w3_first.append(load_w3(0, HALF, HALF, "slot_tanh"))
+        w3_second = load_w3(1, 0, PASS, "slot_gain0")
+        w2_raw = held("w2_raw", [P, M], I32)
+        nc.sync.dma_start(w2_raw[:], words(w2_words[0].rearrange("p c i -> p (c i)")))
+        w3_late = [load_w3(0, PASS, PASS), load_w3(1, PASS, PASS)]
+        for i in range(2):
+            nc.sync.dma_start(
+                gain2_raw[i:P:2, :, 0:7], gain2.rearrange("(a c x) -> c a x", a=2, x=8)[:, :, i : i + 7]
+            )
+        w4_raw = held("w4_raw", [P, 2, PACK, N], F32)
+        for am in range(2):
+            rows = w4[am * PASS : (am + 1) * PASS, :].rearrange("(c t i) n -> i c t n", t=PACK, i=2)
+            for i in range(2):
+                nc.sync.dma_start(w4_raw[i:P:2, am, :, :], rows[i])
+        with nc.allow_non_contiguous_dma(reason="one value a partition"):
+            nc.sync.dma_start(clim_sb[:], clim.rearrange("(b p) -> p b", p=P))
+
 
         v_codes = [held("v_codes%d" % a, [P, S], U32) for a in range(2)]
 
@@ -133,22 +138,9 @@ def tile_list_cyclone_intensity_nowcast_kernel(
                 tables[a][:].bitcast(U32).indirect(offsets[:, j0 // GROUP : (j0 + n) // GROUP]),
             )
 
-        gather_words(0, 0, CHUNK)
-        gather_words(0, CHUNK, S - CHUNK)
+        gather_words(0, 0, S)
         for j0, n in ((0, CHUNK), (CHUNK, CHUNK), (2 * CHUNK, 2 * CHUNK)):
             gather_words(1, j0, n)
-
-        w2s_raw = held("w2s_raw", [P, M], U8, "slot_w1")
-        nc.gpsimd.memset(words(w2s_raw[:]), 0)
-        for r in range(4):
-            nc.sync.dma_start(words(w2s_raw[r:P:32, :]), words(w2_scales[0, r:ROWS:4, :]))
-        w2_raw = held("w2_raw", [P, M], I32, "slot_w2")
-        nc.sync.dma_start(w2_raw[:], words(w2_words[0].rearrange("p c i -> p (c i)")))
-        w2_codes = held("w2_codes", [P, M], I32)
-        nc.vector.tensor_copy(
-            w2_codes[:].rearrange("p (a t c i) -> p a t c i", a=2, t=PACK, i=2),
-            w2_raw[:].rearrange("p (a c t i) -> p a t c i", a=2, t=PACK, i=2),
-        )
 
         def quantize(name, grouped, width):
             codes = held(name + "_codes", [P, width], U32)
@@ -156,39 +148,38 @@ def tile_list_cyclone_intensity_nowcast_kernel(
             nc.vector.quantize_mx(codes[:].bitcast(FP8X4), scales[:], grouped[:])
             return codes, scales
 
-        def prepare_w3(name, parts):
-            grouped = work.tile([P, PASS * PACK], BF16, name="w_bf", tag="w_bf", align_bytes=64)
+        def staging(name, slot=None):
+            return held(name, [P, PASS * PACK], BF16, slot)
+
+        def cast_w3(grouped, m0, raw, cast):
             dst = grouped[:].rearrange("p (t c i x) -> p c t x i", t=PACK, i=2, x=PACK)
-            c0 = 0
-            for raw, cast in parts:
-                src = raw.rearrange("p x (c t i) -> p c t x i", t=PACK, i=2)
-                cast(dst[:, c0 : c0 + src.shape[1]], src)
-                c0 = c0 + src.shape[1]
-            return quantize(name, grouped, PASS)
+            src = raw.rearrange("p x (c t i) -> p c t x i", t=PACK, i=2)
+            cast(dst[:, m0 // 8 : m0 // 8 + src.shape[1]], src)
 
         def columns(done, j0, n):
             first = max(j for j in done if j <= j0)
             cols = slice(j0 - first, j0 - first + n)
             return done[first][0][:, cols].bitcast(FP8X4), done[first][1][:, cols]
 
-        def scale_and_quantize(name, done, runs):
-            total = sum(run[1] for run in runs)
-            grouped = work.tile([P, total * PACK], BF16, name="act16", tag="act16", align_bytes=64)
-            for j0, n, values, gains in runs:
-                c0 = (j0 - runs[0][0]) * PACK
-                dst = grouped[:, c0 : c0 + n * PACK].rearrange("p (j u e) -> p j u e", j=n, u=values.shape[2])
-                nc.vector.tensor_tensor(dst, values, gains.unsqueeze(1).to_broadcast(list(values.shape)), MULT)
-            done[runs[0][0]] = quantize("%s_%d" % (name, runs[0][0]), grouped, total)
+        def apply_gains(j0, n, values, gains, grouped=None):
+            if grouped is None:
+                grouped = work.tile([P, n * PACK], BF16, name="act16", tag="act16", align_bytes=64)
+            dst = grouped[:].rearrange("p (j u e) -> p j u e", j=n, u=values.shape[2])
+            nc.vector.tensor_tensor(dst, values, gains.unsqueeze(1).to_broadcast(list(values.shape)), MULT)
+            return j0, n, grouped
+
+        def quantize_run(name, done, j0, n, grouped):
+            done[j0] = quantize("%s_%d" % (name, j0), grouped, n)
 
         def activations(n):
             return work.tile([P, n * PACK], F32, name="act32", tag="act32", bufs=4)
 
-        def stage1(j0):
-            th = activations(CHUNK)
+        def stage1(j0, th=None):
+            th = activations(CHUNK) if th is None else th
             banks = [psum.tile([P, PACK, P], F32, name="bank", tag="bank") for half in range(CHUNK // P)]
-            for a in range(2):
-                for half, bank in enumerate(banks):
-                    cols = slice(j0 + half * P, j0 + (half + 1) * P)
+            for half, bank in enumerate(banks):
+                cols = slice(j0 + half * P, j0 + (half + 1) * P)
+                for a in range(2):
                     for t in range(PACK):
                         nc.tensor.matmul_mx(
                             bank[:, t, :],
@@ -207,27 +198,6 @@ def tile_list_cyclone_intensity_nowcast_kernel(
                     bias=zero_bias[:],
                 )
             return j0, CHUNK, th[:].rearrange("p (j u e) -> p j u e", u=1, e=PACK), gain1_sb[:].unsqueeze(1)
-
-        h_done, w3_done = {}, {}
-        scale_and_quantize("h", h_done, [stage1(0)])
-        w3_done[(0, 0)] = prepare_w3("w3_00", [(raw[:], nc.scalar.copy) for raw in w3_first])
-        w3_done[(1, 0)] = prepare_w3("w3_10", [(w3_second[:], nc.vector.tensor_copy)])
-        w3_late = [load_w3(0, PASS, PASS, "slot_table1"), load_w3(1, PASS, PASS, "slot_w1_scales")]
-        scale_and_quantize("h", h_done, [stage1(CHUNK)])
-
-        w2_sc = held("w2_sc", [P, M], U8)
-        nc.vector.tensor_copy(
-            w2_sc[:].bitcast(U16).rearrange("p (a t c) -> p a t c", a=2, t=PACK),
-            w2s_raw[:].bitcast(U16).rearrange("p (a c t) -> p a t c", a=2, t=PACK),
-        )
-        for j0 in (2 * CHUNK, 3 * CHUNK):
-            scale_and_quantize("h", h_done, [stage1(j0)])
-
-        w4_raw = held("w4_raw", [P, 2, PACK, N], F32, "slot_scales")
-        for am in range(2):
-            rows = w4[am * PASS : (am + 1) * PASS, :].rearrange("(c t i) n -> i c t n", t=PACK, i=2)
-            for i in range(2):
-                nc.sync.dma_start(w4_raw[i:P:2, am, :, :], rows[i])
 
         def stage2(am, j0, n):
             per_bank = PASS // n
@@ -262,29 +232,9 @@ def tile_list_cyclone_intensity_nowcast_kernel(
                     ACT.Silu,
                 )
             values = sl[:].rearrange("p (u j e) -> p j u e", u=banks, e=per_bank)
-            return j0, n, values, gain2_sb[:, am, :].rearrange("p (u e) -> p u e", u=banks)
+            return j0, n, values, gain2_raw[:, am, 0:8:2].rearrange("p (u e) -> p u e", u=banks)
 
-        z_done = [{}, {}]
-        for c in range(S // CHUNK):
-            scale_and_quantize("z0", z_done[0], [stage2(0, c * CHUNK, CHUNK)])
-            if c < len(w3_late):
-                w3_done[(c, 1)] = prepare_w3("w3_%d1" % c, [(w3_late[c][:], nc.scalar.copy)])
-
-        pieces = [(j0, CHUNK) for j0 in range(0, S - CHUNK, CHUNK)] + [(S - CHUNK, P), (S - P, P)]
-        scale_and_quantize("z1", z_done[1], [stage2(1, *pieces[0])])
-
-        w4_bf = work.tile([P, 2 * N * PACK], BF16, name="w_bf", tag="w_bf", align_bytes=64)
-        for am in range(2):
-            nc.scalar.copy(
-                w4_bf[:, am * N * PACK : (am + 1) * N * PACK].rearrange("p (c i t) -> p c t i", t=PACK, i=2),
-                w4_raw[:, am].rearrange("p t (c i) -> p c t i", i=2),
-            )
-        w4_codes, w4_sc = quantize("w4", w4_bf, 2 * N)
-
-        for j0, n in pieces[1:]:
-            scale_and_quantize("z1", z_done[1], [stage2(1, j0, n)])
-
-        for j0, n in pieces:
+        def stage3(j0, n):
             bank = psum.tile([P, N // P, n], F32, name="bank", tag="bank")
             for am in range(2):
                 z_codes, z_sc = columns(z_done[am], j0, n)
@@ -299,6 +249,77 @@ def tile_list_cyclone_intensity_nowcast_kernel(
                         start=(am == 0 and b == 0),
                         stop=(am == 1 and b == N // P - 1),
                     )
+            return j0, n, bank
+
+        def cast_w4(am, cast):
+            cast(
+                w4_bf[:, am * N * PACK : (am + 1) * N * PACK].rearrange("p (c i t) -> p c t i", t=PACK, i=2),
+                w4_raw[:, am].rearrange("p t (c i) -> p c t i", i=2),
+            )
+
+        h_done, w3_done, z_done = {}, {}, [{}, {}]
+        bf_first, bf_second = staging("bf_first"), staging("bf_second")
+        late_bf = [staging("bf_late0"), staging("bf_late1")]
+        w4_bf = staging("bf_w4")
+        cast_w3(bf_first, 0, w3_first[0], nc.scalar.copy)
+        cast_w3(bf_first, HALF, w3_first[1], nc.scalar.copy)
+        tanh_pair = held("tanh_pair", [P, 2, CHUNK * PACK], F32, "slot_tanh")
+        tanh = [stage1(0, tanh_pair[:, 0, :]), stage1(CHUNK, tanh_pair[:, 1, :]), stage1(2 * CHUNK), stage1(3 * CHUNK)]
+        cast_w3(late_bf[0], 0, w3_late[0], nc.scalar.copy)
+        w2_sc = held("w2_sc", [P, M], U8, "slot_w2_sc")
+        nc.vector.tensor_copy(
+            w2_sc[:].bitcast(U16).rearrange("p (a t c) -> p a t c", a=2, t=PACK),
+            w2s_raw[:].bitcast(U16).rearrange("p (a c t) -> p a t c", a=2, t=PACK),
+        )
+        w3_done[(0, 0)] = quantize("w3_00", bf_first, PASS)
+        cast_w3(bf_second, 0, w3_second, nc.vector.tensor_copy)
+        h_pair = held("h_pair", [P, 2, CHUNK * PACK], BF16, "slot_gain0")
+        h = [apply_gains(*tanh[0], h_pair[:, 0, :])]
+        w3_done[(1, 0)] = quantize("w3_10", bf_second, PASS)
+        w2_codes = held("w2_codes", [P, M], I32)
+        nc.vector.tensor_copy(
+            w2_codes[:].rearrange("p (a t c i) -> p a t c i", a=2, t=PACK, i=2),
+            w2_raw[:].rearrange("p (a c t i) -> p a t c i", a=2, t=PACK, i=2),
+        )
+        quantize_run("h", h_done, *h[0])
+        silu = [stage2(0, 0, CHUNK)]
+        h.append(apply_gains(*tanh[1], h_pair[:, 1, :]))
+        h.append(apply_gains(*tanh[2]))
+        quantize_run("h", h_done, *h[1])
+        silu.append(stage2(0, CHUNK, CHUNK))
+        cast_w3(late_bf[1], 0, w3_late[1], nc.scalar.copy)
+        h.append(apply_gains(*tanh[3]))
+        quantize_run("h", h_done, *h[2])
+        silu.append(stage2(0, 2 * CHUNK, CHUNK))
+        w3_done[(0, 1)] = quantize("w3_01", late_bf[0], PASS)
+        quantize_run("h", h_done, *h[3])
+        silu.append(stage2(0, 3 * CHUNK, CHUNK))
+        z = [apply_gains(*silu[0]), apply_gains(*silu[1])]
+        quantize_run("z0", z_done[0], *z[0])
+        quantize_run("z0", z_done[0], *z[1])
+        w3_done[(1, 1)] = quantize("w3_11", late_bf[1], PASS)
+
+        pieces = [(j0, CHUNK) for j0 in range(0, S - CHUNK, CHUNK)] + [(S - CHUNK, P), (S - P, P)]
+        late = [stage2(1, *pieces[0])]
+        cast_w4(0, nc.scalar.copy)
+        cast_w4(1, nc.scalar.copy)
+        late.append(stage2(1, *pieces[1]))
+        late.append(stage2(1, *pieces[2]))
+        z.extend([apply_gains(*silu[2]), apply_gains(*silu[3])])
+        quantize_run("z0", z_done[0], *z[2])
+        quantize_run("z0", z_done[0], *z[3])
+        late.append(stage2(1, *pieces[3]))
+        late.append(stage2(1, *pieces[4]))
+        scaled = apply_gains(*late[0])
+        w4_codes, w4_sc = quantize("w4", w4_bf, 2 * N)
+        sums = []
+        for k in range(len(pieces)):
+            ahead = apply_gains(*late[k + 1]) if k + 1 < len(pieces) else None
+            quantize_run("z1", z_done[1], *scaled)
+            sums.append(stage3(*pieces[k]))
+            scaled = ahead
+
+        for j0, n, bank in sums:
             res = work.tile([P, N // P, n], F32, name="res", tag="res", bufs=len(pieces))
             if j0 + n == S:
                 nc.vector.tensor_tensor(res[:], bank[:], clim_sb[:].unsqueeze(2).to_broadcast([P, N // P, n]), ADD)

@@ -44,14 +44,14 @@ def tile_list_cyclone_intensity_nowcast_kernel(
         offsets = keep.tile([P, S // GROUP], U16, name="offsets")
         nc.sync.dma_start(offsets[:], offs)
 
+        gain1_sb = held("gain1_sb", [P, PACK], F32)
+        nc.scalar.dma_start(gain1_sb[:], gain1.rearrange("(p t) -> p t", t=PACK))
         w1_raw = held("w1_raw", [P, 2, 2 * H], U8)
         nc.sync.dma_start(words(w1_raw[:]), words(w1_words.rearrange("a p c -> p a c")))
 
         scale_window = held("scale_window", [P, T], U8)
         nc.gpsimd.memset(words(scale_window[:]), 0)
-        for odd in range(2):
-            nc.sync.dma_start(words(scale_window[odd:P:GROUP, :]), words(tab_scales[0, odd:ROWS:2, :]))
-        nc.sync.dma_start(words(scale_window[4:P:8, :]), words(tab_scales[1]))
+        nc.sync.dma_start(words(scale_window[0:P:4, :]), words(tab_scales.rearrange("a q c -> q a c")))
 
         zero_in = held("zero_in", [P, 1], F32)
         zero_bias = held("zero_bias", [P, 1], F32)
@@ -80,17 +80,16 @@ def tile_list_cyclone_intensity_nowcast_kernel(
             )
 
 
-        v_scales = [held("v_scales%d" % a, [P, S], U8) for a in range(2)]
-        nc.gpsimd.memset(words(v_scales[1][:]), 0)
+        v_both = held("v_both", [P, 2 * S], U8)
+        nc.gpsimd.memset(words(v_both[:]), 0)
+        v_scales = [v_both[:, a * S : (a + 1) * S] for a in range(2)]
         w3_first = [load_w3(0, 0, HALF)]
-        tables.append(load_table(1, "slot_w2_sc"))
+        tables.append(load_table(1))
         w2s_raw = held("w2s_raw", [P, M], U8)
         nc.gpsimd.memset(words(w2s_raw[:]), 0)
 
-        gain1_sb = held("gain1_sb", [P, PACK], F32)
         gain2_raw = held("gain2_raw", [P, 2, 8], F32)
         clim_sb = held("clim_sb", [P, N // P], F32)
-        nc.gpsimd.dma_start(gain1_sb[:], gain1.rearrange("(p t) -> p t", t=PACK))
         for r in range(4):
             nc.gpsimd.dma_start(words(w2s_raw[r:P:32, :]), words(w2_scales[0, r:ROWS:4, :]))
 
@@ -107,14 +106,11 @@ def tile_list_cyclone_intensity_nowcast_kernel(
             w1_sc[:].rearrange("p a (t c) -> p a t c", t=PACK),
             w1s_raw[:].rearrange("p (a c t) -> p a t c", a=2, t=PACK),
         )
-        nc.vector.tensor_copy(words(v_scales[0][:]), words(picked_scales[:]))
-        for r in range(4):
-            nc.sync.dma_start(words(v_scales[1][r:P:32, :]), words(picked_scales[8 * r + 4 : P : 32, :]))
-        for r in range(2, 4):
-            nc.sync.dma_start(words(v_scales[0][r:P:32, :]), words(picked_scales[GROUP + r - 2 : P : 32, :]))
+        for d in range(4):
+            nc.sync.dma_start(words(v_both[32 * d : 32 * d + 4, :]), words(picked_scales[32 * d : 32 * d + 32 : 4, :]))
         w3_first.append(load_w3(0, HALF, HALF, "slot_tanh"))
         w3_second = load_w3(1, 0, PASS, "slot_gain0")
-        w2_raw = held("w2_raw", [P, M], I32)
+        w2_raw = held("w2_raw", [P, M], I32, "slot_w2_sc")
         nc.sync.dma_start(w2_raw[:], words(w2_words[0].rearrange("p c i -> p (c i)")))
         w3_late = [load_w3(0, PASS, PASS), load_w3(1, PASS, PASS)]
         for i in range(2):
@@ -266,11 +262,6 @@ def tile_list_cyclone_intensity_nowcast_kernel(
         tanh_pair = held("tanh_pair", [P, 2, CHUNK * PACK], F32, "slot_tanh")
         tanh = [stage1(0, tanh_pair[:, 0, :]), stage1(CHUNK, tanh_pair[:, 1, :]), stage1(2 * CHUNK), stage1(3 * CHUNK)]
         cast_w3(late_bf[0], 0, w3_late[0], nc.scalar.copy)
-        w2_sc = held("w2_sc", [P, M], U8, "slot_w2_sc")
-        nc.vector.tensor_copy(
-            w2_sc[:].bitcast(U16).rearrange("p (a t c) -> p a t c", a=2, t=PACK),
-            w2s_raw[:].bitcast(U16).rearrange("p (a c t) -> p a t c", a=2, t=PACK),
-        )
         w3_done[(0, 0)] = quantize("w3_00", bf_first, PASS)
         cast_w3(bf_second, 0, w3_second, nc.vector.tensor_copy)
         h_pair = held("h_pair", [P, 2, CHUNK * PACK], BF16, "slot_gain0")
@@ -280,6 +271,11 @@ def tile_list_cyclone_intensity_nowcast_kernel(
         nc.vector.tensor_copy(
             w2_codes[:].rearrange("p (a t c i) -> p a t c i", a=2, t=PACK, i=2),
             w2_raw[:].rearrange("p (a c t i) -> p a t c i", a=2, t=PACK, i=2),
+        )
+        w2_sc = held("w2_sc", [P, M], U8, "slot_w2_sc")
+        nc.vector.tensor_copy(
+            w2_sc[:].bitcast(U16).rearrange("p (a t c) -> p a t c", a=2, t=PACK),
+            w2s_raw[:].bitcast(U16).rearrange("p (a c t) -> p a t c", a=2, t=PACK),
         )
         quantize_run("h", h_done, *h[0])
         silu = [stage2(0, 0, CHUNK)]

@@ -44,13 +44,18 @@ def tile_list_cyclone_intensity_nowcast_kernel(
         offsets = keep.tile([P, S // GROUP], U16, name="offsets")
         nc.sync.dma_start(offsets[:], offs)
 
+        w2s_raw = held("w2s_raw", [P, M], U8)
+        nc.gpsimd.memset(words(w2s_raw[:]), 0)
+        for r in range(4):
+            nc.gpsimd.dma_start(words(w2s_raw[r:P:32, :]), words(w2_scales[0, r:ROWS:4, :]))
+
         gain1_sb = held("gain1_sb", [P, PACK], F32)
         nc.scalar.dma_start(gain1_sb[:], gain1.rearrange("(p t) -> p t", t=PACK))
         w1_raw = held("w1_raw", [P, 2, 2 * H], U8)
         nc.sync.dma_start(words(w1_raw[:]), words(w1_words.rearrange("a p c -> p a c")))
 
         scale_window = held("scale_window", [P, T], U8)
-        nc.gpsimd.memset(words(scale_window[:]), 0)
+        nc.vector.memset(words(scale_window[:]), 0)
         nc.sync.dma_start(words(scale_window[0:P:4, :]), words(tab_scales.rearrange("a q c -> q a c")))
 
         zero_in = held("zero_in", [P, 1], F32)
@@ -72,7 +77,7 @@ def tile_list_cyclone_intensity_nowcast_kernel(
         tables = [load_table(0)]
 
         w1s_raw = held("w1s_raw", [P, 2 * H], U8)
-        nc.gpsimd.memset(words(w1s_raw[:]), 0)
+        nc.vector.memset(words(w1s_raw[:]), 0)
         for r in range(4):
             nc.sync.dma_start(
                 words(w1s_raw[r:P:32, :].rearrange("d (a c) -> d a c", a=2)),
@@ -81,17 +86,13 @@ def tile_list_cyclone_intensity_nowcast_kernel(
 
 
         v_both = held("v_both", [P, 2 * S], U8)
-        nc.gpsimd.memset(words(v_both[:]), 0)
+        nc.vector.memset(words(v_both[:]), 0)
         v_scales = [v_both[:, a * S : (a + 1) * S] for a in range(2)]
         w3_first = [load_w3(0, 0, HALF)]
         tables.append(load_table(1))
-        w2s_raw = held("w2s_raw", [P, M], U8)
-        nc.gpsimd.memset(words(w2s_raw[:]), 0)
 
         gain2_raw = held("gain2_raw", [P, 2, 8], F32)
         clim_sb = held("clim_sb", [P, N // P], F32)
-        for r in range(4):
-            nc.gpsimd.dma_start(words(w2s_raw[r:P:32, :]), words(w2_scales[0, r:ROWS:4, :]))
 
         w1_codes = held("w1_codes", [P, 2, 2 * H], U8)
         nc.vector.tensor_copy(
@@ -109,9 +110,9 @@ def tile_list_cyclone_intensity_nowcast_kernel(
         for d in range(4):
             nc.sync.dma_start(words(v_both[32 * d : 32 * d + 4, :]), words(picked_scales[32 * d : 32 * d + 32 : 4, :]))
         w3_first.append(load_w3(0, HALF, HALF, "slot_tanh"))
-        w3_second = load_w3(1, 0, PASS, "slot_gain0")
         w2_raw = held("w2_raw", [P, M], I32, "slot_w2_sc")
         nc.sync.dma_start(w2_raw[:], words(w2_words[0].rearrange("p c i -> p (c i)")))
+        w3_second = load_w3(1, 0, PASS, "slot_gain0")
         w3_late = [load_w3(0, PASS, PASS), load_w3(1, PASS, PASS)]
         for i in range(2):
             nc.sync.dma_start(
@@ -151,6 +152,11 @@ def tile_list_cyclone_intensity_nowcast_kernel(
             dst = grouped[:].rearrange("p (t c i x) -> p c t x i", t=PACK, i=2, x=PACK)
             src = raw.rearrange("p x (c t i) -> p c t x i", t=PACK, i=2)
             cast(dst[:, m0 // 8 : m0 // 8 + src.shape[1]], src)
+
+        def cast_w3_half(grouped, t0, raw, cast):
+            dst = grouped[:].rearrange("p (t c i x) -> p c t x i", t=PACK, i=2, x=PACK)
+            src = raw.rearrange("p x (c t i) -> p c t x i", t=PACK, i=2)
+            cast(dst[:, :, t0 : t0 + 2], src[:, :, t0 : t0 + 2])
 
         def columns(done, j0, n):
             first = max(j for j in done if j <= j0)
@@ -203,7 +209,7 @@ def tile_list_cyclone_intensity_nowcast_kernel(
             h_codes, h_sc = columns(h_done, j0, n)
             for u in range(banks):
                 bank = psum.tile([P, per_bank, n], F32, name="bank", tag="bank")
-                for step in range(3):
+                for place, step in enumerate((0, 2, 1)):
                     for e in range(per_bank):
                         wcols = slice(P * (per_bank * u + e), P * (per_bank * u + e + 1))
                         if step < 2:
@@ -219,8 +225,8 @@ def tile_list_cyclone_intensity_nowcast_kernel(
                             lhsT_scale=w_sc,
                             rhs=x_codes,
                             rhs_scale=x_sc,
-                            start=(step == 0 and e == 0),
-                            stop=(step == 2 and e == per_bank - 1),
+                            start=(place == 0 and e == 0),
+                            stop=(place == 2 and e == per_bank - 1),
                         )
                 nc.scalar.activation(
                     sl[:, u * PASS : (u + 1) * PASS].rearrange("p (j e) -> p j e", e=per_bank),
@@ -262,54 +268,55 @@ def tile_list_cyclone_intensity_nowcast_kernel(
         tanh_pair = held("tanh_pair", [P, 2, CHUNK * PACK], F32, "slot_tanh")
         tanh = [stage1(0, tanh_pair[:, 0, :]), stage1(CHUNK, tanh_pair[:, 1, :]), stage1(2 * CHUNK), stage1(3 * CHUNK)]
         cast_w3(late_bf[0], 0, w3_late[0], nc.scalar.copy)
-        w3_done[(0, 0)] = quantize("w3_00", bf_first, PASS)
-        cast_w3(bf_second, 0, w3_second, nc.vector.tensor_copy)
-        h_pair = held("h_pair", [P, 2, CHUNK * PACK], BF16, "slot_gain0")
-        h = [apply_gains(*tanh[0], h_pair[:, 0, :])]
-        w3_done[(1, 0)] = quantize("w3_10", bf_second, PASS)
         w2_codes = held("w2_codes", [P, M], I32)
         nc.vector.tensor_copy(
             w2_codes[:].rearrange("p (a t c i) -> p a t c i", a=2, t=PACK, i=2),
             w2_raw[:].rearrange("p (a c t i) -> p a t c i", a=2, t=PACK, i=2),
         )
+        w3_done[(0, 0)] = quantize("w3_00", bf_first, PASS)
         w2_sc = held("w2_sc", [P, M], U8, "slot_w2_sc")
         nc.vector.tensor_copy(
             w2_sc[:].bitcast(U16).rearrange("p (a t c) -> p a t c", a=2, t=PACK),
             w2s_raw[:].bitcast(U16).rearrange("p (a c t) -> p a t c", a=2, t=PACK),
         )
+        h = [apply_gains(*tanh[0])]
+        cast_w3(bf_second, 0, w3_second, nc.vector.tensor_copy)
         quantize_run("h", h_done, *h[0])
+        h_pair = held("h_pair", [P, 2, CHUNK * PACK], BF16, "slot_gain0")
+        h.append(apply_gains(*tanh[1], h_pair[:, 0, :]))
+        w3_done[(1, 0)] = quantize("w3_10", bf_second, PASS)
         silu = [stage2(0, 0, CHUNK)]
-        h.append(apply_gains(*tanh[1], h_pair[:, 1, :]))
-        h.append(apply_gains(*tanh[2]))
+        cast_w3(late_bf[1], 0, w3_late[1], nc.scalar.copy)
+        h.append(apply_gains(*tanh[2], h_pair[:, 1, :]))
         quantize_run("h", h_done, *h[1])
         silu.append(stage2(0, CHUNK, CHUNK))
-        cast_w3(late_bf[1], 0, w3_late[1], nc.scalar.copy)
         h.append(apply_gains(*tanh[3]))
         quantize_run("h", h_done, *h[2])
         silu.append(stage2(0, 2 * CHUNK, CHUNK))
         w3_done[(0, 1)] = quantize("w3_01", late_bf[0], PASS)
         quantize_run("h", h_done, *h[3])
         silu.append(stage2(0, 3 * CHUNK, CHUNK))
-        z = [apply_gains(*silu[0]), apply_gains(*silu[1])]
+        z = [apply_gains(*silu[0])]
         quantize_run("z0", z_done[0], *z[0])
-        quantize_run("z0", z_done[0], *z[1])
         w3_done[(1, 1)] = quantize("w3_11", late_bf[1], PASS)
-
         pieces = [(j0, CHUNK) for j0 in range(0, S - CHUNK, CHUNK)] + [(S - CHUNK, P), (S - P, P)]
         late = [stage2(1, *pieces[0])]
         cast_w4(0, nc.scalar.copy)
-        cast_w4(1, nc.scalar.copy)
         late.append(stage2(1, *pieces[1]))
-        late.append(stage2(1, *pieces[2]))
-        z.extend([apply_gains(*silu[2]), apply_gains(*silu[3])])
+        cast_w4(1, nc.scalar.copy)
+        late.extend([stage2(1, *piece) for piece in pieces[2:]])
+        z.extend([apply_gains(*silu[1]), apply_gains(*silu[2])])
+        quantize_run("z0", z_done[0], *z[1])
+        z.append(apply_gains(*silu[3]))
         quantize_run("z0", z_done[0], *z[2])
-        quantize_run("z0", z_done[0], *z[3])
-        late.append(stage2(1, *pieces[3]))
-        late.append(stage2(1, *pieces[4]))
         scaled = apply_gains(*late[0])
+        quantize_run("z0", z_done[0], *z[3])
+        ahead = apply_gains(*late[1])
+        quantize_run("z1", z_done[1], *scaled)
         w4_codes, w4_sc = quantize("w4", w4_bf, 2 * N)
-        sums = []
-        for k in range(len(pieces)):
+        sums = [stage3(*pieces[0])]
+        scaled = ahead
+        for k in range(1, len(pieces)):
             ahead = apply_gains(*late[k + 1]) if k + 1 < len(pieces) else None
             quantize_run("z1", z_done[1], *scaled)
             sums.append(stage3(*pieces[k]))

@@ -1,6 +1,7 @@
 from contextlib import ExitStack
 
 import concourse.mybir as mybir
+from concourse.masks import make_identity
 
 K, T, S, H, M, N = 1024, 2048, 1024, 512, 1024, 256
 FLOPS = 2 * S * (K * H + H * M + K * M + M * N)
@@ -24,6 +25,7 @@ ROWS = PASS // 32
 GROUP = 16
 CHUNK = 256
 HALF = PASS // 2
+ACT_BUFS = 6
 
 
 def tile_list_cyclone_intensity_nowcast_kernel(
@@ -33,7 +35,8 @@ def tile_list_cyclone_intensity_nowcast_kernel(
     with ExitStack() as ctx:
         keep = ctx.enter_context(tc.tile_pool(name="keep", bufs=1))
         work = ctx.enter_context(tc.tile_pool(name="work", bufs=3))
-        psum = ctx.enter_context(tc.psum_pool(name="psum", bufs=8))
+        psum = ctx.enter_context(tc.psum_pool(name="psum", bufs=7))
+        gain_pool = ctx.enter_context(tc.psum_pool(name="gain_pool", bufs=1))
 
         def held(name, shape, dtype, slot=None):
             return keep.tile(shape, dtype, name=name, tag=slot or name, align_bytes=64)
@@ -44,6 +47,8 @@ def tile_list_cyclone_intensity_nowcast_kernel(
         offsets = keep.tile([P, S // GROUP], U16, name="offsets")
         nc.sync.dma_start(offsets[:], offs)
 
+        identity = held("identity", [P, P], F32)
+        make_identity(nc, identity[:])
         w2s_raw = held("w2s_raw", [P, M], U8)
         nc.gpsimd.memset(words(w2s_raw[:]), 0)
         for r in range(4):
@@ -51,6 +56,11 @@ def tile_list_cyclone_intensity_nowcast_kernel(
 
         gain1_sb = held("gain1_sb", [P, PACK], F32)
         nc.scalar.dma_start(gain1_sb[:], gain1.rearrange("(p t) -> p t", t=PACK))
+        gain2_raw = held("gain2_raw", [P, 2, 8], F32)
+        for i in range(2):
+            nc.scalar.dma_start(
+                gain2_raw[i:P:2, :, 0:7], gain2.rearrange("(a c x) -> c a x", a=2, x=8)[:, :, i : i + 7]
+            )
         w1_raw = held("w1_raw", [P, 2, 2 * H], U8)
         nc.sync.dma_start(words(w1_raw[:]), words(w1_words.rearrange("a p c -> p a c")))
 
@@ -75,6 +85,8 @@ def tile_list_cyclone_intensity_nowcast_kernel(
             return raw
 
         tables = [load_table(0)]
+        gains_sb = held("gains_sb", [P, P], F32)
+        nc.vector.memset(gains_sb[:], 0.0)
 
         w1s_raw = held("w1s_raw", [P, 2 * H], U8)
         nc.vector.memset(words(w1s_raw[:]), 0)
@@ -91,7 +103,6 @@ def tile_list_cyclone_intensity_nowcast_kernel(
         w3_first = [load_w3(0, 0, HALF)]
         tables.append(load_table(1))
 
-        gain2_raw = held("gain2_raw", [P, 2, 8], F32)
         clim_sb = held("clim_sb", [P, N // P], F32)
 
         w1_codes = held("w1_codes", [P, 2, 2 * H], U8)
@@ -113,11 +124,7 @@ def tile_list_cyclone_intensity_nowcast_kernel(
         w2_raw = held("w2_raw", [P, M], I32, "slot_w2_sc")
         nc.sync.dma_start(w2_raw[:], words(w2_words[0].rearrange("p c i -> p (c i)")))
         w3_second = load_w3(1, 0, PASS, "slot_gain0")
-        w3_late = [load_w3(0, PASS, PASS), load_w3(1, PASS, PASS)]
-        for i in range(2):
-            nc.sync.dma_start(
-                gain2_raw[i:P:2, :, 0:7], gain2.rearrange("(a c x) -> c a x", a=2, x=8)[:, :, i : i + 7]
-            )
+        w3_late = [load_w3(0, PASS, PASS), load_w3(1, PASS, PASS, "slot_shared")]
         w4_raw = held("w4_raw", [P, 2, PACK, N], F32)
         for am in range(2):
             rows = w4[am * PASS : (am + 1) * PASS, :].rearrange("(c t i) n -> i c t n", t=PACK, i=2)
@@ -163,18 +170,30 @@ def tile_list_cyclone_intensity_nowcast_kernel(
             cols = slice(j0 - first, j0 - first + n)
             return done[first][0][:, cols].bitcast(FP8X4), done[first][1][:, cols]
 
-        def apply_gains(j0, n, values, gains, grouped=None):
-            if grouped is None:
-                grouped = work.tile([P, n * PACK], BF16, name="act16", tag="act16", align_bytes=64)
-            dst = grouped[:].rearrange("p (j u e) -> p j u e", j=n, u=values.shape[2])
-            nc.vector.tensor_tensor(dst, values, gains.unsqueeze(1).to_broadcast(list(values.shape)), MULT)
-            return j0, n, grouped
+        def apply_gains(engine, gains, values, first, grouped):
+            n, u, e = values.shape[1:]
+            gains = gains[:, first : first + PACK].rearrange("p (u e) -> p u e", u=u)
+            dst = grouped.rearrange("p (j u e) -> p j u e", j=n, u=u)
+            engine.tensor_tensor(dst, values, gains.unsqueeze(1).to_broadcast([P, n, u, e]), MULT)
 
-        def quantize_run(name, done, j0, n, grouped):
-            done[j0] = quantize("%s_%d" % (name, j0), grouped, n)
+        def gain(values, first, grouped=None):
+            n = values.shape[1]
+            if grouped is None:
+                grouped = work.tile([P, n * PACK], BF16, name="act16", tag="act16", align_bytes=64)[:]
+            apply_gains(nc.vector, gains_ps, values, first, grouped)
+            return grouped
+
+        def shared_tile():
+            return held("shared", [P, CHUNK * PACK], BF16, "bf_second")[:]
+
+        def pool_gain(values, first, grouped):
+            apply_gains(nc.gpsimd, gains_sb, values, first, grouped)
+
+        def quantize_run(name, done, j0, grouped):
+            done[j0] = quantize("%s_%d" % (name, j0), grouped, grouped.shape[1] // PACK)
 
         def activations(n):
-            return work.tile([P, n * PACK], F32, name="act32", tag="act32", bufs=4)
+            return work.tile([P, n * PACK], F32, name="act32", tag="act32", bufs=ACT_BUFS)
 
         def stage1(j0, th=None):
             th = activations(CHUNK) if th is None else th
@@ -199,12 +218,12 @@ def tile_list_cyclone_intensity_nowcast_kernel(
                     ACT.Tanh,
                     bias=zero_bias[:],
                 )
-            return j0, CHUNK, th[:].rearrange("p (j u e) -> p j u e", u=1, e=PACK), gain1_sb[:].unsqueeze(1)
+            return th[:].rearrange("p (j u e) -> p j u e", u=1, e=PACK)
 
-        def stage2(am, j0, n):
+        def stage2(am, j0, n, sl=None):
             per_bank = PASS // n
             banks = PACK // per_bank
-            sl = activations(n)
+            sl = activations(n) if sl is None else sl
             cols = slice(j0, j0 + n)
             h_codes, h_sc = columns(h_done, j0, n)
             for u in range(banks):
@@ -233,8 +252,7 @@ def tile_list_cyclone_intensity_nowcast_kernel(
                     bank[:].rearrange("p e j -> p j e"),
                     ACT.Silu,
                 )
-            values = sl[:].rearrange("p (u j e) -> p j u e", u=banks, e=per_bank)
-            return j0, n, values, gain2_raw[:, am, 0:8:2].rearrange("p (u e) -> p u e", u=banks)
+            return sl[:].rearrange("p (u j e) -> p j u e", u=banks, e=per_bank)
 
         def stage3(j0, n):
             bank = psum.tile([P, N // P, n], F32, name="bank", tag="bank")
@@ -263,6 +281,16 @@ def tile_list_cyclone_intensity_nowcast_kernel(
         bf_first, bf_second = staging("bf_first"), staging("bf_second")
         late_bf = [staging("bf_late0"), staging("bf_late1")]
         w4_bf = staging("bf_w4")
+
+        nc.scalar.copy(gains_sb[:, 0:PACK], gain1_sb[:])
+        nc.scalar.copy(gains_sb[:, PACK : 3 * PACK].rearrange("p (a t) -> p a t", a=2), gain2_raw[:, :, 0:8:2])
+        gain_bank = gain_pool.tile([P, 2, P], F32, name="gain_bank")
+        nc.tensor.transpose(gain_bank[:, 1, :], gains_sb[:], identity[:])
+        gains_turned = held("gains_turned", [P, P], F32)
+        nc.scalar.copy(gains_turned[:], gain_bank[:, 1, :])
+        nc.tensor.transpose(gain_bank[:, 0, :], gains_turned[:], identity[:])
+        gains_ps = gain_bank[:, 0, :]
+
         cast_w3(bf_first, 0, w3_first[0], nc.scalar.copy)
         cast_w3(bf_first, HALF, w3_first[1], nc.scalar.copy)
         tanh_pair = held("tanh_pair", [P, 2, CHUNK * PACK], F32, "slot_tanh")
@@ -279,52 +307,71 @@ def tile_list_cyclone_intensity_nowcast_kernel(
             w2_sc[:].bitcast(U16).rearrange("p (a t c) -> p a t c", a=2, t=PACK),
             w2s_raw[:].bitcast(U16).rearrange("p (a c t) -> p a t c", a=2, t=PACK),
         )
-        h = [apply_gains(*tanh[0])]
+        h0 = gain(tanh[0], 0)
         cast_w3(bf_second, 0, w3_second, nc.vector.tensor_copy)
-        quantize_run("h", h_done, *h[0])
-        h_pair = held("h_pair", [P, 2, CHUNK * PACK], BF16, "slot_gain0")
-        h.append(apply_gains(*tanh[1], h_pair[:, 0, :]))
+        quantize_run("h", h_done, 0, h0)
         w3_done[(1, 0)] = quantize("w3_10", bf_second, PASS)
-        silu = [stage2(0, 0, CHUNK)]
-        cast_w3(late_bf[1], 0, w3_late[1], nc.scalar.copy)
-        h.append(apply_gains(*tanh[2], h_pair[:, 1, :]))
-        quantize_run("h", h_done, *h[1])
-        silu.append(stage2(0, CHUNK, CHUNK))
-        h.append(apply_gains(*tanh[3]))
-        quantize_run("h", h_done, *h[2])
-        silu.append(stage2(0, 2 * CHUNK, CHUNK))
+        silu0 = stage2(0, 0, CHUNK)
+
+        def window(own_values, own_first, pool_values, rest_values, first, own=None, slot="bf_second"):
+            shared = held("shared", [P, CHUNK * PACK], BF16, slot)[:]
+            pool_gain(pool_values, first, shared[:, 0:PASS])
+            own = gain(own_values, own_first, own)
+            gain(rest_values, first, shared[:, PASS : 2 * PASS])
+            return own, shared
+
+        h1_tile = held("h1_tile", [P, CHUNK * PACK], BF16, "slot_gain0")[:]
+        own, shared = window(tanh[1], 0, tanh[2][:, 0:P], tanh[2][:, P:CHUNK], 0, h1_tile)
+        quantize_run("h", h_done, CHUNK, own)
+        silu1 = [stage2(0, CHUNK, P), stage2(0, CHUNK + P, P)]
+        quantize_run("h", h_done, 2 * CHUNK, shared)
+        silu2 = [stage2(0, 2 * CHUNK, P), stage2(0, 2 * CHUNK + P, P)]
+        h3 = gain(tanh[3], 0)
         w3_done[(0, 1)] = quantize("w3_01", late_bf[0], PASS)
-        quantize_run("h", h_done, *h[3])
-        silu.append(stage2(0, 3 * CHUNK, CHUNK))
-        z = [apply_gains(*silu[0])]
-        quantize_run("z0", z_done[0], *z[0])
+        quantize_run("h", h_done, 3 * CHUNK, h3)
+        silu3 = stage2(0, 3 * CHUNK, CHUNK)
+        cast_w3(late_bf[1], 0, w3_late[1], nc.vector.tensor_copy)
+        own, shared = window(silu0, PACK, silu1[0], silu1[1], PACK, None, "slot_shared")
         w3_done[(1, 1)] = quantize("w3_11", late_bf[1], PASS)
-        pieces = [(j0, CHUNK) for j0 in range(0, S - CHUNK, CHUNK)] + [(S - CHUNK, P), (S - P, P)]
-        late = [stage2(1, *pieces[0])]
+        quantize_run("z0", z_done[0], 0, own)
+        quantize_run("z0", z_done[0], CHUNK, shared)
+        own, shared = window(silu3, PACK, silu2[0], silu2[1], PACK, None, "slot_shared")
         cast_w4(0, nc.scalar.copy)
-        late.append(stage2(1, *pieces[1]))
         cast_w4(1, nc.scalar.copy)
-        late.extend([stage2(1, *piece) for piece in pieces[2:]])
-        z.extend([apply_gains(*silu[1]), apply_gains(*silu[2])])
-        quantize_run("z0", z_done[0], *z[1])
-        z.append(apply_gains(*silu[3]))
-        quantize_run("z0", z_done[0], *z[2])
-        scaled = apply_gains(*late[0])
-        quantize_run("z0", z_done[0], *z[3])
-        ahead = apply_gains(*late[1])
-        quantize_run("z1", z_done[1], *scaled)
+        late_four = held("late_four", [P, PACK, PASS], F32, "w4_raw")
+        late = [stage2(1, k * P, P, late_four[:, k, :]) for k in range(4)]
+        late.extend([stage2(1, k * P, P) for k in range(4, 8)])
+        quantize_run("z0", z_done[0], 3 * CHUNK, own)
         w4_codes, w4_sc = quantize("w4", w4_bf, 2 * N)
-        sums = [stage3(*pieces[0])]
-        scaled = ahead
-        for k in range(1, len(pieces)):
-            ahead = apply_gains(*late[k + 1]) if k + 1 < len(pieces) else None
-            quantize_run("z1", z_done[1], *scaled)
-            sums.append(stage3(*pieces[k]))
-            scaled = ahead
+        quantize_run("z0", z_done[0], 2 * CHUNK, shared)
+
+        def pair_tile():
+            return work.tile([P, CHUNK * PACK], BF16, name="act16", tag="act16", align_bytes=64)[:]
+
+        shared = held("shared", [P, CHUNK * PACK], BF16, "slot_shared")[:]
+        pool_gain(late[0], 2 * PACK, shared[:, 0:PASS])
+        gain(late[1], 2 * PACK, shared[:, PASS : 2 * PASS])
+        own = pair_tile()
+        gain(late[2], 2 * PACK, own[:, 0:PASS])
+        gain(late[3], 2 * PACK, own[:, PASS : 2 * PASS])
+        quantize_run("z1", z_done[1], 0, shared)
+        quantize_run("z1", z_done[1], CHUNK, own)
+        sums = [stage3(0, CHUNK), stage3(CHUNK, CHUNK)]
+        shared = held("shared", [P, CHUNK * PACK], BF16, "slot_shared")[:]
+        pool_gain(late[4], 2 * PACK, shared[:, 0:PASS])
+        gain(late[5], 2 * PACK, shared[:, PASS : 2 * PASS])
+        third = gain(late[6], 2 * PACK)
+        last = gain(late[7], 2 * PACK)
+        quantize_run("z1", z_done[1], 2 * CHUNK, shared)
+        sums.append(stage3(2 * CHUNK, CHUNK))
+        quantize_run("z1", z_done[1], 3 * CHUNK, third)
+        sums.append(stage3(3 * CHUNK, P))
+        quantize_run("z1", z_done[1], 3 * CHUNK + P, last)
+        sums.append(stage3(3 * CHUNK + P, P))
 
         for j0, n, bank in sums:
-            res = work.tile([P, N // P, n], F32, name="res", tag="res", bufs=len(pieces))
-            if j0 + n == S:
+            res = work.tile([P, N // P, n], F32, name="res", tag="res", bufs=len(sums))
+            if n == P:
                 nc.vector.tensor_tensor(res[:], bank[:], clim_sb[:].unsqueeze(2).to_broadcast([P, N // P, n]), ADD)
             else:
                 for b in range(N // P):

@@ -26,6 +26,7 @@ GROUP = 16
 CHUNK = 256
 HALF = PASS // 2
 ACT_BUFS = 6
+SHARE_H0, SHARE_H2, SHARE_H3, SHARE_Z1, SHARE_WIDE, SHARE_Z4, SHARE_Z6 = 64, 128, 64, 96, 160, 144, 96
 
 
 def tile_list_cyclone_intensity_nowcast_kernel(
@@ -123,16 +124,25 @@ def tile_list_cyclone_intensity_nowcast_kernel(
         w3_first.append(load_w3(0, HALF, HALF, "slot_tanh"))
         w2_raw = held("w2_raw", [P, M], I32, "slot_w2_sc")
         nc.sync.dma_start(w2_raw[:], words(w2_words[0].rearrange("p c i -> p (c i)")))
-        w3_second = load_w3(1, 0, PASS, "slot_gain0")
+        w3_second = [load_w3(1, 0, HALF, "slot_second0"), load_w3(1, HALF, HALF, "slot_second1")]
         w3_late = [load_w3(0, PASS, PASS), load_w3(1, PASS, PASS, "slot_shared")]
-        w4_raw = held("w4_raw", [P, 2, PACK, N], F32)
+        w4_raw = [held("w4_first", [P, PACK, N], F32), held("w4_second", [P, PACK, N], F32)]
         for am in range(2):
             rows = w4[am * PASS : (am + 1) * PASS, :].rearrange("(c t i) n -> i c t n", t=PACK, i=2)
             for i in range(2):
-                nc.sync.dma_start(w4_raw[i:P:2, am, :, :], rows[i])
+                nc.sync.dma_start(w4_raw[am][i:P:2, :, :], rows[i])
         with nc.allow_non_contiguous_dma(reason="one value a partition"):
             nc.sync.dma_start(clim_sb[:], clim.rearrange("(b p) -> p b", p=P))
 
+
+        nc.scalar.copy(gains_sb[:, 0:PACK], gain1_sb[:])
+        nc.scalar.copy(gains_sb[:, PACK : 3 * PACK].rearrange("p (a t) -> p a t", a=2), gain2_raw[:, :, 0:8:2])
+        gain_bank = gain_pool.tile([P, 2, P], F32, name="gain_bank")
+        nc.tensor.transpose(gain_bank[:, 1, :], gains_sb[:], identity[:])
+        gains_turned = held("gains_turned", [P, P], F32)
+        nc.scalar.copy(gains_turned[:], gain_bank[:, 1, :])
+        nc.tensor.transpose(gain_bank[:, 0, :], gains_turned[:], identity[:])
+        gains_ps = gain_bank[:, 0, :]
 
         v_codes = [held("v_codes%d" % a, [P, S], U32) for a in range(2)]
 
@@ -254,48 +264,53 @@ def tile_list_cyclone_intensity_nowcast_kernel(
                 )
             return sl[:].rearrange("p (u j e) -> p j u e", u=banks, e=per_bank)
 
-        def stage3(j0, n):
-            bank = psum.tile([P, N // P, n], F32, name="bank", tag="bank")
-            for am in range(2):
-                z_codes, z_sc = columns(z_done[am], j0, n)
-                for b in range(N // P):
-                    wcols = slice(am * N + b * P, am * N + (b + 1) * P)
-                    nc.tensor.matmul_mx(
-                        bank[:, b, :],
-                        lhsT=w4_codes[:, wcols].bitcast(FP8X4),
-                        lhsT_scale=w4_sc[:, wcols],
-                        rhs=z_codes,
-                        rhs_scale=z_sc,
-                        start=(am == 0 and b == 0),
-                        stop=(am == 1 and b == N // P - 1),
-                    )
+        def stage3_pass(am, j0, n, bank):
+            z_codes, z_sc = columns(z_done[am], j0, n)
+            for b in range(N // P):
+                wcols = slice(am * N + b * P, am * N + (b + 1) * P)
+                nc.tensor.matmul_mx(
+                    bank[:, b, :],
+                    lhsT=w4_codes[:, wcols].bitcast(FP8X4),
+                    lhsT_scale=w4_sc[:, wcols],
+                    rhs=z_codes,
+                    rhs_scale=z_sc,
+                    start=(am == 0 and b == 0),
+                    stop=(am == 1 and b == N // P - 1),
+                )
             return j0, n, bank
+
+        def stage3_open(j0, n):
+            return stage3_pass(0, j0, n, psum.tile([P, N // P, n], F32, name="bank", tag="bank"))
+
+        def stage3(j0, n):
+            return stage3_pass(1, *stage3_open(j0, n))
 
         def cast_w4(am, cast):
             cast(
                 w4_bf[:, am * N * PACK : (am + 1) * N * PACK].rearrange("p (c i t) -> p c t i", t=PACK, i=2),
-                w4_raw[:, am].rearrange("p t (c i) -> p c t i", i=2),
+                w4_raw[am][:].rearrange("p t (c i) -> p c t i", i=2),
             )
+
+        def share_first(values, first, share, slot):
+            shared = held("shared", [P, CHUNK * PACK], BF16, slot)[:]
+            pool_gain(values[:, 0:share], first, shared[:, 0 : share * PACK])
+            return lambda: gain(values[:, share:CHUNK], first, shared[:, share * PACK : CHUNK * PACK]), shared
+
+        def share_out(values, first, share, slot):
+            shared = held("shared", [P, CHUNK * PACK], BF16, slot)[:]
+            cut = CHUNK - share
+            pool_gain(values[:, cut:CHUNK], first, shared[:, cut * PACK : CHUNK * PACK])
+            return lambda: gain(values[:, 0:cut], first, shared[:, 0 : cut * PACK]), shared
 
         h_done, w3_done, z_done = {}, {}, [{}, {}]
         bf_first, bf_second = staging("bf_first"), staging("bf_second")
         late_bf = [staging("bf_late0"), staging("bf_late1")]
         w4_bf = staging("bf_w4")
 
-        nc.scalar.copy(gains_sb[:, 0:PACK], gain1_sb[:])
-        nc.scalar.copy(gains_sb[:, PACK : 3 * PACK].rearrange("p (a t) -> p a t", a=2), gain2_raw[:, :, 0:8:2])
-        gain_bank = gain_pool.tile([P, 2, P], F32, name="gain_bank")
-        nc.tensor.transpose(gain_bank[:, 1, :], gains_sb[:], identity[:])
-        gains_turned = held("gains_turned", [P, P], F32)
-        nc.scalar.copy(gains_turned[:], gain_bank[:, 1, :])
-        nc.tensor.transpose(gain_bank[:, 0, :], gains_turned[:], identity[:])
-        gains_ps = gain_bank[:, 0, :]
-
         cast_w3(bf_first, 0, w3_first[0], nc.scalar.copy)
         cast_w3(bf_first, HALF, w3_first[1], nc.scalar.copy)
-        tanh_pair = held("tanh_pair", [P, 2, CHUNK * PACK], F32, "slot_tanh")
-        tanh = [stage1(0, tanh_pair[:, 0, :]), stage1(CHUNK, tanh_pair[:, 1, :]), stage1(2 * CHUNK), stage1(3 * CHUNK)]
-        cast_w3(late_bf[0], 0, w3_late[0], nc.scalar.copy)
+        tanh = [stage1(0, held("tanh_first", [P, CHUNK * PACK], F32, "slot_tanh")[:])]
+        cast_w3(bf_second, 0, w3_second[0], nc.scalar.copy)
         w2_codes = held("w2_codes", [P, M], I32)
         nc.vector.tensor_copy(
             w2_codes[:].rearrange("p (a t c i) -> p a t c i", a=2, t=PACK, i=2),
@@ -307,67 +322,66 @@ def tile_list_cyclone_intensity_nowcast_kernel(
             w2_sc[:].bitcast(U16).rearrange("p (a t c) -> p a t c", a=2, t=PACK),
             w2s_raw[:].bitcast(U16).rearrange("p (a c t) -> p a t c", a=2, t=PACK),
         )
-        h0 = gain(tanh[0], 0)
-        cast_w3(bf_second, 0, w3_second, nc.vector.tensor_copy)
+        rest, h0 = share_out(tanh[0], 0, SHARE_H0, "h0")
+        rest()
+        cast_w3(bf_second, HALF, w3_second[1], nc.vector.tensor_copy)
+        tanh_rest = held("tanh_rest", [P, 3, CHUNK * PACK], F32, "slot_second0")
+        tanh.extend([stage1(k * CHUNK, tanh_rest[:, k - 1, :]) for k in range(1, 4)])
+        cast_w3(late_bf[0], 0, w3_late[0], nc.scalar.copy)
         quantize_run("h", h_done, 0, h0)
         w3_done[(1, 0)] = quantize("w3_10", bf_second, PASS)
         silu0 = stage2(0, 0, CHUNK)
 
-        def window(own_values, own_first, pool_values, rest_values, first, own=None, slot="bf_second"):
-            shared = held("shared", [P, CHUNK * PACK], BF16, slot)[:]
-            pool_gain(pool_values, first, shared[:, 0:PASS])
-            own = gain(own_values, own_first, own)
-            gain(rest_values, first, shared[:, PASS : 2 * PASS])
-            return own, shared
-
-        h1_tile = held("h1_tile", [P, CHUNK * PACK], BF16, "slot_gain0")[:]
-        own, shared = window(tanh[1], 0, tanh[2][:, 0:P], tanh[2][:, P:CHUNK], 0, h1_tile)
+        h1_tile = held("h1_tile", [P, CHUNK * PACK], BF16, "slot_second1")[:]
+        rest, shared = share_first(tanh[2], 0, SHARE_H2, "bf_second")
+        own = gain(tanh[1], 0, h1_tile)
+        rest()
         quantize_run("h", h_done, CHUNK, own)
-        silu1 = [stage2(0, CHUNK, P), stage2(0, CHUNK + P, P)]
+        silu1 = stage2(0, CHUNK, CHUNK)
         quantize_run("h", h_done, 2 * CHUNK, shared)
-        silu2 = [stage2(0, 2 * CHUNK, P), stage2(0, 2 * CHUNK + P, P)]
-        h3 = gain(tanh[3], 0)
-        w3_done[(0, 1)] = quantize("w3_01", late_bf[0], PASS)
+        silu2 = stage2(0, 2 * CHUNK, CHUNK)
+        rest, h3 = share_first(tanh[3], 0, SHARE_H3, "bf_second")
+        cast_w3_half(late_bf[1], 0, w3_late[1], nc.vector.tensor_copy)
+        rest()
+        cast_w3_half(late_bf[1], 2, w3_late[1], nc.vector.tensor_copy)
         quantize_run("h", h_done, 3 * CHUNK, h3)
         silu3 = stage2(0, 3 * CHUNK, CHUNK)
-        cast_w3(late_bf[1], 0, w3_late[1], nc.vector.tensor_copy)
-        own, shared = window(silu0, PACK, silu1[0], silu1[1], PACK, None, "slot_shared")
+        w3_done[(0, 1)] = quantize("w3_01", late_bf[0], PASS)
+        rest, shared = share_out(silu1, PACK, SHARE_Z1, "slot_shared")
+        own = gain(silu0, PACK)
+        rest()
         w3_done[(1, 1)] = quantize("w3_11", late_bf[1], PASS)
         quantize_run("z0", z_done[0], 0, own)
         quantize_run("z0", z_done[0], CHUNK, shared)
-        own, shared = window(silu3, PACK, silu2[0], silu2[1], PACK, None, "slot_shared")
+        rest, shared = share_out(silu2, PACK, SHARE_WIDE, "slot_shared")
+        own = gain(silu3, PACK)
+        rest()
         cast_w4(0, nc.scalar.copy)
-        cast_w4(1, nc.scalar.copy)
-        late_four = held("late_four", [P, PACK, PASS], F32, "w4_raw")
-        late = [stage2(1, k * P, P, late_four[:, k, :]) for k in range(4)]
-        late.extend([stage2(1, k * P, P) for k in range(4, 8)])
+        late_tile = held("late_tile", [P, 2, CHUNK * PACK], F32, "w4_first")
+        late = [stage2(1, k * CHUNK, CHUNK, late_tile[:, k, :]) for k in range(2)]
+        late.append(stage2(1, 2 * CHUNK, CHUNK))
+        late.extend([stage2(1, 3 * CHUNK, P), stage2(1, 3 * CHUNK + P, P)])
+        cast_w4(1, nc.vector.tensor_copy)
         quantize_run("z0", z_done[0], 3 * CHUNK, own)
         w4_codes, w4_sc = quantize("w4", w4_bf, 2 * N)
         quantize_run("z0", z_done[0], 2 * CHUNK, shared)
-
-        def pair_tile():
-            return work.tile([P, CHUNK * PACK], BF16, name="act16", tag="act16", align_bytes=64)[:]
-
-        shared = held("shared", [P, CHUNK * PACK], BF16, "slot_shared")[:]
-        pool_gain(late[0], 2 * PACK, shared[:, 0:PASS])
-        gain(late[1], 2 * PACK, shared[:, PASS : 2 * PASS])
-        own = pair_tile()
-        gain(late[2], 2 * PACK, own[:, 0:PASS])
-        gain(late[3], 2 * PACK, own[:, PASS : 2 * PASS])
+        rest, shared = share_out(late[0], 2 * PACK, SHARE_Z4, "slot_shared")
+        rest()
+        own = gain(late[1], 2 * PACK)
         quantize_run("z1", z_done[1], 0, shared)
         quantize_run("z1", z_done[1], CHUNK, own)
         sums = [stage3(0, CHUNK), stage3(CHUNK, CHUNK)]
-        shared = held("shared", [P, CHUNK * PACK], BF16, "slot_shared")[:]
-        pool_gain(late[4], 2 * PACK, shared[:, 0:PASS])
-        gain(late[5], 2 * PACK, shared[:, PASS : 2 * PASS])
-        third = gain(late[6], 2 * PACK)
-        last = gain(late[7], 2 * PACK)
+        opened = [stage3_open(2 * CHUNK, CHUNK), stage3_open(3 * CHUNK, P), stage3_open(3 * CHUNK + P, P)]
+        rest, shared = share_out(late[2], 2 * PACK, SHARE_Z6, "slot_shared")
+        rest()
+        third = gain(late[3], 2 * PACK)
         quantize_run("z1", z_done[1], 2 * CHUNK, shared)
-        sums.append(stage3(2 * CHUNK, CHUNK))
+        sums.append(stage3_pass(1, *opened[0]))
+        last = gain(late[4], 2 * PACK)
         quantize_run("z1", z_done[1], 3 * CHUNK, third)
-        sums.append(stage3(3 * CHUNK, P))
+        sums.append(stage3_pass(1, *opened[1]))
         quantize_run("z1", z_done[1], 3 * CHUNK + P, last)
-        sums.append(stage3(3 * CHUNK + P, P))
+        sums.append(stage3_pass(1, *opened[2]))
 
         for j0, n, bank in sums:
             res = work.tile([P, N // P, n], F32, name="res", tag="res", bufs=len(sums))

@@ -26,7 +26,7 @@ GROUP = 16
 CHUNK = 256
 HALF = PASS // 2
 ACT_BUFS = 6
-SHARE_H0, SHARE_H2, SHARE_H3, SHARE_Z1, SHARE_WIDE, SHARE_Z4, SHARE_Z6 = 64, 128, 64, 96, 160, 144, 96
+SHARE_H0, SHARE_H2, SHARE_H3, SHARE_Z1, SHARE_WIDE, SHARE_Z4, SHARE_Z6 = 0, 128, 64, 128, 128, 128, 96
 
 
 def tile_list_cyclone_intensity_nowcast_kernel(
@@ -50,10 +50,11 @@ def tile_list_cyclone_intensity_nowcast_kernel(
 
         identity = held("identity", [P, P], F32)
         make_identity(nc, identity[:])
-        w2s_raw = held("w2s_raw", [P, M], U8)
+        w2s_raw = held("w2s_raw", [P, PASS], U8)
         nc.gpsimd.memset(words(w2s_raw[:]), 0)
-        for r in range(4):
-            nc.gpsimd.dma_start(words(w2s_raw[r:P:32, :]), words(w2_scales[0, r:ROWS:4, :]))
+        for d in range(4):
+            rows = w2_scales[0, 4 * d : 4 * d + 4, :].rearrange("r (a c) -> a r c", a=2)
+            nc.gpsimd.dma_start(words(w2s_raw[32 * d : 32 * d + 8, :]), words(rows))
 
         gain1_sb = held("gain1_sb", [P, PACK], F32)
         nc.scalar.dma_start(gain1_sb[:], gain1.rearrange("(p t) -> p t", t=PACK))
@@ -246,7 +247,7 @@ def tile_list_cyclone_intensity_nowcast_kernel(
                             x_codes, x_sc = v_codes[step][:, cols].bitcast(FP8X4), v_scales[step][:, cols]
                         else:
                             w2cols = slice(am * PASS + wcols.start, am * PASS + wcols.stop)
-                            w_codes, w_sc = w2_codes[:, w2cols], w2_sc[:, w2cols]
+                            w_codes, w_sc = w2_codes[:, w2cols], w2_sc[4 * am : P, wcols]
                             x_codes, x_sc = h_codes, h_sc
                         nc.tensor.matmul_mx(
                             bank[:, e, :],
@@ -285,22 +286,33 @@ def tile_list_cyclone_intensity_nowcast_kernel(
         def stage3(j0, n):
             return stage3_pass(1, *stage3_open(j0, n))
 
-        def cast_w4(am, cast):
-            cast(
-                w4_bf[:, am * N * PACK : (am + 1) * N * PACK].rearrange("p (c i t) -> p c t i", t=PACK, i=2),
-                w4_raw[am][:].rearrange("p t (c i) -> p c t i", i=2),
-            )
+        def cast_w4(am, n0, n1, cast):
+            dst = w4_bf[:, am * N * PACK : (am + 1) * N * PACK].rearrange("p (c i t) -> p c t i", t=PACK, i=2)
+            src = w4_raw[am][:].rearrange("p t (c i) -> p c t i", i=2)
+            cast(dst[:, n0 // 2 : n1 // 2], src[:, n0 // 2 : n1 // 2])
 
-        def share_first(values, first, share, slot):
+        def share_out(pieces, first, share, slot):
             shared = held("shared", [P, CHUNK * PACK], BF16, slot)[:]
-            pool_gain(values[:, 0:share], first, shared[:, 0 : share * PACK])
-            return lambda: gain(values[:, share:CHUNK], first, shared[:, share * PACK : CHUNK * PACK]), shared
+            pool_gain(pieces[0][:, 0:share], first, shared[:, 0 : share * PACK])
 
-        def share_out(values, first, share, slot):
-            shared = held("shared", [P, CHUNK * PACK], BF16, slot)[:]
-            cut = CHUNK - share
-            pool_gain(values[:, cut:CHUNK], first, shared[:, cut * PACK : CHUNK * PACK])
-            return lambda: gain(values[:, 0:cut], first, shared[:, 0 : cut * PACK]), shared
+            def rest():
+                if share < P:
+                    gain(pieces[0][:, share:P], first, shared[:, share * PACK : PASS])
+                gain(pieces[1], first, shared[:, PASS : 2 * PASS])
+
+            return rest, shared
+
+        def two_pieces(am, j0, tile=None):
+            return [stage2(am, j0 + k * P, P, None if tile is None else tile[:, k * PASS : (k + 1) * PASS]) for k in range(2)]
+
+        def store(j0, n, bank):
+            res = work.tile([P, N // P, n], F32, name="res", tag="res", bufs=5)
+            if n == P:
+                nc.vector.tensor_tensor(res[:], bank[:], clim_sb[:].unsqueeze(2).to_broadcast([P, N // P, n]), ADD)
+            else:
+                for b in range(N // P):
+                    nc.scalar.activation(res[:, b, :], bank[:, b, :], ACT.Identity, bias=clim_sb[:, b : b + 1])
+            nc.sync.dma_start(out[:, j0 : j0 + n].rearrange("(b p) j -> p b j", p=P), res[:])
 
         h_done, w3_done, z_done = {}, {}, [{}, {}]
         bf_first, bf_second = staging("bf_first"), staging("bf_second")
@@ -317,13 +329,12 @@ def tile_list_cyclone_intensity_nowcast_kernel(
             w2_raw[:].rearrange("p (a c t i) -> p a t c i", a=2, t=PACK, i=2),
         )
         w3_done[(0, 0)] = quantize("w3_00", bf_first, PASS)
-        w2_sc = held("w2_sc", [P, M], U8, "slot_w2_sc")
+        w2_sc = held("w2_sc", [P, PASS], U8, "slot_w2_sc")
         nc.vector.tensor_copy(
-            w2_sc[:].bitcast(U16).rearrange("p (a t c) -> p a t c", a=2, t=PACK),
-            w2s_raw[:].bitcast(U16).rearrange("p (a c t) -> p a t c", a=2, t=PACK),
+            w2_sc[:].bitcast(U16).rearrange("p (t c) -> p t c", t=PACK),
+            w2s_raw[:].bitcast(U16).rearrange("p (c t) -> p t c", t=PACK),
         )
-        rest, h0 = share_out(tanh[0], 0, SHARE_H0, "h0")
-        rest()
+        h0 = gain(tanh[0], 0)
         cast_w3(bf_second, HALF, w3_second[1], nc.vector.tensor_copy)
         tanh_rest = held("tanh_rest", [P, 3, CHUNK * PACK], F32, "slot_second0")
         tanh.extend([stage1(k * CHUNK, tanh_rest[:, k - 1, :]) for k in range(1, 4)])
@@ -333,61 +344,53 @@ def tile_list_cyclone_intensity_nowcast_kernel(
         silu0 = stage2(0, 0, CHUNK)
 
         h1_tile = held("h1_tile", [P, CHUNK * PACK], BF16, "slot_second1")[:]
-        rest, shared = share_first(tanh[2], 0, SHARE_H2, "bf_second")
+        rest, shared = share_out([tanh[2][:, 0:P], tanh[2][:, P:CHUNK]], 0, P, "bf_second")
         own = gain(tanh[1], 0, h1_tile)
         rest()
         quantize_run("h", h_done, CHUNK, own)
-        silu1 = stage2(0, CHUNK, CHUNK)
+        silu1 = two_pieces(0, CHUNK)
         quantize_run("h", h_done, 2 * CHUNK, shared)
-        silu2 = stage2(0, 2 * CHUNK, CHUNK)
-        rest, h3 = share_first(tanh[3], 0, SHARE_H3, "bf_second")
+        silu2 = two_pieces(0, 2 * CHUNK)
+        h3 = gain(tanh[3], 0)
         cast_w3_half(late_bf[1], 0, w3_late[1], nc.vector.tensor_copy)
-        rest()
-        cast_w3_half(late_bf[1], 2, w3_late[1], nc.vector.tensor_copy)
         quantize_run("h", h_done, 3 * CHUNK, h3)
         silu3 = stage2(0, 3 * CHUNK, CHUNK)
+        cast_w3_half(late_bf[1], 2, w3_late[1], nc.vector.tensor_copy)
         w3_done[(0, 1)] = quantize("w3_01", late_bf[0], PASS)
         rest, shared = share_out(silu1, PACK, SHARE_Z1, "slot_shared")
         own = gain(silu0, PACK)
         rest()
         w3_done[(1, 1)] = quantize("w3_11", late_bf[1], PASS)
+        cast_w4(1, 0, N, nc.vector.tensor_copy)
         quantize_run("z0", z_done[0], 0, own)
         quantize_run("z0", z_done[0], CHUNK, shared)
         rest, shared = share_out(silu2, PACK, SHARE_WIDE, "slot_shared")
         own = gain(silu3, PACK)
         rest()
-        cast_w4(0, nc.scalar.copy)
+        cast_w4(0, 0, N, nc.scalar.copy)
         late_tile = held("late_tile", [P, 2, CHUNK * PACK], F32, "w4_first")
-        late = [stage2(1, k * CHUNK, CHUNK, late_tile[:, k, :]) for k in range(2)]
-        late.append(stage2(1, 2 * CHUNK, CHUNK))
-        late.extend([stage2(1, 3 * CHUNK, P), stage2(1, 3 * CHUNK + P, P)])
-        cast_w4(1, nc.vector.tensor_copy)
-        quantize_run("z0", z_done[0], 3 * CHUNK, own)
+        late = [two_pieces(1, 0, late_tile[:, 0, :]), stage2(1, CHUNK, CHUNK, late_tile[:, 1, :])]
+        late.append(two_pieces(1, 2 * CHUNK))
+        late.append(stage2(1, 3 * CHUNK, P))
         w4_codes, w4_sc = quantize("w4", w4_bf, 2 * N)
         quantize_run("z0", z_done[0], 2 * CHUNK, shared)
+        quantize_run("z0", z_done[0], 3 * CHUNK, own)
         rest, shared = share_out(late[0], 2 * PACK, SHARE_Z4, "slot_shared")
         rest()
         own = gain(late[1], 2 * PACK)
         quantize_run("z1", z_done[1], 0, shared)
+        store(*stage3(0, CHUNK))
+        late.append(stage2(1, 3 * CHUNK + P, P))
         quantize_run("z1", z_done[1], CHUNK, own)
-        sums = [stage3(0, CHUNK), stage3(CHUNK, CHUNK)]
+        store(*stage3(CHUNK, CHUNK))
         opened = [stage3_open(2 * CHUNK, CHUNK), stage3_open(3 * CHUNK, P), stage3_open(3 * CHUNK + P, P)]
         rest, shared = share_out(late[2], 2 * PACK, SHARE_Z6, "slot_shared")
         rest()
         third = gain(late[3], 2 * PACK)
         quantize_run("z1", z_done[1], 2 * CHUNK, shared)
-        sums.append(stage3_pass(1, *opened[0]))
+        store(*stage3_pass(1, *opened[0]))
         last = gain(late[4], 2 * PACK)
         quantize_run("z1", z_done[1], 3 * CHUNK, third)
-        sums.append(stage3_pass(1, *opened[1]))
+        store(*stage3_pass(1, *opened[1]))
         quantize_run("z1", z_done[1], 3 * CHUNK + P, last)
-        sums.append(stage3_pass(1, *opened[2]))
-
-        for j0, n, bank in sums:
-            res = work.tile([P, N // P, n], F32, name="res", tag="res", bufs=len(sums))
-            if n == P:
-                nc.vector.tensor_tensor(res[:], bank[:], clim_sb[:].unsqueeze(2).to_broadcast([P, N // P, n]), ADD)
-            else:
-                for b in range(N // P):
-                    nc.scalar.activation(res[:, b, :], bank[:, b, :], ACT.Identity, bias=clim_sb[:, b : b + 1])
-            nc.sync.dma_start(out[:, j0 : j0 + n].rearrange("(b p) j -> p b j", p=P), res[:])
+        store(*stage3_pass(1, *opened[2]))

@@ -26,7 +26,10 @@ GROUP = 16
 CHUNK = 256
 HALF = PASS // 2
 ACT_BUFS = 6
-SHARE_H0, SHARE_H2, SHARE_H3, SHARE_Z1, SHARE_WIDE, SHARE_Z4, SHARE_Z6 = 0, 128, 64, 128, 128, 128, 96
+SHARE_ALONE = CHUNK // 4
+SHARE_PAIR = P
+SHARE_LAST = 3 * P // 4
+GAIN_H, GAIN_Z = 0, (PACK, 2 * PACK)
 
 
 def tile_list_cyclone_intensity_nowcast_kernel(
@@ -75,8 +78,8 @@ def tile_list_cyclone_intensity_nowcast_kernel(
         nc.vector.memset(zero_in[:], 0.0)
         nc.scalar.activation(zero_bias[:], zero_in[:], ACT.Silu)
 
-        def load_table(a, slot=None):
-            window = held("table%d" % a, [P, T], I32, slot)
+        def load_table(a):
+            window = held("table%d" % a, [P, T], I32)
             nc.sync.dma_start(window[:], words(tab_words[a].rearrange("p t i -> p (t i)")))
             return window
 
@@ -97,7 +100,6 @@ def tile_list_cyclone_intensity_nowcast_kernel(
                 words(w1s_raw[r:P:32, :].rearrange("d (a c) -> d a c", a=2)),
                 words(w1_scales[:, r:ROWS:4, :].rearrange("a d c -> d a c")),
             )
-
 
         v_both = held("v_both", [P, 2 * S], U8)
         nc.vector.memset(words(v_both[:]), 0)
@@ -123,10 +125,16 @@ def tile_list_cyclone_intensity_nowcast_kernel(
         for d in range(4):
             nc.sync.dma_start(words(v_both[32 * d : 32 * d + 4, :]), words(picked_scales[32 * d : 32 * d + 32 : 4, :]))
         w3_first.append(load_w3(0, HALF, HALF, "slot_tanh"))
-        w2_raw = held("w2_raw", [P, M], I32, "slot_w2_sc")
-        nc.sync.dma_start(w2_raw[:], words(w2_words[0].rearrange("p c i -> p (c i)")))
-        w3_second = [load_w3(1, 0, HALF, "slot_second0"), load_w3(1, HALF, HALF, "slot_second1")]
-        w3_late = [load_w3(0, PASS, PASS), load_w3(1, PASS, PASS, "slot_shared")]
+
+        def load_w2(am, slot=None):
+            raw = held("w2_raw%d" % am, [P, PASS], I32, slot)
+            nc.sync.dma_start(raw[:], words(w2_words[0, :, am * PASS : (am + 1) * PASS].rearrange("p c i -> p (c i)")))
+            return raw
+
+        w2_raw = [load_w2(0, "slot_w2_sc")]
+        w3_second = load_w3(1, 0, PASS, "slot_gain0")
+        w3_late = [load_w3(0, PASS, PASS), load_w3(1, PASS, PASS)]
+        w2_raw.append(load_w2(1))
         w4_raw = [held("w4_first", [P, PACK, N], F32), held("w4_second", [P, PACK, N], F32)]
         for am in range(2):
             rows = w4[am * PASS : (am + 1) * PASS, :].rearrange("(c t i) n -> i c t n", t=PACK, i=2)
@@ -135,9 +143,8 @@ def tile_list_cyclone_intensity_nowcast_kernel(
         with nc.allow_non_contiguous_dma(reason="one value a partition"):
             nc.sync.dma_start(clim_sb[:], clim.rearrange("(b p) -> p b", p=P))
 
-
-        nc.scalar.copy(gains_sb[:, 0:PACK], gain1_sb[:])
-        nc.scalar.copy(gains_sb[:, PACK : 3 * PACK].rearrange("p (a t) -> p a t", a=2), gain2_raw[:, :, 0:8:2])
+        nc.scalar.copy(gains_sb[:, GAIN_H : GAIN_H + PACK], gain1_sb[:])
+        nc.scalar.copy(gains_sb[:, GAIN_Z[0] : GAIN_Z[1] + PACK].rearrange("p (a t) -> p a t", a=2), gain2_raw[:, :, 0:8:2])
         gain_bank = gain_pool.tile([P, 2, P], F32, name="gain_bank")
         nc.tensor.transpose(gain_bank[:, 1, :], gains_sb[:], identity[:])
         gains_turned = held("gains_turned", [P, P], F32)
@@ -163,8 +170,8 @@ def tile_list_cyclone_intensity_nowcast_kernel(
             nc.vector.quantize_mx(codes[:].bitcast(FP8X4), scales[:], grouped[:])
             return codes, scales
 
-        def staging(name, slot=None):
-            return held(name, [P, PASS * PACK], BF16, slot)
+        def staging(name):
+            return held(name, [P, PASS * PACK], BF16)
 
         def cast_w3(grouped, m0, raw, cast):
             dst = grouped[:].rearrange("p (t c i x) -> p c t x i", t=PACK, i=2, x=PACK)
@@ -187,15 +194,13 @@ def tile_list_cyclone_intensity_nowcast_kernel(
             dst = grouped.rearrange("p (j u e) -> p j u e", j=n, u=u)
             engine.tensor_tensor(dst, values, gains.unsqueeze(1).to_broadcast([P, n, u, e]), MULT)
 
+        def products(n):
+            return work.tile([P, n * PACK], BF16, name="act16", tag="act16", align_bytes=64)[:]
+
         def gain(values, first, grouped=None):
-            n = values.shape[1]
-            if grouped is None:
-                grouped = work.tile([P, n * PACK], BF16, name="act16", tag="act16", align_bytes=64)[:]
+            grouped = products(values.shape[1]) if grouped is None else grouped
             apply_gains(nc.vector, gains_ps, values, first, grouped)
             return grouped
-
-        def shared_tile():
-            return held("shared", [P, CHUNK * PACK], BF16, "bf_second")[:]
 
         def pool_gain(values, first, grouped):
             apply_gains(nc.gpsimd, gains_sb, values, first, grouped)
@@ -302,8 +307,16 @@ def tile_list_cyclone_intensity_nowcast_kernel(
 
             return rest, shared
 
+        def gain_with_pool(values, first, slot):
+            grouped = held("shared", [P, CHUNK * PACK], BF16, slot)[:]
+            cut = CHUNK - SHARE_ALONE
+            pool_gain(values[:, cut:CHUNK], first, grouped[:, cut * PACK : CHUNK * PACK])
+            gain(values[:, 0:cut], first, grouped[:, 0 : cut * PACK])
+            return grouped
+
         def two_pieces(am, j0, tile=None):
-            return [stage2(am, j0 + k * P, P, None if tile is None else tile[:, k * PASS : (k + 1) * PASS]) for k in range(2)]
+            tiles = [None, None] if tile is None else [tile[:, 0:PASS], tile[:, PASS : 2 * PASS]]
+            return [stage2(am, j0 + k * P, P, tiles[k]) for k in range(2)]
 
         def store(j0, n, bank):
             res = work.tile([P, N // P, n], F32, name="res", tag="res", bufs=5)
@@ -321,76 +334,84 @@ def tile_list_cyclone_intensity_nowcast_kernel(
 
         cast_w3(bf_first, 0, w3_first[0], nc.scalar.copy)
         cast_w3(bf_first, HALF, w3_first[1], nc.scalar.copy)
-        tanh = [stage1(0, held("tanh_first", [P, CHUNK * PACK], F32, "slot_tanh")[:])]
-        cast_w3(bf_second, 0, w3_second[0], nc.scalar.copy)
+        tanh_pair = held("tanh_pair", [P, 2, CHUNK * PACK], F32, "slot_tanh")
+        tanh = [stage1(0, tanh_pair[:, 0, :]), stage1(CHUNK, tanh_pair[:, 1, :]), stage1(2 * CHUNK), stage1(3 * CHUNK)]
+        cast_w3(late_bf[0], 0, w3_late[0], nc.scalar.copy)
         w2_codes = held("w2_codes", [P, M], I32)
-        nc.vector.tensor_copy(
-            w2_codes[:].rearrange("p (a t c i) -> p a t c i", a=2, t=PACK, i=2),
-            w2_raw[:].rearrange("p (a c t i) -> p a t c i", a=2, t=PACK, i=2),
-        )
+
+        def reorder_w2(am):
+            nc.vector.tensor_copy(
+                w2_codes[:, am * PASS : (am + 1) * PASS].rearrange("p (t c i) -> p t c i", t=PACK, i=2),
+                w2_raw[am][:].rearrange("p (c t i) -> p t c i", t=PACK, i=2),
+            )
+
+        reorder_w2(0)
         w3_done[(0, 0)] = quantize("w3_00", bf_first, PASS)
         w2_sc = held("w2_sc", [P, PASS], U8, "slot_w2_sc")
         nc.vector.tensor_copy(
             w2_sc[:].bitcast(U16).rearrange("p (t c) -> p t c", t=PACK),
             w2s_raw[:].bitcast(U16).rearrange("p (c t) -> p t c", t=PACK),
         )
-        h0 = gain(tanh[0], 0)
-        cast_w3(bf_second, HALF, w3_second[1], nc.vector.tensor_copy)
-        tanh_rest = held("tanh_rest", [P, 3, CHUNK * PACK], F32, "slot_second0")
-        tanh.extend([stage1(k * CHUNK, tanh_rest[:, k - 1, :]) for k in range(1, 4)])
-        cast_w3(late_bf[0], 0, w3_late[0], nc.scalar.copy)
-        quantize_run("h", h_done, 0, h0)
+        h_first = gain_with_pool(tanh[0], GAIN_H, "bf_first")
+        cast_w3(bf_second, 0, w3_second, nc.vector.tensor_copy)
+        quantize_run("h", h_done, 0, h_first)
         w3_done[(1, 0)] = quantize("w3_10", bf_second, PASS)
-        silu0 = stage2(0, 0, CHUNK)
+        early = [stage2(0, 0, CHUNK)]
 
-        h1_tile = held("h1_tile", [P, CHUNK * PACK], BF16, "slot_second1")[:]
-        rest, shared = share_out([tanh[2][:, 0:P], tanh[2][:, P:CHUNK]], 0, P, "bf_second")
-        own = gain(tanh[1], 0, h1_tile)
+        h_second = held("h_second", [P, CHUNK * PACK], BF16, "slot_gain0")[:]
+        rest, shared = share_out([tanh[2][:, 0:P], tanh[2][:, P:CHUNK]], GAIN_H, SHARE_PAIR, "bf_second")
+        gain(tanh[1], GAIN_H, h_second)
         rest()
-        quantize_run("h", h_done, CHUNK, own)
-        silu1 = two_pieces(0, CHUNK)
+        quantize_run("h", h_done, CHUNK, h_second)
+        early.append(two_pieces(0, CHUNK))
         quantize_run("h", h_done, 2 * CHUNK, shared)
-        silu2 = two_pieces(0, 2 * CHUNK)
-        h3 = gain(tanh[3], 0)
+        early.append(two_pieces(0, 2 * CHUNK))
+        h_last = gain_with_pool(tanh[3], GAIN_H, "slot_gain0")
         cast_w3_half(late_bf[1], 0, w3_late[1], nc.vector.tensor_copy)
-        quantize_run("h", h_done, 3 * CHUNK, h3)
-        silu3 = stage2(0, 3 * CHUNK, CHUNK)
+        quantize_run("h", h_done, 3 * CHUNK, h_last)
+        early.append(stage2(0, 3 * CHUNK, CHUNK))
         cast_w3_half(late_bf[1], 2, w3_late[1], nc.vector.tensor_copy)
+        reorder_w2(1)
         w3_done[(0, 1)] = quantize("w3_01", late_bf[0], PASS)
-        rest, shared = share_out(silu1, PACK, SHARE_Z1, "slot_shared")
-        own = gain(silu0, PACK)
-        rest()
         w3_done[(1, 1)] = quantize("w3_11", late_bf[1], PASS)
-        cast_w4(1, 0, N, nc.vector.tensor_copy)
+
+        rest, shared = share_out(early[1], GAIN_Z[0], SHARE_PAIR, "bf_late1")
+        own = gain(early[0], GAIN_Z[0])
+        rest()
+        cast_w4(0, P, N, nc.vector.tensor_copy)
         quantize_run("z0", z_done[0], 0, own)
         quantize_run("z0", z_done[0], CHUNK, shared)
-        rest, shared = share_out(silu2, PACK, SHARE_WIDE, "slot_shared")
-        own = gain(silu3, PACK)
+        rest, shared = share_out(early[2], GAIN_Z[0], SHARE_PAIR, "bf_late1")
+        own = gain(early[3], GAIN_Z[0])
         rest()
-        cast_w4(0, 0, N, nc.scalar.copy)
-        late_tile = held("late_tile", [P, 2, CHUNK * PACK], F32, "w4_first")
-        late = [two_pieces(1, 0, late_tile[:, 0, :]), stage2(1, CHUNK, CHUNK, late_tile[:, 1, :])]
+        cast_w4(0, 0, P, nc.scalar.copy)
+        cast_w4(1, 0, N, nc.scalar.copy)
+        late_pair = held("late_pair", [P, 2, CHUNK * PACK], F32, "w4_second")
+        late = [two_pieces(1, 0, late_pair[:, 0, :]), two_pieces(1, CHUNK, late_pair[:, 1, :])]
         late.append(two_pieces(1, 2 * CHUNK))
-        late.append(stage2(1, 3 * CHUNK, P))
+        last_pieces = [stage2(1, 3 * CHUNK, P)]
         w4_codes, w4_sc = quantize("w4", w4_bf, 2 * N)
         quantize_run("z0", z_done[0], 2 * CHUNK, shared)
         quantize_run("z0", z_done[0], 3 * CHUNK, own)
-        rest, shared = share_out(late[0], 2 * PACK, SHARE_Z4, "slot_shared")
+
+        rest, shared = share_out(late[0], GAIN_Z[1], SHARE_PAIR, "bf_late1")
         rest()
-        own = gain(late[1], 2 * PACK)
+        own = products(CHUNK)
+        for k in range(2):
+            gain(late[1][k], GAIN_Z[1], own[:, k * PASS : (k + 1) * PASS])
         quantize_run("z1", z_done[1], 0, shared)
         store(*stage3(0, CHUNK))
-        late.append(stage2(1, 3 * CHUNK + P, P))
+        last_pieces.append(stage2(1, 3 * CHUNK + P, P))
         quantize_run("z1", z_done[1], CHUNK, own)
         store(*stage3(CHUNK, CHUNK))
         opened = [stage3_open(2 * CHUNK, CHUNK), stage3_open(3 * CHUNK, P), stage3_open(3 * CHUNK + P, P)]
-        rest, shared = share_out(late[2], 2 * PACK, SHARE_Z6, "slot_shared")
+        rest, shared = share_out(late[2], GAIN_Z[1], SHARE_LAST, "bf_late1")
         rest()
-        third = gain(late[3], 2 * PACK)
+        before_last = gain(last_pieces[0], GAIN_Z[1])
         quantize_run("z1", z_done[1], 2 * CHUNK, shared)
         store(*stage3_pass(1, *opened[0]))
-        last = gain(late[4], 2 * PACK)
-        quantize_run("z1", z_done[1], 3 * CHUNK, third)
+        last = gain(last_pieces[1], GAIN_Z[1])
+        quantize_run("z1", z_done[1], 3 * CHUNK, before_last)
         store(*stage3_pass(1, *opened[1]))
         quantize_run("z1", z_done[1], 3 * CHUNK + P, last)
         store(*stage3_pass(1, *opened[2]))

@@ -29,7 +29,9 @@ ACT_BUFS = 6
 SHARE_ALONE = CHUNK // 4
 SHARE_PAIR = P
 SHARE_LAST = 3 * P // 4
-GAIN_H, GAIN_Z = 0, (PACK, 2 * PACK)
+REPEAT = 8
+WIDE = REPEAT * PACK
+GAIN_H, GAIN_Z = 0, (WIDE, 2 * WIDE)
 
 
 def tile_list_cyclone_intensity_nowcast_kernel(
@@ -143,8 +145,14 @@ def tile_list_cyclone_intensity_nowcast_kernel(
         with nc.allow_non_contiguous_dma(reason="one value a partition"):
             nc.sync.dma_start(clim_sb[:], clim.rearrange("(b p) -> p b", p=P))
 
-        nc.scalar.copy(gains_sb[:, GAIN_H : GAIN_H + PACK], gain1_sb[:])
-        nc.scalar.copy(gains_sb[:, GAIN_Z[0] : GAIN_Z[1] + PACK].rearrange("p (a t) -> p a t", a=2), gain2_raw[:, :, 0:8:2])
+        nc.scalar.copy(
+            gains_sb[:, GAIN_H : GAIN_H + WIDE].rearrange("p (j t) -> p j t", t=PACK),
+            gain1_sb[:].unsqueeze(1).to_broadcast([P, REPEAT, PACK]),
+        )
+        nc.scalar.copy(
+            gains_sb[:, GAIN_Z[0] : GAIN_Z[1] + WIDE].rearrange("p (a j t) -> p a j t", a=2, t=PACK),
+            gain2_raw[:, :, 0:8:2].unsqueeze(2).to_broadcast([P, 2, REPEAT, PACK]),
+        )
         gain_bank = gain_pool.tile([P, 2, P], F32, name="gain_bank")
         nc.tensor.transpose(gain_bank[:, 1, :], gains_sb[:], identity[:])
         gains_turned = held("gains_turned", [P, P], F32)
@@ -203,7 +211,13 @@ def tile_list_cyclone_intensity_nowcast_kernel(
             return grouped
 
         def pool_gain(values, first, grouped):
-            apply_gains(nc.gpsimd, gains_sb, values, first, grouped)
+            rows = values.shape[1] // REPEAT
+            nc.gpsimd.tensor_tensor(
+                grouped.rearrange("p (r x) -> p r x", x=WIDE),
+                values.rearrange("p (r j) u e -> p r (j u e)", j=REPEAT),
+                gains_sb[:, first : first + WIDE].unsqueeze(1).to_broadcast([P, rows, WIDE]),
+                MULT,
+            )
 
         def quantize_run(name, done, j0, grouped):
             done[j0] = quantize("%s_%d" % (name, j0), grouped, grouped.shape[1] // PACK)

@@ -62,14 +62,12 @@ def tile_list_cyclone_intensity_nowcast_kernel(
             nc.gpsimd.dma_start(words(w2s_raw[32 * d : 32 * d + 8, :]), words(rows))
 
         gain1_sb = held("gain1_sb", [P, PACK], F32)
-        nc.scalar.dma_start(gain1_sb[:], gain1.rearrange("(p t) -> p t", t=PACK))
+        nc.sync.dma_start(gain1_sb[:], gain1.rearrange("(p t) -> p t", t=PACK))
         gain2_raw = held("gain2_raw", [P, 2, 8], F32)
         for i in range(2):
             nc.scalar.dma_start(
                 gain2_raw[i:P:2, :, 0:7], gain2.rearrange("(a c x) -> c a x", a=2, x=8)[:, :, i : i + 7]
             )
-        w1_raw = held("w1_raw", [P, 2, 2 * H], U8)
-        nc.sync.dma_start(words(w1_raw[:]), words(w1_words.rearrange("a p c -> p a c")))
 
         scale_window = held("scale_window", [P, T], U8)
         nc.vector.memset(words(scale_window[:]), 0)
@@ -92,6 +90,8 @@ def tile_list_cyclone_intensity_nowcast_kernel(
             return raw
 
         tables = [load_table(0)]
+        w1_raw = held("w1_raw", [P, 2, 2 * H], U8)
+        nc.sync.dma_start(words(w1_raw[:]), words(w1_words.rearrange("a p c -> p a c")))
         gains_sb = held("gains_sb", [P, P], F32)
         nc.vector.memset(gains_sb[:], 0.0)
 
@@ -106,27 +106,21 @@ def tile_list_cyclone_intensity_nowcast_kernel(
         v_both = held("v_both", [P, 2 * S], U8)
         nc.vector.memset(words(v_both[:]), 0)
         v_scales = [v_both[:, a * S : (a + 1) * S] for a in range(2)]
-        w3_first = [load_w3(0, 0, HALF)]
         tables.append(load_table(1))
 
         clim_sb = held("clim_sb", [P, N // P], F32)
 
         w1_codes = held("w1_codes", [P, 2, 2 * H], U8)
-        nc.vector.tensor_copy(
+        nc.scalar.copy(
             w1_codes[:].bitcast(U16).rearrange("p a (t c) -> p a t c", t=PACK),
             w1_raw[:].bitcast(U16).rearrange("p a (c t) -> p a t c", t=PACK),
         )
 
         picked_scales = held("picked_scales", [P, S], U8)
         nc.vector.tensor_copy(picked_scales[:], scale_window[:].indirect(offsets[:]))
-        w1_sc = held("w1_sc", [P, 2, H], U8)
-        nc.vector.tensor_copy(
-            w1_sc[:].rearrange("p a (t c) -> p a t c", t=PACK),
-            w1s_raw[:].rearrange("p (a c t) -> p a t c", a=2, t=PACK),
-        )
         for d in range(4):
             nc.sync.dma_start(words(v_both[32 * d : 32 * d + 4, :]), words(picked_scales[32 * d : 32 * d + 32 : 4, :]))
-        w3_first.append(load_w3(0, HALF, HALF, "slot_tanh"))
+        w3_first = load_w3(0, 0, PASS)
 
         def load_w2(am, slot=None):
             raw = held("w2_raw%d" % am, [P, PASS], I32, slot)
@@ -169,6 +163,11 @@ def tile_list_cyclone_intensity_nowcast_kernel(
             )
 
         gather_words(0, 0, S)
+        w1_sc = held("w1_sc", [P, 2, H], U8)
+        nc.vector.tensor_copy(
+            w1_sc[:].rearrange("p a (t c) -> p a t c", t=PACK),
+            w1s_raw[:].rearrange("p (a c t) -> p a t c", a=2, t=PACK),
+        )
         for j0, n in ((0, CHUNK), (CHUNK, CHUNK), (2 * CHUNK, 2 * CHUNK)):
             gather_words(1, j0, n)
 
@@ -225,30 +224,32 @@ def tile_list_cyclone_intensity_nowcast_kernel(
         def activations(n):
             return work.tile([P, n * PACK], F32, name="act32", tag="act32", bufs=ACT_BUFS)
 
-        def stage1(j0, th=None):
-            th = activations(CHUNK) if th is None else th
-            banks = [psum.tile([P, PACK, P], F32, name="bank", tag="bank") for half in range(CHUNK // P)]
-            for half, bank in enumerate(banks):
-                cols = slice(j0 + half * P, j0 + (half + 1) * P)
+        def stage1(j0, n, th=None):
+            per_bank = PASS // n
+            banks = PACK // per_bank
+            th = activations(n) if th is None else th
+            cols = slice(j0, j0 + n)
+            for u in range(banks):
+                bank = psum.tile([P, per_bank, n], F32, name="bank", tag="bank")
                 for a in range(2):
-                    for t in range(PACK):
+                    for e in range(per_bank):
+                        t = per_bank * u + e
                         nc.tensor.matmul_mx(
-                            bank[:, t, :],
+                            bank[:, e, :],
                             lhsT=w1_codes[:, a, 2 * P * t : 2 * P * (t + 1)].bitcast(FP4X4),
                             lhsT_scale=w1_sc[:, a, P * t : P * (t + 1)],
                             rhs=v_codes[a][:, cols].bitcast(FP8X4),
                             rhs_scale=v_scales[a][:, cols],
-                            start=(a == 0 and t == 0),
-                            stop=(a == 1 and t == PACK - 1),
+                            start=(a == 0 and e == 0),
+                            stop=(a == 1 and e == per_bank - 1),
                         )
-            for half, bank in enumerate(banks):
                 nc.scalar.activation(
-                    th[:, half * PASS : (half + 1) * PASS].rearrange("p (j t) -> p j t", t=PACK),
-                    bank[:].rearrange("p t j -> p j t"),
+                    th[:, u * PASS : (u + 1) * PASS].rearrange("p (j e) -> p j e", e=per_bank),
+                    bank[:].rearrange("p e j -> p j e"),
                     ACT.Tanh,
                     bias=zero_bias[:],
                 )
-            return th[:].rearrange("p (j u e) -> p j u e", u=1, e=PACK)
+            return th[:].rearrange("p (u j e) -> p j u e", u=banks, e=per_bank)
 
         def stage2(am, j0, n, sl=None):
             per_bank = PASS // n
@@ -346,11 +347,17 @@ def tile_list_cyclone_intensity_nowcast_kernel(
         late_bf = [staging("bf_late0"), staging("bf_late1")]
         w4_bf = staging("bf_w4")
 
-        cast_w3(bf_first, 0, w3_first[0], nc.scalar.copy)
-        cast_w3(bf_first, HALF, w3_first[1], nc.scalar.copy)
         tanh_pair = held("tanh_pair", [P, 2, CHUNK * PACK], F32, "slot_tanh")
-        tanh = [stage1(0, tanh_pair[:, 0, :]), stage1(CHUNK, tanh_pair[:, 1, :]), stage1(2 * CHUNK), stage1(3 * CHUNK)]
+
+        def tanh_pieces(j0, tile):
+            for k in range(2):
+                stage1(j0 + k * P, P, tile[:, k * PASS : (k + 1) * PASS])
+            return tile.rearrange("p (j u e) -> p j u e", u=1, e=PACK)
+
+        tanh = [tanh_pieces(0, tanh_pair[:, 0, :]), stage1(CHUNK, CHUNK, tanh_pair[:, 1, :])]
+        tanh.extend([tanh_pieces(c * CHUNK, activations(CHUNK)[:]) for c in (2, 3)])
         cast_w3(late_bf[0], 0, w3_late[0], nc.scalar.copy)
+        cast_w3_half(late_bf[1], 2, w3_late[1], nc.scalar.copy)
         w2_codes = held("w2_codes", [P, M], I32)
 
         def reorder_w2(am):
@@ -359,6 +366,7 @@ def tile_list_cyclone_intensity_nowcast_kernel(
                 w2_raw[am][:].rearrange("p (c t i) -> p t c i", t=PACK, i=2),
             )
 
+        cast_w3(bf_first, 0, w3_first, nc.vector.tensor_copy)
         reorder_w2(0)
         w3_done[(0, 0)] = quantize("w3_00", bf_first, PASS)
         w2_sc = held("w2_sc", [P, PASS], U8, "slot_w2_sc")
@@ -384,7 +392,6 @@ def tile_list_cyclone_intensity_nowcast_kernel(
         cast_w3_half(late_bf[1], 0, w3_late[1], nc.vector.tensor_copy)
         quantize_run("h", h_done, 3 * CHUNK, h_last)
         early.append(stage2(0, 3 * CHUNK, CHUNK))
-        cast_w3_half(late_bf[1], 2, w3_late[1], nc.vector.tensor_copy)
         reorder_w2(1)
         w3_done[(0, 1)] = quantize("w3_01", late_bf[0], PASS)
         w3_done[(1, 1)] = quantize("w3_11", late_bf[1], PASS)
@@ -392,13 +399,12 @@ def tile_list_cyclone_intensity_nowcast_kernel(
         rest, shared = share_out(early[1], GAIN_Z[0], SHARE_PAIR, "bf_late1")
         own = gain(early[0], GAIN_Z[0])
         rest()
-        cast_w4(0, P, N, nc.vector.tensor_copy)
         quantize_run("z0", z_done[0], 0, own)
         quantize_run("z0", z_done[0], CHUNK, shared)
         rest, shared = share_out(early[2], GAIN_Z[0], SHARE_PAIR, "bf_late1")
         own = gain(early[3], GAIN_Z[0])
         rest()
-        cast_w4(0, 0, P, nc.scalar.copy)
+        cast_w4(0, 0, N, nc.scalar.copy)
         cast_w4(1, 0, N, nc.scalar.copy)
         late_pair = held("late_pair", [P, 2, CHUNK * PACK], F32, "w4_second")
         late = [two_pieces(1, 0, late_pair[:, 0, :]), two_pieces(1, CHUNK, late_pair[:, 1, :])]

@@ -118,17 +118,17 @@ def tile_list_cyclone_intensity_nowcast_kernel(
 
         picked_scales = held("picked_scales", [P, S], U8)
         nc.vector.tensor_copy(picked_scales[:], scale_window[:].indirect(offsets[:]))
-        for d in range(4):
+        for d in (0, 2, 1, 3):
             nc.sync.dma_start(words(v_both[32 * d : 32 * d + 4, :]), words(picked_scales[32 * d : 32 * d + 32 : 4, :]))
-        w3_first = load_w3(0, 0, PASS)
+        w3_first = load_w3(0, 0, PASS, "slot_w2_sc")
 
         def load_w2(am, slot=None):
             raw = held("w2_raw%d" % am, [P, PASS], I32, slot)
             nc.sync.dma_start(raw[:], words(w2_words[0, :, am * PASS : (am + 1) * PASS].rearrange("p c i -> p (c i)")))
             return raw
 
-        w2_raw = [load_w2(0, "slot_w2_sc")]
         w3_second = load_w3(1, 0, PASS, "slot_gain0")
+        w2_raw = [load_w2(0)]
         w3_late = [load_w3(0, PASS, PASS), load_w3(1, PASS, PASS)]
         w2_raw.append(load_w2(1))
         w4_raw = [held("w4_first", [P, PACK, N], F32), held("w4_second", [P, PACK, N], F32)]
@@ -367,7 +367,6 @@ def tile_list_cyclone_intensity_nowcast_kernel(
             )
 
         cast_w3(bf_first, 0, w3_first, nc.vector.tensor_copy)
-        reorder_w2(0)
         w3_done[(0, 0)] = quantize("w3_00", bf_first, PASS)
         w2_sc = held("w2_sc", [P, PASS], U8, "slot_w2_sc")
         nc.vector.tensor_copy(
@@ -377,6 +376,7 @@ def tile_list_cyclone_intensity_nowcast_kernel(
         h_first = gain_with_pool(tanh[0], GAIN_H, "bf_first")
         cast_w3(bf_second, 0, w3_second, nc.vector.tensor_copy)
         quantize_run("h", h_done, 0, h_first)
+        reorder_w2(0)
         w3_done[(1, 0)] = quantize("w3_10", bf_second, PASS)
         early = [stage2(0, 0, CHUNK)]
 

from contextlib import ExitStack

import concourse.mybir as mybir
from concourse.masks import make_identity

K, T, S, H, M, N = 1024, 2048, 1024, 512, 1024, 256
FLOPS = 2 * S * (K * H + H * M + K * M + M * N)

F32 = mybir.dt.float32
BF16 = mybir.dt.bfloat16
I32 = mybir.dt.int32
U32 = mybir.dt.uint32
U16 = mybir.dt.uint16
U8 = mybir.dt.uint8
FP8X4 = mybir.dt.float8_e4m3fn_x4
FP4X4 = mybir.dt.float4_e2m1fn_x4
ACT = mybir.ActivationFunctionType
MULT = mybir.AluOpType.mult
ADD = mybir.AluOpType.add

P = 128
PACK = 4
PASS = P * PACK
ROWS = PASS // 32
GROUP = 16
CHUNK = 256
HALF = PASS // 2
ACT_BUFS = 6
SHARE_ALONE = CHUNK // 4
SHARE_PAIR = P
SHARE_LAST = 3 * P // 4
REPEAT = 8
WIDE = REPEAT * PACK
GAIN_H, GAIN_Z = 0, (WIDE, 2 * WIDE)


def tile_list_cyclone_intensity_nowcast_kernel(
    tc, tab_words, tab_scales, offs, w1_words, w1_scales, w2_words, w2_scales, w3, w4, gain1, gain2, clim, out
):
    nc = tc.nc
    with ExitStack() as ctx:
        keep = ctx.enter_context(tc.tile_pool(name="keep", bufs=1))
        work = ctx.enter_context(tc.tile_pool(name="work", bufs=3))
        psum = ctx.enter_context(tc.psum_pool(name="psum", bufs=7))
        gain_pool = ctx.enter_context(tc.psum_pool(name="gain_pool", bufs=1))

        def held(name, shape, dtype, slot=None):
            return keep.tile(shape, dtype, name=name, tag=slot or name, align_bytes=64)

        def words(ap):
            return ap.bitcast(I32)

        offsets = keep.tile([P, S // GROUP], U16, name="offsets")
        nc.sync.dma_start(offsets[:], offs)

        identity = held("identity", [P, P], F32)
        make_identity(nc, identity[:])
        w2s_raw = held("w2s_raw", [P, PASS], U8)
        nc.gpsimd.memset(words(w2s_raw[:]), 0)
        for d in range(4):
            rows = w2_scales[0, 4 * d : 4 * d + 4, :].rearrange("r (a c) -> a r c", a=2)
            nc.gpsimd.dma_start(words(w2s_raw[32 * d : 32 * d + 8, :]), words(rows))

        gain1_sb = held("gain1_sb", [P, PACK], F32)
        nc.sync.dma_start(gain1_sb[:], gain1.rearrange("(p t) -> p t", t=PACK))
        gain2_raw = held("gain2_raw", [P, 2, 8], F32)
        for i in range(2):
            nc.scalar.dma_start(
                gain2_raw[i:P:2, :, 0:7], gain2.rearrange("(a c x) -> c a x", a=2, x=8)[:, :, i : i + 7]
            )

        scale_window = held("scale_window", [P, T], U8)
        nc.vector.memset(words(scale_window[:]), 0)
        nc.sync.dma_start(words(scale_window[0:P:4, :]), words(tab_scales.rearrange("a q c -> q a c")))

        zero_in = held("zero_in", [P, 1], F32)
        zero_bias = held("zero_bias", [P, 1], F32)
        nc.vector.memset(zero_in[:], 0.0)
        nc.scalar.activation(zero_bias[:], zero_in[:], ACT.Silu)

        def load_table(a):
            window = held("table%d" % a, [P, T], I32)
            nc.sync.dma_start(window[:], words(tab_words[a].rearrange("p t i -> p (t i)")))
            return window

        def load_w3(a, m0, width, slot=None):
            raw = held("w3_raw%d_%d" % (a, m0), [P, PACK, width], F32, slot)[:]
            rows = w3[a * PASS : (a + 1) * PASS, m0 : m0 + width]
            nc.sync.dma_start(raw, rows.rearrange("(p t) m -> p t m", t=PACK))
            return raw

        tables = [load_table(0)]
        w1_raw = held("w1_raw", [P, 2, 2 * H], U8)
        nc.sync.dma_start(words(w1_raw[:]), words(w1_words.rearrange("a p c -> p a c")))
        gains_sb = held("gains_sb", [P, P], F32)
        nc.vector.memset(gains_sb[:], 0.0)

        w1s_raw = held("w1s_raw", [P, 2 * H], U8)
        nc.vector.memset(words(w1s_raw[:]), 0)
        for r in range(4):
            nc.sync.dma_start(
                words(w1s_raw[r:P:32, :].rearrange("d (a c) -> d a c", a=2)),
                words(w1_scales[:, r:ROWS:4, :].rearrange("a d c -> d a c")),
            )

        v_both = held("v_both", [P, 2 * S], U8)
        nc.vector.memset(words(v_both[:]), 0)
        v_scales = [v_both[:, a * S : (a + 1) * S] for a in range(2)]
        tables.append(load_table(1))

        clim_sb = held("clim_sb", [P, N // P], F32)

        w1_codes = held("w1_codes", [P, 2, 2 * H], U8)
        nc.scalar.copy(
            w1_codes[:].bitcast(U16).rearrange("p a (t c) -> p a t c", t=PACK),
            w1_raw[:].bitcast(U16).rearrange("p a (c t) -> p a t c", t=PACK),
        )

        picked_scales = held("picked_scales", [P, S], U8)
        nc.vector.tensor_copy(picked_scales[:], scale_window[:].indirect(offsets[:]))
        for d in (0, 2, 1, 3):
            nc.sync.dma_start(words(v_both[32 * d : 32 * d + 4, :]), words(picked_scales[32 * d : 32 * d + 32 : 4, :]))
        w3_first = load_w3(0, 0, PASS, "slot_w2_sc")

        def load_w2(am, slot=None):
            raw = held("w2_raw%d" % am, [P, PASS], I32, slot)
            nc.sync.dma_start(raw[:], words(w2_words[0, :, am * PASS : (am + 1) * PASS].rearrange("p c i -> p (c i)")))
            return raw

        w3_second = load_w3(1, 0, PASS, "slot_gain0")
        w2_raw = [load_w2(0)]
        w3_late = [load_w3(0, PASS, PASS), load_w3(1, PASS, PASS)]
        w2_raw.append(load_w2(1))
        w4_raw = [held("w4_first", [P, PACK, N], F32), held("w4_second", [P, PACK, N], F32)]
        for am in range(2):
            rows = w4[am * PASS : (am + 1) * PASS, :].rearrange("(c t i) n -> i c t n", t=PACK, i=2)
            for i in range(2):
                nc.sync.dma_start(w4_raw[am][i:P:2, :, :], rows[i])
        with nc.allow_non_contiguous_dma(reason="one value a partition"):
            nc.sync.dma_start(clim_sb[:], clim.rearrange("(b p) -> p b", p=P))

        nc.scalar.copy(
            gains_sb[:, GAIN_H : GAIN_H + WIDE].rearrange("p (j t) -> p j t", t=PACK),
            gain1_sb[:].unsqueeze(1).to_broadcast([P, REPEAT, PACK]),
        )
        nc.scalar.copy(
            gains_sb[:, GAIN_Z[0] : GAIN_Z[1] + WIDE].rearrange("p (a j t) -> p a j t", a=2, t=PACK),
            gain2_raw[:, :, 0:8:2].unsqueeze(2).to_broadcast([P, 2, REPEAT, PACK]),
        )
        gain_bank = gain_pool.tile([P, 2, P], F32, name="gain_bank")
        nc.tensor.transpose(gain_bank[:, 1, :], gains_sb[:], identity[:])
        gains_turned = held("gains_turned", [P, P], F32)
        nc.scalar.copy(gains_turned[:], gain_bank[:, 1, :])
        nc.tensor.transpose(gain_bank[:, 0, :], gains_turned[:], identity[:])
        gains_ps = gain_bank[:, 0, :]

        v_codes = [held("v_codes%d" % a, [P, S], U32) for a in range(2)]

        def gather_words(a, j0, n):
            nc.vector.tensor_copy(
                v_codes[a][:, j0 : j0 + n],
                tables[a][:].bitcast(U32).indirect(offsets[:, j0 // GROUP : (j0 + n) // GROUP]),
            )

        gather_words(0, 0, S)
        w1_sc = held("w1_sc", [P, 2, H], U8)
        nc.vector.tensor_copy(
            w1_sc[:].rearrange("p a (t c) -> p a t c", t=PACK),
            w1s_raw[:].rearrange("p (a c t) -> p a t c", a=2, t=PACK),
        )
        for j0, n in ((0, CHUNK), (CHUNK, CHUNK), (2 * CHUNK, 2 * CHUNK)):
            gather_words(1, j0, n)

        def quantize(name, grouped, width):
            codes = held(name + "_codes", [P, width], U32)
            scales = held(name + "_sc", [P, width], U8)
            nc.vector.quantize_mx(codes[:].bitcast(FP8X4), scales[:], grouped[:])
            return codes, scales

        def staging(name):
            return held(name, [P, PASS * PACK], BF16)

        def cast_w3(grouped, m0, raw, cast):
            dst = grouped[:].rearrange("p (t c i x) -> p c t x i", t=PACK, i=2, x=PACK)
            src = raw.rearrange("p x (c t i) -> p c t x i", t=PACK, i=2)
            cast(dst[:, m0 // 8 : m0 // 8 + src.shape[1]], src)

        def cast_w3_half(grouped, t0, raw, cast):
            dst = grouped[:].rearrange("p (t c i x) -> p c t x i", t=PACK, i=2, x=PACK)
            src = raw.rearrange("p x (c t i) -> p c t x i", t=PACK, i=2)
            cast(dst[:, :, t0 : t0 + 2], src[:, :, t0 : t0 + 2])

        def columns(done, j0, n):
            first = max(j for j in done if j <= j0)
            cols = slice(j0 - first, j0 - first + n)
            return done[first][0][:, cols].bitcast(FP8X4), done[first][1][:, cols]

        def apply_gains(engine, gains, values, first, grouped):
            n, u, e = values.shape[1:]
            gains = gains[:, first : first + PACK].rearrange("p (u e) -> p u e", u=u)
            dst = grouped.rearrange("p (j u e) -> p j u e", j=n, u=u)
            engine.tensor_tensor(dst, values, gains.unsqueeze(1).to_broadcast([P, n, u, e]), MULT)

        def products(n):
            return work.tile([P, n * PACK], BF16, name="act16", tag="act16", align_bytes=64)[:]

        def gain(values, first, grouped=None):
            grouped = products(values.shape[1]) if grouped is None else grouped
            apply_gains(nc.vector, gains_ps, values, first, grouped)
            return grouped

        def pool_gain(values, first, grouped):
            rows = values.shape[1] // REPEAT
            nc.gpsimd.tensor_tensor(
                grouped.rearrange("p (r x) -> p r x", x=WIDE),
                values.rearrange("p (r j) u e -> p r (j u e)", j=REPEAT),
                gains_sb[:, first : first + WIDE].unsqueeze(1).to_broadcast([P, rows, WIDE]),
                MULT,
            )

        def quantize_run(name, done, j0, grouped):
            done[j0] = quantize("%s_%d" % (name, j0), grouped, grouped.shape[1] // PACK)

        def activations(n):
            return work.tile([P, n * PACK], F32, name="act32", tag="act32", bufs=ACT_BUFS)

        def stage1(j0, n, th=None):
            per_bank = PASS // n
            banks = PACK // per_bank
            th = activations(n) if th is None else th
            cols = slice(j0, j0 + n)
            for u in range(banks):
                bank = psum.tile([P, per_bank, n], F32, name="bank", tag="bank")
                for a in range(2):
                    for e in range(per_bank):
                        t = per_bank * u + e
                        nc.tensor.matmul_mx(
                            bank[:, e, :],
                            lhsT=w1_codes[:, a, 2 * P * t : 2 * P * (t + 1)].bitcast(FP4X4),
                            lhsT_scale=w1_sc[:, a, P * t : P * (t + 1)],
                            rhs=v_codes[a][:, cols].bitcast(FP8X4),
                            rhs_scale=v_scales[a][:, cols],
                            start=(a == 0 and e == 0),
                            stop=(a == 1 and e == per_bank - 1),
                        )
                nc.scalar.activation(
                    th[:, u * PASS : (u + 1) * PASS].rearrange("p (j e) -> p j e", e=per_bank),
                    bank[:].rearrange("p e j -> p j e"),
                    ACT.Tanh,
                    bias=zero_bias[:],
                )
            return th[:].rearrange("p (u j e) -> p j u e", u=banks, e=per_bank)

        def stage2(am, j0, n, sl=None):
            per_bank = PASS // n
            banks = PACK // per_bank
            sl = activations(n) if sl is None else sl
            cols = slice(j0, j0 + n)
            h_codes, h_sc = columns(h_done, j0, n)
            for u in range(banks):
                bank = psum.tile([P, per_bank, n], F32, name="bank", tag="bank")
                for place, step in enumerate((0, 2, 1)):
                    for e in range(per_bank):
                        wcols = slice(P * (per_bank * u + e), P * (per_bank * u + e + 1))
                        if step < 2:
                            w_codes, w_sc = w3_done[(step, am)][0][:, wcols], w3_done[(step, am)][1][:, wcols]
                            x_codes, x_sc = v_codes[step][:, cols].bitcast(FP8X4), v_scales[step][:, cols]
                        else:
                            w2cols = slice(am * PASS + wcols.start, am * PASS + wcols.stop)
                            w_codes, w_sc = w2_codes[:, w2cols], w2_sc[4 * am : P, wcols]
                            x_codes, x_sc = h_codes, h_sc
                        nc.tensor.matmul_mx(
                            bank[:, e, :],
                            lhsT=w_codes.bitcast(FP8X4),
                            lhsT_scale=w_sc,
                            rhs=x_codes,
                            rhs_scale=x_sc,
                            start=(place == 0 and e == 0),
                            stop=(place == 2 and e == per_bank - 1),
                        )
                nc.scalar.activation(
                    sl[:, u * PASS : (u + 1) * PASS].rearrange("p (j e) -> p j e", e=per_bank),
                    bank[:].rearrange("p e j -> p j e"),
                    ACT.Silu,
                )
            return sl[:].rearrange("p (u j e) -> p j u e", u=banks, e=per_bank)

        def stage3_pass(am, j0, n, bank):
            z_codes, z_sc = columns(z_done[am], j0, n)
            for b in range(N // P):
                wcols = slice(am * N + b * P, am * N + (b + 1) * P)
                nc.tensor.matmul_mx(
                    bank[:, b, :],
                    lhsT=w4_codes[:, wcols].bitcast(FP8X4),
                    lhsT_scale=w4_sc[:, wcols],
                    rhs=z_codes,
                    rhs_scale=z_sc,
                    start=(am == 0 and b == 0),
                    stop=(am == 1 and b == N // P - 1),
                )
            return j0, n, bank

        def stage3_open(j0, n):
            return stage3_pass(0, j0, n, psum.tile([P, N // P, n], F32, name="bank", tag="bank"))

        def stage3(j0, n):
            return stage3_pass(1, *stage3_open(j0, n))

        def cast_w4(am, n0, n1, cast):
            dst = w4_bf[:, am * N * PACK : (am + 1) * N * PACK].rearrange("p (c i t) -> p c t i", t=PACK, i=2)
            src = w4_raw[am][:].rearrange("p t (c i) -> p c t i", i=2)
            cast(dst[:, n0 // 2 : n1 // 2], src[:, n0 // 2 : n1 // 2])

        def share_out(pieces, first, share, slot):
            shared = held("shared", [P, CHUNK * PACK], BF16, slot)[:]
            pool_gain(pieces[0][:, 0:share], first, shared[:, 0 : share * PACK])

            def rest():
                if share < P:
                    gain(pieces[0][:, share:P], first, shared[:, share * PACK : PASS])
                gain(pieces[1], first, shared[:, PASS : 2 * PASS])

            return rest, shared

        def gain_with_pool(values, first, slot):
            grouped = held("shared", [P, CHUNK * PACK], BF16, slot)[:]
            cut = CHUNK - SHARE_ALONE
            pool_gain(values[:, cut:CHUNK], first, grouped[:, cut * PACK : CHUNK * PACK])
            gain(values[:, 0:cut], first, grouped[:, 0 : cut * PACK])
            return grouped

        def two_pieces(am, j0, tile=None):
            tiles = [None, None] if tile is None else [tile[:, 0:PASS], tile[:, PASS : 2 * PASS]]
            return [stage2(am, j0 + k * P, P, tiles[k]) for k in range(2)]

        def store(j0, n, bank):
            res = work.tile([P, N // P, n], F32, name="res", tag="res", bufs=5)
            if n == P:
                nc.vector.tensor_tensor(res[:], bank[:], clim_sb[:].unsqueeze(2).to_broadcast([P, N // P, n]), ADD)
            else:
                for b in range(N // P):
                    nc.scalar.activation(res[:, b, :], bank[:, b, :], ACT.Identity, bias=clim_sb[:, b : b + 1])
            nc.sync.dma_start(out[:, j0 : j0 + n].rearrange("(b p) j -> p b j", p=P), res[:])

        h_done, w3_done, z_done = {}, {}, [{}, {}]
        bf_first, bf_second = staging("bf_first"), staging("bf_second")
        late_bf = [staging("bf_late0"), staging("bf_late1")]
        w4_bf = staging("bf_w4")

        tanh_pair = held("tanh_pair", [P, 2, CHUNK * PACK], F32, "slot_tanh")

        def tanh_pieces(j0, tile):
            for k in range(2):
                stage1(j0 + k * P, P, tile[:, k * PASS : (k + 1) * PASS])
            return tile.rearrange("p (j u e) -> p j u e", u=1, e=PACK)

        tanh = [tanh_pieces(0, tanh_pair[:, 0, :]), stage1(CHUNK, CHUNK, tanh_pair[:, 1, :])]
        tanh.extend([tanh_pieces(c * CHUNK, activations(CHUNK)[:]) for c in (2, 3)])
        cast_w3(late_bf[0], 0, w3_late[0], nc.scalar.copy)
        cast_w3_half(late_bf[1], 2, w3_late[1], nc.scalar.copy)
        w2_codes = held("w2_codes", [P, M], I32)

        def reorder_w2(am):
            nc.vector.tensor_copy(
                w2_codes[:, am * PASS : (am + 1) * PASS].rearrange("p (t c i) -> p t c i", t=PACK, i=2),
                w2_raw[am][:].rearrange("p (c t i) -> p t c i", t=PACK, i=2),
            )

        cast_w3(bf_first, 0, w3_first, nc.vector.tensor_copy)
        w3_done[(0, 0)] = quantize("w3_00", bf_first, PASS)
        w2_sc = held("w2_sc", [P, PASS], U8, "slot_w2_sc")
        nc.vector.tensor_copy(
            w2_sc[:].bitcast(U16).rearrange("p (t c) -> p t c", t=PACK),
            w2s_raw[:].bitcast(U16).rearrange("p (c t) -> p t c", t=PACK),
        )
        h_first = gain_with_pool(tanh[0], GAIN_H, "bf_first")
        cast_w3(bf_second, 0, w3_second, nc.vector.tensor_copy)
        quantize_run("h", h_done, 0, h_first)
        reorder_w2(0)
        w3_done[(1, 0)] = quantize("w3_10", bf_second, PASS)
        early = [stage2(0, 0, CHUNK)]

        h_second = held("h_second", [P, CHUNK * PACK], BF16, "slot_gain0")[:]
        rest, shared = share_out([tanh[2][:, 0:P], tanh[2][:, P:CHUNK]], GAIN_H, SHARE_PAIR, "bf_second")
        gain(tanh[1], GAIN_H, h_second)
        rest()
        quantize_run("h", h_done, CHUNK, h_second)
        early.append(two_pieces(0, CHUNK))
        quantize_run("h", h_done, 2 * CHUNK, shared)
        early.append(two_pieces(0, 2 * CHUNK))
        h_last = gain_with_pool(tanh[3], GAIN_H, "slot_gain0")
        cast_w3_half(late_bf[1], 0, w3_late[1], nc.vector.tensor_copy)
        quantize_run("h", h_done, 3 * CHUNK, h_last)
        early.append(stage2(0, 3 * CHUNK, CHUNK))
        reorder_w2(1)
        w3_done[(0, 1)] = quantize("w3_01", late_bf[0], PASS)
        w3_done[(1, 1)] = quantize("w3_11", late_bf[1], PASS)

        rest, shared = share_out(early[1], GAIN_Z[0], SHARE_PAIR, "bf_late1")
        own = gain(early[0], GAIN_Z[0])
        rest()
        quantize_run("z0", z_done[0], 0, own)
        quantize_run("z0", z_done[0], CHUNK, shared)
        rest, shared = share_out(early[2], GAIN_Z[0], SHARE_PAIR, "bf_late1")
        own = gain(early[3], GAIN_Z[0])
        rest()
        cast_w4(0, 0, N, nc.scalar.copy)
        cast_w4(1, 0, N, nc.scalar.copy)
        late_pair = held("late_pair", [P, 2, CHUNK * PACK], F32, "w4_second")
        late = [two_pieces(1, 0, late_pair[:, 0, :]), two_pieces(1, CHUNK, late_pair[:, 1, :])]
        late.append(two_pieces(1, 2 * CHUNK))
        last_pieces = [stage2(1, 3 * CHUNK, P)]
        w4_codes, w4_sc = quantize("w4", w4_bf, 2 * N)
        quantize_run("z0", z_done[0], 2 * CHUNK, shared)
        quantize_run("z0", z_done[0], 3 * CHUNK, own)

        rest, shared = share_out(late[0], GAIN_Z[1], SHARE_PAIR, "bf_late1")
        rest()
        own = products(CHUNK)
        for k in range(2):
            gain(late[1][k], GAIN_Z[1], own[:, k * PASS : (k + 1) * PASS])
        quantize_run("z1", z_done[1], 0, shared)
        store(*stage3(0, CHUNK))
        last_pieces.append(stage2(1, 3 * CHUNK + P, P))
        quantize_run("z1", z_done[1], CHUNK, own)
        store(*stage3(CHUNK, CHUNK))
        opened = [stage3_open(2 * CHUNK, CHUNK), stage3_open(3 * CHUNK, P), stage3_open(3 * CHUNK + P, P)]
        rest, shared = share_out(late[2], GAIN_Z[1], SHARE_LAST, "bf_late1")
        rest()
        before_last = gain(last_pieces[0], GAIN_Z[1])
        quantize_run("z1", z_done[1], 2 * CHUNK, shared)
        store(*stage3_pass(1, *opened[0]))
        last = gain(last_pieces[1], GAIN_Z[1])
        quantize_run("z1", z_done[1], 3 * CHUNK, before_last)
        store(*stage3_pass(1, *opened[1]))
        quantize_run("z1", z_done[1], 3 * CHUNK + P, last)
        store(*stage3_pass(1, *opened[2]))
